import numpy as np
import ml_dtypes


def mxq(x, axis, fmt="e4m3"):
    dtype, down = {"e4m3": (ml_dtypes.float8_e4m3fn, 7), "e5m2": (ml_dtypes.float8_e5m2, 14)}[fmt]
    v = np.moveaxis(np.asarray(x, np.float32).astype(ml_dtypes.bfloat16).astype(np.float64), axis, -1)
    blocks = v.reshape(v.shape[:-1] + (-1, 32))
    amax = np.abs(blocks).max(-1, keepdims=True)
    byte = np.maximum(np.where(amax > 0, np.frexp(amax)[1] - 1 + 127, 0) - down, 1)
    scale = np.exp2(byte - 127.0)
    codes = (blocks / scale).astype(np.float32).astype(dtype).astype(np.float64)
    return np.moveaxis((codes * scale).reshape(v.shape), -1, axis)


WIDE = False


def mx_kscale(k):
    if not WIDE:
        return np.ones(k)
    levels = np.array([10, -10, 5, -5, 0])
    if k % 512:
        return np.exp2(np.random.permutation(np.resize(levels, k // 32))).repeat(32)
    a = np.empty((k // 512, 16))
    for p in range(k // 512):
        a[p, :8] = np.random.permutation(np.resize(levels, 8))
        for g in range(8):
            far = levels[np.abs(levels - a[p, g]) >= 10]
            a[p, g + 8] = far[np.random.randint(len(far))]
    return np.exp2(a.ravel()).repeat(32)


def f64(x):
    return np.asarray(x).astype(np.float64)


def striped(idx):
    return np.tile(idx.reshape(-1, 16).T, (8, 1)).astype(np.uint16)


def unstriped(offs):
    return offs[:16].T.reshape(-1).astype(np.int64)


E2M1 = np.array([0.0, 0.5, 1.0, 1.5, 2.0, 3.0, 4.0, 6.0, -0.0, -0.5, -1.0, -1.5, -2.0, -3.0, -4.0, -6.0])


def pack_weight(w, fmt):
    k, n = w.shape
    w = f64(np.asarray(w, np.float32).astype(ml_dtypes.bfloat16)).reshape(k // 32, 32, n)
    amax = np.abs(w).max(1)
    if fmt == "e4m3":
        byte = np.frexp(amax)[1] - 1 + 127 - 7
    else:
        mant, ex = np.frexp(amax / 6.0)
        byte = np.where(mant > 0.5, ex, ex - 1) + 127
    byte = np.clip(np.where(amax > 0, byte, 1), 1, 254)
    scaled = (w * np.exp2(127.0 - byte)[:, None, :]).reshape(k, n).astype(np.float32)
    by_word = np.ascontiguousarray(scaled.reshape(k // 512, 128, 4, n).transpose(0, 1, 3, 2))
    if fmt == "e4m3":
        words = by_word.astype(ml_dtypes.float8_e4m3fn).view(np.uint8)
    else:
        c = by_word.astype(ml_dtypes.float4_e2m1fn).view(np.uint8) & 0xF
        words = (c[..., 0::2] | (c[..., 1::2] << 4)).reshape(k // 512, 128, 2 * n)
    return np.ascontiguousarray(words), np.ascontiguousarray(byte.astype(np.uint8).reshape(k // 512, 16, n))


def unpack_weight(words, scales, fmt):
    g, _, n = scales.shape
    words = np.ascontiguousarray(words).reshape(g, 128, n, -1)
    if fmt == "e4m3":
        vals = words.view(ml_dtypes.float8_e4m3fn).astype(np.float64)
    else:
        nib = np.empty((g, 128, n, 4), np.uint8)
        nib[..., 0::2] = words & 0xF
        nib[..., 1::2] = words >> 4
        vals = E2M1[nib]
    vals = vals * np.repeat(np.exp2(scales.astype(np.float64) - 127.0), 8, axis=1)[..., None]
    return vals.transpose(0, 1, 3, 2).reshape(g * 512, n)


K, T, E, C, N = 1536, 512, 8, 256, 384
TOP = 4
K8 = 512


def by_expert(wq, xq):
    return np.concatenate([wq[e].T @ xq[:, e * C:(e + 1) * C] for e in range(E)], axis=1)


def setup_inputs():
    n = np.random.standard_normal
    s = mx_kscale(K)[:, None]
    deal = np.repeat(np.arange(E), C).reshape(TOP, T)[:, np.random.permutation(T)]
    deal = np.take_along_axis(deal, np.argsort(np.random.rand(TOP, T), axis=0), axis=0)
    for _ in range(8):
        s_, t_ = np.random.permutation(T).reshape(2, -1); r = np.random.randint(TOP, size=T // 2); x, y = deal[r, s_].copy(), deal[r, t_].copy()
        ok = ~((deal[:, s_] == y).any(0) | (deal[:, t_] == x).any(0)); deal[r[ok], s_[ok]] = y[ok]; deal[r[ok], t_[ok]] = x[ok]
    order = np.lexsort((np.random.rand(TOP * T), deal.reshape(-1)))
    slot_token = order % T; pos = np.empty(TOP * T, np.int64); pos[order] = np.arange(TOP * T); pos = pos.reshape(TOP, T)
    g = np.random.uniform(0.5, 1.5, (TOP, T)); g = g / g.sum(0)
    w = n((E, K, N)) / np.sqrt(K) / s[None]
    w8 = [pack_weight(m[:K8], "e4m3") for m in w]
    w4 = [pack_weight(m[K8:], "e2m1") for m in w]
    return {
        "xT": (n((K, T)) * s).astype(np.float32),
        "w8_words": np.stack([m[0] for m in w8]),
        "w8_scales": np.stack([m[1] for m in w8]),
        "w4_words": np.stack([m[0] for m in w4]),
        "w4_scales": np.stack([m[1] for m in w4]),
        "b": (0.3 * n((N, E))).astype(np.float32),
        "gate": np.stack([np.tile(r, (N, 1)) for r in g]).astype(np.float32),
        "offs": striped(slot_token),
        "pos1": striped(pos[0]),
        "pos2": striped(pos[1]),
        "pos3": striped(pos[2]),
        "pos4": striped(pos[3]),
    }


def reference(xT, w8_words, w8_scales, w4_words, w4_scales, b, gate, offs, pos1, pos2, pos3, pos4):
    idx = unstriped(offs)
    w = np.stack([np.concatenate([unpack_weight(w8_words[e], w8_scales[e], "e4m3"), unpack_weight(w4_words[e], w4_scales[e], "e2m1")]) for e in range(E)])
    xq = mxq(f64(xT)[:, idx], 0, "e4m3")
    y = by_expert(w, xq)
    y = y + np.repeat(f64(b), C, axis=1)
    return sum(f64(gate[r]) * y[:, unstriped(p)] for r, p in enumerate((pos1, pos2, pos3, pos4)))

@@ -1,0 +1,195 @@
+from contextlib import ExitStack
+
+import concourse.mybir as mybir
+
+K, T, E, C, N = 1536, 512, 8, 256, 384
+S = E * C
+FLOPS = 2 * K * N * S
+BYTES = 4 * K * T + E * K * N // 3 + E * K * N // 3 + E * K * N // 32 + 4 * N * E + 16 * T + 2 * 128 * (S + 4 * T) // 16 + 4 * N * T
+
+F32 = mybir.dt.float32
+BF16 = mybir.dt.bfloat16
+U32 = mybir.dt.uint32
+I32 = mybir.dt.int32
+U16 = mybir.dt.uint16
+U8 = mybir.dt.uint8
+FP8X4 = mybir.dt.float8_e4m3fn_x4
+FP4X4 = mybir.dt.float4_e2m1fn_x4
+COPY = mybir.ActivationFunctionType.Copy
+IDENT = mybir.ActivationFunctionType.Identity
+MULT = mybir.AluOpType.mult
+ADD = mybir.AluOpType.add
+
+P = 128
+NT = N // P
+WIN = (1376, 704, 704)
+ROW = (4, 0, 8)
+
+
+def tile_moe_tk_lin_bias_kernel(
+    tc, xT, w8_words, w8_scales, w4_words, w4_scales, b, gate, offs, pos1, pos2, pos3, pos4, out
+):
+    nc = tc.nc
+    with ExitStack() as ctx:
+        keep = ctx.enter_context(tc.tile_pool(name="keep", bufs=1))
+        psum = ctx.enter_context(tc.psum_pool(name="psum", bufs=8))
+
+        offs_t = keep.tile([P, S // 16], U16, name="offs_t")
+        pos_t = [keep.tile([P, T // 16], U16, name="pos_t%d" % r) for r in range(4)]
+        raw = [keep.tile([P, 4, T], F32, name="raw%d" % a) for a in range(3)]
+        grp = [keep.tile([P, T, 4], BF16, name="grp%d" % a, align_bytes=64) for a in range(3)]
+        words = [keep.tile([P, WIN[a]], U32, name="words%d" % a, align_bytes=64) for a in range(3)]
+        planes = keep.tile([P, WIN[0]], U8, name="planes", align_bytes=64)
+        gw = [keep.tile([P, S], U32, name="gw%d" % a, align_bytes=64) for a in range(3)]
+        gp = keep.tile([P, S], U8, name="gp", align_bytes=64)
+        gp_late = keep.tile([P, S], U8, name="gp_late", align_bytes=64)
+        gp2 = keep.tile([P, S], U8, name="gp2", align_bytes=64)
+        w8 = keep.tile([P, E, 4 * N], U8, name="w8", align_bytes=64)
+        w4 = keep.tile([P, 2 * E, 2 * N], U8, name="w4", align_bytes=64)
+        s8 = keep.tile([P, E, N], U8, name="s8", align_bytes=64)
+        s4 = keep.tile([P, 2 * E, N], U8, name="s4", align_bytes=64)
+        bias = keep.tile([P, NT, E], F32, name="bias")
+        gates = keep.tile([P, 4, T], F32, name="gates")
+        y = [keep.tile([P, S], F32, name="y%d" % n) for n in range(NT)]
+
+        nc.vector.memset(s8[:].rearrange("p e n -> p (e n)").bitcast(I32), 0)
+        xv = xT.rearrange("(a p j) t -> a p j t", p=P, j=4)
+        half = T // 2
+        cut = 256
+        nc.sync.dma_start(raw[0][:, :, :cut], xv[0, :, :, :cut])
+        nc.sync.dma_start(raw[0][:, :, cut:], xv[0, :, :, cut:])
+        nc.sync.dma_start(offs_t[:], offs)
+        nc.sync.dma_start(raw[1][:], xv[1])
+        nc.sync.dma_start(raw[2][:], xv[2])
+        v8 = w8_scales.rearrange("e a q n -> q (e a) n")
+        v4 = w4_scales.rearrange("e a q n -> q (e a) n")
+        for q in range(4):
+            nc.sync.dma_start(s8[32 * q : 32 * q + 4, :, :].bitcast(I32), v8[4 * q : 4 * q + 4].bitcast(I32))
+        nc.sync.dma_start(bias[:], b.rearrange("(c p) e -> p c e", p=P))
+        w8v = w8_words.rearrange("e a p n r -> p (e a) (n r)")
+        w4v = w4_words.rearrange("e a p n -> p (e a) n")
+        for e in range(0, E, 4):
+            nc.sync.dma_start(w8[:, e : e + 4, :].bitcast(I32), w8v[:, e : e + 4, :].bitcast(I32))
+            nc.sync.dma_start(w4[:, 2 * e : 2 * e + 8, :].bitcast(I32), w4v[:, 2 * e : 2 * e + 8, :].bitcast(I32))
+        for r, pos in enumerate((pos1, pos2, pos3, pos4)):
+            nc.sync.dma_start(pos_t[r][:], pos)
+        nc.sync.dma_start(gates[:], gate[:, :P, :].rearrange("r p t -> p r t"))
+
+        nc.gpsimd.memset(s4[:].rearrange("p e n -> p (e n)").bitcast(I32), 0)
+        for q in range(4):
+            nc.gpsimd.dma_start(s4[32 * q : 32 * q + 4, :, :].bitcast(I32), v4[4 * q : 4 * q + 4].bitcast(I32))
+        nc.vector.memset(planes[:].bitcast(I32), 0)
+        for a in range(3):
+            nc.vector.memset(words[a][:, T:].bitcast(I32), 0)
+        nc.vector.memset(gp2[:].bitcast(I32), 0)
+
+        def interleave(a, lo, hi, engine):
+            dst = grp[a][:, lo:hi, :].rearrange("p (c i) j -> p c j i", i=4)
+            src = raw[a][:, :, lo:hi].rearrange("p j (c i) -> p c j i", i=4)
+            if engine == 0:
+                nc.vector.tensor_copy(dst, src)
+            else:
+                nc.scalar.activation(dst, src, COPY)
+
+        def quantise(a, lo, hi):
+            nc.vector.quantize_mx(
+                out=words[a][:, lo:hi].bitcast(FP8X4),
+                scales=planes[ROW[a] :, lo:hi],
+                in_=grp[a][:, lo:hi, :].rearrange("p t j -> p (t j)"),
+            )
+
+        def gather_words(a, lo, hi):
+            nc.vector.tensor_copy(gw[a][:, lo:hi], words[a][:].indirect(offs_t[:, lo // 16 : hi // 16]))
+
+        def gather_bytes(lo, hi):
+            nc.vector.tensor_copy(gp[:, lo:hi], planes[:].indirect(offs_t[:, lo // 16 : hi // 16]))
+            nc.scalar.dma_start(gp2[: P - 8, lo:hi].bitcast(I32), gp[8:, lo:hi].bitcast(I32))
+
+        def multiply(e, n, first_plane):
+            acc = psum.tile([P, C], F32, name="acc")
+            for h in range(2):
+                cols = slice(C * e + P * h, C * e + P * (h + 1))
+                for a in range(3):
+                    if a == 0:
+                        lw = w8[:, e, 4 * P * n : 4 * P * (n + 1)].bitcast(FP8X4)
+                        ls = s8[:, e, P * n : P * (n + 1)]
+                        rs = first_plane[ROW[0] :, cols]
+                    else:
+                        lw = w4[:, 2 * e + a - 1, 2 * P * n : 2 * P * (n + 1)].bitcast(FP4X4)
+                        ls = s4[:, 2 * e + a - 1, P * n : P * (n + 1)]
+                        rs = gp[:, cols] if a == 1 else gp2[:, cols]
+                    nc.tensor.matmul_mx(
+                        out=acc[:, P * h : P * (h + 1)],
+                        lhsT=lw,
+                        lhsT_scale=ls,
+                        rhs=gw[a][:, cols].bitcast(FP8X4),
+                        rhs_scale=rs,
+                        start=(a == 0),
+                        stop=(a == 2),
+                    )
+            nc.scalar.activation(y[n][:, C * e : C * (e + 1)], acc[:], IDENT, bias=bias[:, n, e : e + 1])
+
+        interleave(0, 0, cut, 1)
+        interleave(0, cut, T, 0)
+        interleave(1, 0, T, 1)
+        interleave(2, 0, T, 1)
+        quantise(0, 0, cut)
+        quantise(0, cut, T)
+        gather_words(0, 0, S // 2)
+        gather_words(0, S // 2, S)
+        quantise(1, 0, T)
+        quantise(2, 0, T)
+        gather_bytes(0, S // 2)
+        gather_bytes(S // 2, S)
+        for e in range(0, E, 2):
+            gather_words(1, C * e, C * (e + 2))
+            for f in range(e, e + 2):
+                gather_words(2, C * f, C * (f + 1))
+                multiply(f, 0, gp)
+        nc.vector.tensor_copy(gp_late[:].bitcast(I32), gp[:].bitcast(I32))
+        for n in range(1, NT):
+            for e in range(E):
+                multiply(e, n, gp if n == 1 and e < 4 else gp_late)
+
+        prod = [keep.tile([P, 4, T], F32, name="prod%d" % n) for n in range(NT)]
+        pair = [keep.tile([P, 2, T], F32, name="pair%d" % n) for n in range(NT)]
+        res = [keep.tile([P, T], F32, name="res%d" % n) for n in range(NT)]
+
+        def fetch(n, r):
+            nc.vector.tensor_tensor(prod[n][:, r, :], y[n][:].indirect(pos_t[r][:]), gates[:, r, :], MULT)
+
+        def pair_up(n):
+            nc.vector.tensor_tensor(pair[n][:], prod[n][:, 0:2, :], prod[n][:, 2:4, :], ADD)
+
+        def finish(n):
+            nc.vector.tensor_tensor(res[n][:], pair[n][:, 0, :], pair[n][:, 1, :], ADD)
+            nc.sync.dma_start(out[P * n : P * (n + 1), :], res[n][:])
+
+        for n in range(NT - 1):
+            fetch(n, 0)
+            if n:
+                pair_up(n - 1)
+            fetch(n, 1)
+            if n:
+                finish(n - 1)
+            fetch(n, 2)
+            fetch(n, 3)
+
+        n = NT - 1
+        fetch(n, 0)
+        pair_up(n - 1)
+        fetch(n, 1)
+        finish(n - 1)
+        fetch(n, 2)
+        nc.vector.tensor_tensor(pair[n][:, 0, :], prod[n][:, 0, :], prod[n][:, 1, :], ADD)
+        for h in range(2):
+            cols = slice(half * h, half * (h + 1))
+            nc.vector.tensor_tensor(
+                prod[n][:, 3, cols], y[n][:].indirect(pos_t[3][:, T // 32 * h : T // 32 * (h + 1)]), gates[:, 3, cols], MULT
+            )
+            if h == 0:
+                nc.vector.tensor_tensor(pair[n][:, 1, :], pair[n][:, 0, :], prod[n][:, 2, :], ADD)
+        for h in range(2):
+            cols = slice(half * h, half * (h + 1))
+            nc.vector.tensor_tensor(res[n][:, cols], pair[n][:, 1, cols], prod[n][:, 3, cols], ADD)
+            nc.sync.dma_start(out[P * n : P * (n + 1), cols], res[n][:, cols])

@@ -1,6 +1,7 @@
 from contextlib import ExitStack
 
 import concourse.mybir as mybir
+from concourse.masks import make_identity
 
 K, T, E, C, N = 1536, 512, 8, 256, 384
 S = E * C
@@ -22,7 +23,9 @@ ADD = mybir.AluOpType.add
 
 P = 128
 NT = N // P
-WIN = (1376, 704, 704)
+WIN = 704
+WIN_BYTES = 1376
+EARLY = 512
 ROW = (4, 0, 8)
 
 
@@ -38,11 +41,11 @@ def tile_moe_tk_lin_bias_kernel(
         pos_t = [keep.tile([P, T // 16], U16, name="pos_t%d" % r) for r in range(4)]
         raw = [keep.tile([P, 4, T], F32, name="raw%d" % a) for a in range(3)]
         grp = [keep.tile([P, T, 4], BF16, name="grp%d" % a, align_bytes=64) for a in range(3)]
-        words = [keep.tile([P, WIN[a]], U32, name="words%d" % a, align_bytes=64) for a in range(3)]
-        planes = keep.tile([P, WIN[0]], U8, name="planes", align_bytes=64)
-        gw = [keep.tile([P, S], U32, name="gw%d" % a, align_bytes=64) for a in range(3)]
+        words = [keep.tile([P, WIN], U32, name="words%d" % a, align_bytes=64) for a in range(3)]
+        planes = keep.tile([P, WIN_BYTES], U8, name="planes", align_bytes=64)
+        gw = [keep.tile([P, EARLY if a == 1 else S], U32, name="gw%d" % a, align_bytes=64) for a in range(3)]
         gp = keep.tile([P, S], U8, name="gp", align_bytes=64)
-        gp_late = keep.tile([P, S], U8, name="gp_late", align_bytes=64)
+        ident = keep.tile([P, P], F32, name="ident")
         gp2 = keep.tile([P, S], U8, name="gp2", align_bytes=64)
         w8 = keep.tile([P, E, 4 * N], U8, name="w8", align_bytes=64)
         w4 = keep.tile([P, 2 * E, 2 * N], U8, name="w4", align_bytes=64)
@@ -75,6 +78,7 @@ def tile_moe_tk_lin_bias_kernel(
             nc.sync.dma_start(pos_t[r][:], pos)
         nc.sync.dma_start(gates[:], gate[:, :P, :].rearrange("r p t -> p r t"))
 
+        make_identity(nc, ident[:])
         nc.gpsimd.memset(s4[:].rearrange("p e n -> p (e n)").bitcast(I32), 0)
         for q in range(4):
             nc.gpsimd.dma_start(s4[32 * q : 32 * q + 4, :, :].bitcast(I32), v4[4 * q : 4 * q + 4].bitcast(I32))
@@ -98,14 +102,19 @@ def tile_moe_tk_lin_bias_kernel(
                 in_=grp[a][:, lo:hi, :].rearrange("p t j -> p (t j)"),
             )
 
+        def slots(a, lo, hi):
+            if a == 1 and lo >= EARLY:
+                return late[0][:, lo - EARLY : hi - EARLY]
+            return gw[a][:, lo:hi]
+
         def gather_words(a, lo, hi):
-            nc.vector.tensor_copy(gw[a][:, lo:hi], words[a][:].indirect(offs_t[:, lo // 16 : hi // 16]))
+            nc.vector.tensor_copy(slots(a, lo, hi), words[a][:].indirect(offs_t[:, lo // 16 : hi // 16]))
 
         def gather_bytes(lo, hi):
             nc.vector.tensor_copy(gp[:, lo:hi], planes[:].indirect(offs_t[:, lo // 16 : hi // 16]))
             nc.scalar.dma_start(gp2[: P - 8, lo:hi].bitcast(I32), gp[8:, lo:hi].bitcast(I32))
 
-        def multiply(e, n, first_plane):
+        def multiply(e, n):
             acc = psum.tile([P, C], F32, name="acc")
             for h in range(2):
                 cols = slice(C * e + P * h, C * e + P * (h + 1))
@@ -113,7 +122,7 @@ def tile_moe_tk_lin_bias_kernel(
                     if a == 0:
                         lw = w8[:, e, 4 * P * n : 4 * P * (n + 1)].bitcast(FP8X4)
                         ls = s8[:, e, P * n : P * (n + 1)]
-                        rs = first_plane[ROW[0] :, cols]
+                        rs = gp[ROW[0] :, cols]
                     else:
                         lw = w4[:, 2 * e + a - 1, 2 * P * n : 2 * P * (n + 1)].bitcast(FP4X4)
                         ls = s4[:, 2 * e + a - 1, P * n : P * (n + 1)]
@@ -122,74 +131,98 @@ def tile_moe_tk_lin_bias_kernel(
                         out=acc[:, P * h : P * (h + 1)],
                         lhsT=lw,
                         lhsT_scale=ls,
-                        rhs=gw[a][:, cols].bitcast(FP8X4),
+                        rhs=slots(a, cols.start, cols.stop).bitcast(FP8X4),
                         rhs_scale=rs,
                         start=(a == 0),
                         stop=(a == 2),
                     )
             nc.scalar.activation(y[n][:, C * e : C * (e + 1)], acc[:], IDENT, bias=bias[:, n, e : e + 1])
 
-        interleave(0, 0, cut, 1)
-        interleave(0, cut, T, 0)
+        late = []
+        interleave(0, 0, cut, 0)
+        quantise(0, 0, cut)
+        interleave(0, cut, cut + 160, 0)
+        interleave(0, cut + 160, T, 1)
+        quantise(0, cut, T)
         interleave(1, 0, T, 1)
         interleave(2, 0, T, 1)
-        quantise(0, 0, cut)
-        quantise(0, cut, T)
-        gather_words(0, 0, S // 2)
-        gather_words(0, S // 2, S)
+        for lo in range(0, S, T):
+            gather_words(0, lo, lo + T)
         quantise(1, 0, T)
+        gather_words(1, 0, EARLY)
         quantise(2, 0, T)
+        late.append(keep.tile([P, S - EARLY], U32, name="grp2", align_bytes=64))
         gather_bytes(0, S // 2)
-        gather_bytes(S // 2, S)
         for e in range(0, E, 2):
-            gather_words(1, C * e, C * (e + 2))
+            if e:
+                gather_words(1, C * e, C * (e + 2))
             for f in range(e, e + 2):
-                gather_words(2, C * f, C * (f + 1))
-                multiply(f, 0, gp)
-        nc.vector.tensor_copy(gp_late[:].bitcast(I32), gp[:].bitcast(I32))
-        for n in range(1, NT):
-            for e in range(E):
-                multiply(e, n, gp if n == 1 and e < 4 else gp_late)
+                if f < E - 1:
+                    gather_words(2, C * f, C * (f + 1))
+                else:
+                    gather_words(2, C * f, C * f + P)
+                    gather_words(2, C * f + P, C * (f + 1))
+                multiply(f, 0)
+            if e == 0:
+                gather_bytes(S // 2, S)
+            if e < E // 2:
+                for f in range(e, e + 2):
+                    multiply(f, 1)
+        for e in range(E // 2, E):
+            multiply(e, 1)
+        for e in range(E):
+            multiply(e, 2)
 
         prod = [keep.tile([P, 4, T], F32, name="prod%d" % n) for n in range(NT)]
-        pair = [keep.tile([P, 2, T], F32, name="pair%d" % n) for n in range(NT)]
+        turned = [keep.tile([P, T], F32, name="turned%d" % n) for n in range(NT)]
         res = [keep.tile([P, T], F32, name="res%d" % n) for n in range(NT)]
 
-        def fetch(n, r):
-            nc.vector.tensor_tensor(prod[n][:, r, :], y[n][:].indirect(pos_t[r][:]), gates[:, r, :], MULT)
+        def fetch(n, r, lo, hi):
+            nc.vector.tensor_tensor(
+                prod[n][:, r, lo:hi], y[n][:].indirect(pos_t[r][:, lo // 16 : hi // 16]), gates[:, r, lo:hi], MULT
+            )
 
-        def pair_up(n):
-            nc.vector.tensor_tensor(pair[n][:], prod[n][:, 0:2, :], prod[n][:, 2:4, :], ADD)
+        def add_turned(bank, n, r, lo, hi, last):
+            for c in range(lo, hi, P):
+                nc.tensor.matmul(
+                    bank[:, c - lo : c - lo + P],
+                    lhsT=prod[n][:, r, c : c + P],
+                    rhs=ident[:],
+                    is_transpose=True,
+                    start=(r == 0 and c == lo),
+                    stop=(r == last and c == hi - P),
+                )
 
-        def finish(n):
-            nc.vector.tensor_tensor(res[n][:], pair[n][:, 0, :], pair[n][:, 1, :], ADD)
-            nc.sync.dma_start(out[P * n : P * (n + 1), :], res[n][:])
+        def turn_back(bank, n, lo, hi):
+            nc.scalar.copy(turned[n][:, lo:hi], bank[:])
+            back = psum.tile([P, hi - lo], F32, name="acc")
+            for c in range(lo, hi, P):
+                nc.tensor.transpose(back[:, c - lo : c - lo + P], turned[n][:, c : c + P], ident[:])
+            return back
 
         for n in range(NT - 1):
-            fetch(n, 0)
-            if n:
-                pair_up(n - 1)
-            fetch(n, 1)
-            if n:
-                finish(n - 1)
-            fetch(n, 2)
-            fetch(n, 3)
+            bank = psum.tile([P, T], F32, name="acc")
+            for r in range(4):
+                fetch(n, r, 0, T)
+                add_turned(bank, n, r, 0, T, 3)
+            back = turn_back(bank, n, 0, T)
+            nc.scalar.copy(res[n][:], back[:])
+            nc.sync.dma_start(out[P * n : P * (n + 1), :], res[n][:])
 
         n = NT - 1
-        fetch(n, 0)
-        pair_up(n - 1)
-        fetch(n, 1)
-        finish(n - 1)
-        fetch(n, 2)
-        nc.vector.tensor_tensor(pair[n][:, 0, :], prod[n][:, 0, :], prod[n][:, 1, :], ADD)
+        banks = [psum.tile([P, half], F32, name="acc") for h in range(2)]
+        for r in range(2):
+            fetch(n, r, 0, T)
+            for h in range(2):
+                add_turned(banks[h], n, r, half * h, half * (h + 1), 2)
+        backs = []
+        for h in range(2):
+            fetch(n, 2, half * h, half * (h + 1))
+            add_turned(banks[h], n, 2, half * h, half * (h + 1), 2)
+            backs.append(turn_back(banks[h], n, half * h, half * (h + 1)))
+        for h in range(2):
+            fetch(n, 3, half * h, half * (h + 1))
         for h in range(2):
             cols = slice(half * h, half * (h + 1))
-            nc.vector.tensor_tensor(
-                prod[n][:, 3, cols], y[n][:].indirect(pos_t[3][:, T // 32 * h : T // 32 * (h + 1)]), gates[:, 3, cols], MULT
-            )
-            if h == 0:
-                nc.vector.tensor_tensor(pair[n][:, 1, :], pair[n][:, 0, :], prod[n][:, 2, :], ADD)
-        for h in range(2):
-            cols = slice(half * h, half * (h + 1))
-            nc.vector.tensor_tensor(res[n][:, cols], pair[n][:, 1, cols], prod[n][:, 3, cols], ADD)
+            nc.vector.tensor_tensor(res[n][:, cols], backs[h][:], prod[n][:, 3, cols], ADD)
             nc.sync.dma_start(out[P * n : P * (n + 1), cols], res[n][:, cols])

@@ -25,7 +25,7 @@ P = 128
 NT = N // P
 WIN = 704
 WIN_BYTES = 1376
-EARLY = 512
+EARLY = 1024
 ROW = (4, 0, 8)
 
 
@@ -55,6 +55,7 @@ def tile_moe_tk_lin_bias_kernel(
         gates = keep.tile([P, 4, T], F32, name="gates")
         y = [keep.tile([P, S], F32, name="y%d" % n) for n in range(NT)]
 
+        nc.vector.memset(s4[:].rearrange("p e n -> p (e n)").bitcast(I32), 0)
         nc.vector.memset(s8[:].rearrange("p e n -> p (e n)").bitcast(I32), 0)
         xv = xT.rearrange("(a p j) t -> a p j t", p=P, j=4)
         half = T // 2
@@ -79,7 +80,6 @@ def tile_moe_tk_lin_bias_kernel(
         nc.sync.dma_start(gates[:], gate[:, :P, :].rearrange("r p t -> p r t"))
 
         make_identity(nc, ident[:])
-        nc.gpsimd.memset(s4[:].rearrange("p e n -> p (e n)").bitcast(I32), 0)
         for q in range(4):
             nc.gpsimd.dma_start(s4[32 * q : 32 * q + 4, :, :].bitcast(I32), v4[4 * q : 4 * q + 4].bitcast(I32))
         nc.vector.memset(planes[:].bitcast(I32), 0)
@@ -114,29 +114,31 @@ def tile_moe_tk_lin_bias_kernel(
             nc.vector.tensor_copy(gp[:, lo:hi], planes[:].indirect(offs_t[:, lo // 16 : hi // 16]))
             nc.scalar.dma_start(gp2[: P - 8, lo:hi].bitcast(I32), gp[8:, lo:hi].bitcast(I32))
 
-        def multiply(e, n):
-            acc = psum.tile([P, C], F32, name="acc")
-            for h in range(2):
-                cols = slice(C * e + P * h, C * e + P * (h + 1))
-                for a in range(3):
-                    if a == 0:
-                        lw = w8[:, e, 4 * P * n : 4 * P * (n + 1)].bitcast(FP8X4)
-                        ls = s8[:, e, P * n : P * (n + 1)]
-                        rs = gp[ROW[0] :, cols]
-                    else:
-                        lw = w4[:, 2 * e + a - 1, 2 * P * n : 2 * P * (n + 1)].bitcast(FP4X4)
-                        ls = s4[:, 2 * e + a - 1, P * n : P * (n + 1)]
-                        rs = gp[:, cols] if a == 1 else gp2[:, cols]
+        def multiply(e, n, lo=0, hi=C):
+            acc = psum.tile([P, hi - lo], F32, name="acc")
+            cols = slice(C * e + lo, C * e + hi)
+            nc.tensor.matmul_mx(
+                out=acc[:],
+                lhsT=w8[:, e, 4 * P * n : 4 * P * (n + 1)].bitcast(FP8X4),
+                lhsT_scale=s8[:, e, P * n : P * (n + 1)],
+                rhs=gw[0][:, cols].bitcast(FP8X4),
+                rhs_scale=gp[ROW[0] :, cols],
+                start=True,
+                stop=False,
+            )
+            for a in (1, 2):
+                for c in range(lo, hi, P):
+                    part = slice(C * e + c, C * e + c + P)
                     nc.tensor.matmul_mx(
-                        out=acc[:, P * h : P * (h + 1)],
-                        lhsT=lw,
-                        lhsT_scale=ls,
-                        rhs=slots(a, cols.start, cols.stop).bitcast(FP8X4),
-                        rhs_scale=rs,
-                        start=(a == 0),
-                        stop=(a == 2),
+                        out=acc[:, c - lo : c - lo + P],
+                        lhsT=w4[:, 2 * e + a - 1, 2 * P * n : 2 * P * (n + 1)].bitcast(FP4X4),
+                        lhsT_scale=s4[:, 2 * e + a - 1, P * n : P * (n + 1)],
+                        rhs=slots(a, part.start, part.stop).bitcast(FP8X4),
+                        rhs_scale=gp[:, part] if a == 1 else gp2[:, part],
+                        start=False,
+                        stop=(a == 2 and c == hi - P),
                     )
-            nc.scalar.activation(y[n][:, C * e : C * (e + 1)], acc[:], IDENT, bias=bias[:, n, e : e + 1])
+            nc.scalar.activation(y[n][:, cols], acc[:], IDENT, bias=bias[:, n, e : e + 1])
 
         late = []
         interleave(0, 0, cut, 0)
@@ -149,28 +151,33 @@ def tile_moe_tk_lin_bias_kernel(
         for lo in range(0, S, T):
             gather_words(0, lo, lo + T)
         quantise(1, 0, T)
-        gather_words(1, 0, EARLY)
+        for lo in range(0, EARLY, T):
+            gather_words(1, lo, lo + T)
         quantise(2, 0, T)
         late.append(keep.tile([P, S - EARLY], U32, name="grp2", align_bytes=64))
         gather_bytes(0, S // 2)
-        for e in range(0, E, 2):
-            if e:
-                gather_words(1, C * e, C * (e + 2))
-            for f in range(e, e + 2):
-                if f < E - 1:
-                    gather_words(2, C * f, C * (f + 1))
-                else:
-                    gather_words(2, C * f, C * f + P)
-                    gather_words(2, C * f + P, C * (f + 1))
-                multiply(f, 0)
-            if e == 0:
-                gather_bytes(S // 2, S)
-            if e < E // 2:
-                for f in range(e, e + 2):
-                    multiply(f, 1)
-        for e in range(E // 2, E):
+        gather_words(2, 0, 2 * C)
+        for n in range(NT):
+            for e in range(2):
+                multiply(e, n)
+        gather_bytes(S // 2, S)
+        gather_words(2, 2 * C, 4 * C)
+        for n in range(NT - 1):
+            for e in range(2, 4):
+                multiply(e, n)
+        for lo in range(EARLY, S, T):
+            gather_words(1, lo, lo + T)
+        gather_words(2, 4 * C, 6 * C)
+        for e in range(4, 6):
+            multiply(e, 0)
+        gather_words(2, 6 * C, 7 * C)
+        multiply(6, 0)
+        for lo in range(0, C, P):
+            gather_words(2, 7 * C + lo, 7 * C + lo + P)
+            multiply(7, 0, lo, lo + P)
+        for e in range(4, E):
             multiply(e, 1)
-        for e in range(E):
+        for e in range(2, E):
             multiply(e, 2)
 
         prod = [keep.tile([P, 4, T], F32, name="prod%d" % n) for n in range(NT)]
@@ -210,19 +217,21 @@ def tile_moe_tk_lin_bias_kernel(
             nc.sync.dma_start(out[P * n : P * (n + 1), :], res[n][:])
 
         n = NT - 1
-        banks = [psum.tile([P, half], F32, name="acc") for h in range(2)]
+        ends = ((0, half), (half, half + P), (half + P, T))
+        banks = [psum.tile([P, hi - lo], F32, name="acc") for lo, hi in ends]
         for r in range(2):
             fetch(n, r, 0, T)
-            for h in range(2):
-                add_turned(banks[h], n, r, half * h, half * (h + 1), 2)
+            for bank, (lo, hi) in zip(banks, ends):
+                add_turned(bank, n, r, lo, hi, 2)
         backs = []
-        for h in range(2):
-            fetch(n, 2, half * h, half * (h + 1))
-            add_turned(banks[h], n, 2, half * h, half * (h + 1), 2)
-            backs.append(turn_back(banks[h], n, half * h, half * (h + 1)))
+        for bank, (lo, hi) in zip(banks, ends):
+            fetch(n, 2, lo, hi)
+            add_turned(bank, n, 2, lo, hi, 2)
+            backs.append(turn_back(bank, n, lo, hi))
         for h in range(2):
             fetch(n, 3, half * h, half * (h + 1))
-        for h in range(2):
-            cols = slice(half * h, half * (h + 1))
-            nc.vector.tensor_tensor(res[n][:, cols], backs[h][:], prod[n][:, 3, cols], ADD)
-            nc.sync.dma_start(out[P * n : P * (n + 1), cols], res[n][:, cols])
+        for back, (lo, hi) in zip(backs, ends):
+            nc.vector.tensor_tensor(res[n][:, lo:hi], back[:], prod[n][:, 3, lo:hi], ADD)
+            if hi != half + P:
+                cols = slice(hi - half, hi)
+                nc.sync.dma_start(out[P * n : P * (n + 1), cols], res[n][:, cols])

@@ -52,11 +52,13 @@ def tile_moe_tk_lin_bias_kernel(
         s8 = keep.tile([P, E, N], U8, name="s8", align_bytes=64)
         s4 = keep.tile([P, 2 * E, N], U8, name="s4", align_bytes=64)
         bias = keep.tile([P, NT, E], F32, name="bias")
-        gates = keep.tile([P, 4, T], F32, name="gates")
         y = [keep.tile([P, S], F32, name="y%d" % n) for n in range(NT)]
 
-        nc.vector.memset(s4[:].rearrange("p e n -> p (e n)").bitcast(I32), 0)
+        gate_rows = keep.tile([P, P], F32, name="gate_rows")
+        nc.gpsimd.memset(gate_rows[:], 0.0)
+        make_identity(nc, ident[:])
         nc.vector.memset(s8[:].rearrange("p e n -> p (e n)").bitcast(I32), 0)
+        nc.vector.memset(s4[:].rearrange("p e n -> p (e n)").bitcast(I32), 0)
         xv = xT.rearrange("(a p j) t -> a p j t", p=P, j=4)
         half = T // 2
         cut = 256
@@ -65,23 +67,24 @@ def tile_moe_tk_lin_bias_kernel(
         nc.sync.dma_start(offs_t[:], offs)
         nc.sync.dma_start(raw[1][:], xv[1])
         nc.sync.dma_start(raw[2][:], xv[2])
+        runs = gate.rearrange("r n (b t) -> (r n b) t", t=P)
+        nc.gpsimd.dma_start(gate_rows[:16, :], runs[0 : 15 * (N + 1) + 1 : N + 1])
+        nc.sync.dma_start(bias[:], b.rearrange("(c p) e -> p c e", p=P))
         v8 = w8_scales.rearrange("e a q n -> q (e a) n")
         v4 = w4_scales.rearrange("e a q n -> q (e a) n")
-        for q in range(4):
-            nc.sync.dma_start(s8[32 * q : 32 * q + 4, :, :].bitcast(I32), v8[4 * q : 4 * q + 4].bitcast(I32))
-        nc.sync.dma_start(bias[:], b.rearrange("(c p) e -> p c e", p=P))
         w8v = w8_words.rearrange("e a p n r -> p (e a) (n r)")
         w4v = w4_words.rearrange("e a p n -> p (e a) n")
         for e in range(0, E, 4):
             nc.sync.dma_start(w8[:, e : e + 4, :].bitcast(I32), w8v[:, e : e + 4, :].bitcast(I32))
             nc.sync.dma_start(w4[:, 2 * e : 2 * e + 8, :].bitcast(I32), w4v[:, 2 * e : 2 * e + 8, :].bitcast(I32))
+            if e == 0:
+                for q in range(4):
+                    nc.sync.dma_start(s8[q:P:32, :, :].bitcast(I32), v8[q:16:4].bitcast(I32))
         for r, pos in enumerate((pos1, pos2, pos3, pos4)):
             nc.sync.dma_start(pos_t[r][:], pos)
-        nc.sync.dma_start(gates[:], gate[:, :P, :].rearrange("r p t -> p r t"))
 
-        make_identity(nc, ident[:])
         for q in range(4):
-            nc.gpsimd.dma_start(s4[32 * q : 32 * q + 4, :, :].bitcast(I32), v4[4 * q : 4 * q + 4].bitcast(I32))
+            nc.gpsimd.dma_start(s4[q:P:32, :, :].bitcast(I32), v4[q:16:4].bitcast(I32))
         nc.vector.memset(planes[:].bitcast(I32), 0)
         for a in range(3):
             nc.vector.memset(words[a][:, T:].bitcast(I32), 0)
@@ -154,6 +157,17 @@ def tile_moe_tk_lin_bias_kernel(
         for lo in range(0, EARLY, T):
             gather_words(1, lo, lo + T)
         quantise(2, 0, T)
+        gates = keep.tile([P, 4 * T + 16], F32, name="raw2")
+        gate_cols = gates[:, 4 * T :]
+        bank = psum.tile([P, P], F32, name="acc")
+        nc.tensor.transpose(bank[:], gate_rows[:], ident[:])
+        nc.scalar.copy(gate_cols, bank[:, :16])
+        for r in range(4):
+            bank = psum.tile([P, T], F32, name="acc")
+            for c in range(4):
+                column = gates[:, 4 * T + 4 * r + c : 4 * T + 4 * r + c + 1]
+                nc.tensor.transpose(bank[:, P * c : P * (c + 1)], column.to_broadcast([P, P]), ident[:])
+            nc.scalar.copy(gates[:, T * r : T * (r + 1)], bank[:])
         late.append(keep.tile([P, S - EARLY], U32, name="grp2", align_bytes=64))
         gather_bytes(0, S // 2)
         gather_words(2, 0, 2 * C)
@@ -186,7 +200,7 @@ def tile_moe_tk_lin_bias_kernel(
 
         def fetch(n, r, lo, hi):
             nc.vector.tensor_tensor(
-                prod[n][:, r, lo:hi], y[n][:].indirect(pos_t[r][:, lo // 16 : hi // 16]), gates[:, r, lo:hi], MULT
+                prod[n][:, r, lo:hi], y[n][:].indirect(pos_t[r][:, lo // 16 : hi // 16]), gates[:, T * r + lo : T * r + hi], MULT
             )
 
         def add_turned(bank, n, r, lo, hi, last):

@@ -35,13 +35,14 @@ def tile_moe_tk_lin_bias_kernel(
     nc = tc.nc
     with ExitStack() as ctx:
         keep = ctx.enter_context(tc.tile_pool(name="keep", bufs=1))
-        psum = ctx.enter_context(tc.psum_pool(name="psum", bufs=8))
+        psum = ctx.enter_context(tc.psum_pool(name="psum", bufs=4))
+        held = ctx.enter_context(tc.psum_pool(name="held", bufs=1))
 
         offs_t = keep.tile([P, S // 16], U16, name="offs_t")
         pos_t = [keep.tile([P, T // 16], U16, name="pos_t%d" % r) for r in range(4)]
         raw = [keep.tile([P, 4, T], F32, name="raw%d" % a) for a in range(3)]
         grp = [keep.tile([P, T, 4], BF16, name="grp%d" % a, align_bytes=64) for a in range(3)]
-        words = [keep.tile([P, WIN], U32, name="words%d" % a, align_bytes=64) for a in range(3)]
+        words = keep.tile([P, 2 * T + WIN], U32, name="words", align_bytes=64)
         planes = keep.tile([P, WIN_BYTES], U8, name="planes", align_bytes=64)
         gw = [keep.tile([P, EARLY if a == 1 else S], U32, name="gw%d" % a, align_bytes=64) for a in range(3)]
         gp = keep.tile([P, S], U8, name="gp", align_bytes=64)
@@ -86,8 +87,7 @@ def tile_moe_tk_lin_bias_kernel(
         for q in range(4):
             nc.gpsimd.dma_start(s4[q:P:32, :, :].bitcast(I32), v4[q:16:4].bitcast(I32))
         nc.vector.memset(planes[:].bitcast(I32), 0)
-        for a in range(3):
-            nc.vector.memset(words[a][:, T:].bitcast(I32), 0)
+        nc.vector.memset(words[:, 3 * T :].bitcast(I32), 0)
         nc.vector.memset(gp2[:].bitcast(I32), 0)
 
         def interleave(a, lo, hi, engine):
@@ -100,7 +100,7 @@ def tile_moe_tk_lin_bias_kernel(
 
         def quantise(a, lo, hi):
             nc.vector.quantize_mx(
-                out=words[a][:, lo:hi].bitcast(FP8X4),
+                out=words[:, (2 - a) * T + lo : (2 - a) * T + hi].bitcast(FP8X4),
                 scales=planes[ROW[a] :, lo:hi],
                 in_=grp[a][:, lo:hi, :].rearrange("p t j -> p (t j)"),
             )
@@ -111,14 +111,17 @@ def tile_moe_tk_lin_bias_kernel(
             return gw[a][:, lo:hi]
 
         def gather_words(a, lo, hi):
-            nc.vector.tensor_copy(slots(a, lo, hi), words[a][:].indirect(offs_t[:, lo // 16 : hi // 16]))
+            nc.vector.tensor_copy(slots(a, lo, hi), words[:, (2 - a) * T : (2 - a) * T + WIN].indirect(offs_t[:, lo // 16 : hi // 16]))
 
         def gather_bytes(lo, hi):
             nc.vector.tensor_copy(gp[:, lo:hi], planes[:].indirect(offs_t[:, lo // 16 : hi // 16]))
             nc.scalar.dma_start(gp2[: P - 8, lo:hi].bitcast(I32), gp[8:, lo:hi].bitcast(I32))
 
-        def multiply(e, n, lo=0, hi=C):
-            acc = psum.tile([P, hi - lo], F32, name="acc")
+        def multiply(e, n, lo=0, hi=C, side=None):
+            if side is None:
+                acc = psum.tile([P, hi - lo], F32, name="acc")
+            else:
+                acc = held.tile([P, hi - lo], F32, name="side%d" % side)
             cols = slice(C * e + lo, C * e + hi)
             nc.tensor.matmul_mx(
                 out=acc[:],
@@ -170,29 +173,28 @@ def tile_moe_tk_lin_bias_kernel(
             nc.scalar.copy(gates[:, T * r : T * (r + 1)], bank[:])
         late.append(keep.tile([P, S - EARLY], U32, name="grp2", align_bytes=64))
         gather_bytes(0, S // 2)
+        gather_bytes(S // 2, S)
         gather_words(2, 0, 2 * C)
         for n in range(NT):
             for e in range(2):
-                multiply(e, n)
-        gather_bytes(S // 2, S)
+                multiply(e, n, side=2 + e if n == 2 else None)
         gather_words(2, 2 * C, 4 * C)
-        for n in range(NT - 1):
-            for e in range(2, 4):
-                multiply(e, n)
-        for lo in range(EARLY, S, T):
-            gather_words(1, lo, lo + T)
+        for e in range(2, 4):
+            multiply(e, 0, side=e % 2)
+        gather_words(1, 4 * C, 6 * C)
         gather_words(2, 4 * C, 6 * C)
         for e in range(4, 6):
             multiply(e, 0)
+        gather_words(1, 6 * C, 8 * C)
         gather_words(2, 6 * C, 7 * C)
         multiply(6, 0)
         for lo in range(0, C, P):
             gather_words(2, 7 * C + lo, 7 * C + lo + P)
-            multiply(7, 0, lo, lo + P)
-        for e in range(4, E):
-            multiply(e, 1)
-        for e in range(2, E):
-            multiply(e, 2)
+            multiply(7, 0, lo, lo + P, side=lo // P)
+        for n in range(1, NT):
+            multiply(7, n, side=n + 1)
+        for e in range(2, 7):
+            multiply(e, 1, side=(e - 2) % 4)
 
         prod = [keep.tile([P, 4, T], F32, name="prod%d" % n) for n in range(NT)]
         turned = [keep.tile([P, T], F32, name="turned%d" % n) for n in range(NT)]
@@ -214,21 +216,32 @@ def tile_moe_tk_lin_bias_kernel(
                     stop=(r == last and c == hi - P),
                 )
 
-        def turn_back(bank, n, lo, hi):
+        def turn_back(bank, back, n, lo, hi):
             nc.scalar.copy(turned[n][:, lo:hi], bank[:])
-            back = psum.tile([P, hi - lo], F32, name="acc")
             for c in range(lo, hi, P):
                 nc.tensor.transpose(back[:, c - lo : c - lo + P], turned[n][:, c : c + P], ident[:])
-            return back
 
-        for n in range(NT - 1):
-            bank = psum.tile([P, T], F32, name="acc")
-            for r in range(4):
-                fetch(n, r, 0, T)
-                add_turned(bank, n, r, 0, T, 3)
-            back = turn_back(bank, n, 0, T)
+        def leave(n, bank):
+            back = psum.tile([P, T], F32, name="acc")
+            turn_back(bank, back, n, 0, T)
             nc.scalar.copy(res[n][:], back[:])
             nc.sync.dma_start(out[P * n : P * (n + 1), :], res[n][:])
+
+        sides = (2, 3, 0)
+        bank = held.tile([P, T], F32, name="side1")
+        for r in range(4):
+            fetch(0, r, 0, T)
+            add_turned(bank, 0, r, 0, T, 3)
+            if r:
+                multiply(r + 1, 2, side=sides[r - 1])
+        multiply(5, 2, side=sides[0])
+        leave(0, bank)
+        multiply(6, 2, side=sides[1])
+        bank = held.tile([P, T], F32, name="side%d" % sides[1])
+        for r in range(4):
+            fetch(1, r, 0, T)
+            add_turned(bank, 1, r, 0, T, 3)
+        leave(1, bank)
 
         n = NT - 1
         ends = ((0, half), (half, half + P), (half + P, T))
@@ -241,7 +254,8 @@ def tile_moe_tk_lin_bias_kernel(
         for bank, (lo, hi) in zip(banks, ends):
             fetch(n, 2, lo, hi)
             add_turned(bank, n, 2, lo, hi, 2)
-            backs.append(turn_back(bank, n, lo, hi))
+            backs.append(psum.tile([P, hi - lo], F32, name="acc"))
+            turn_back(bank, backs[-1], n, lo, hi)
         for h in range(2):
             fetch(n, 3, half * h, half * (h + 1))
         for back, (lo, hi) in zip(backs, ends):

@@ -23,10 +23,13 @@ ADD = mybir.AluOpType.add
 
 P = 128
 NT = N // P
-WIN = 704
-WIN_BYTES = 1376
-EARLY = 1024
+TOP = 4
+BLOCKS = T // P
+HALF = T // 2
+LONG = 1376
+SHORT = 1024
 ROW = (4, 0, 8)
+VECTOR_SHARE = 192
 
 
 def tile_moe_tk_lin_bias_kernel(
@@ -36,64 +39,64 @@ def tile_moe_tk_lin_bias_kernel(
     with ExitStack() as ctx:
         keep = ctx.enter_context(tc.tile_pool(name="keep", bufs=1))
         psum = ctx.enter_context(tc.psum_pool(name="psum", bufs=4))
-        held = ctx.enter_context(tc.psum_pool(name="held", bufs=1))
+        named = ctx.enter_context(tc.psum_pool(name="named", bufs=1))
 
         offs_t = keep.tile([P, S // 16], U16, name="offs_t")
-        pos_t = [keep.tile([P, T // 16], U16, name="pos_t%d" % r) for r in range(4)]
+        pos_t = [keep.tile([P, T // 16], U16, name="pos_t%d" % r) for r in range(TOP)]
         raw = [keep.tile([P, 4, T], F32, name="raw%d" % a) for a in range(3)]
-        grp = [keep.tile([P, T, 4], BF16, name="grp%d" % a, align_bytes=64) for a in range(3)]
-        words = keep.tile([P, 2 * T + WIN], U32, name="words", align_bytes=64)
-        planes = keep.tile([P, WIN_BYTES], U8, name="planes", align_bytes=64)
-        gw = [keep.tile([P, EARLY if a == 1 else S], U32, name="gw%d" % a, align_bytes=64) for a in range(3)]
-        gp = keep.tile([P, S], U8, name="gp", align_bytes=64)
+        grouped = [keep.tile([P, T, 4], BF16, name="grouped%d" % a, align_bytes=64) for a in range(3)]
+        words = keep.tile([P, 4 * T], U32, name="words", align_bytes=64)
+        scales = keep.tile([P, LONG], U8, name="scales", align_bytes=64)
+        slot_words = [keep.tile([P, S // 2 if a == 1 else S], U32, name="slot_words%d" % a, align_bytes=64) for a in range(3)]
+        slot_scales = keep.tile([P, S], U8, name="slot_scales", align_bytes=64)
         ident = keep.tile([P, P], F32, name="ident")
-        gp2 = keep.tile([P, S], U8, name="gp2", align_bytes=64)
+        moved_scales = keep.tile([P, S], U8, name="moved_scales", align_bytes=64)
         w8 = keep.tile([P, E, 4 * N], U8, name="w8", align_bytes=64)
         w4 = keep.tile([P, 2 * E, 2 * N], U8, name="w4", align_bytes=64)
         s8 = keep.tile([P, E, N], U8, name="s8", align_bytes=64)
         s4 = keep.tile([P, 2 * E, N], U8, name="s4", align_bytes=64)
         bias = keep.tile([P, NT, E], F32, name="bias")
         y = [keep.tile([P, S], F32, name="y%d" % n) for n in range(NT)]
-
         gate_rows = keep.tile([P, P], F32, name="gate_rows")
+
         nc.gpsimd.memset(gate_rows[:], 0.0)
         make_identity(nc, ident[:])
-        nc.vector.memset(s8[:].rearrange("p e n -> p (e n)").bitcast(I32), 0)
         nc.vector.memset(s4[:].rearrange("p e n -> p (e n)").bitcast(I32), 0)
+        nc.vector.memset(s8[:].rearrange("p e n -> p (e n)").bitcast(I32), 0)
         xv = xT.rearrange("(a p j) t -> a p j t", p=P, j=4)
-        half = T // 2
-        cut = 256
-        nc.sync.dma_start(raw[0][:, :, :cut], xv[0, :, :, :cut])
-        nc.sync.dma_start(raw[0][:, :, cut:], xv[0, :, :, cut:])
+        nc.sync.dma_start(raw[0][:, :, :HALF], xv[0, :, :, :HALF])
+        nc.sync.dma_start(raw[0][:, :, HALF:], xv[0, :, :, HALF:])
         nc.sync.dma_start(offs_t[:], offs)
         nc.sync.dma_start(raw[1][:], xv[1])
         nc.sync.dma_start(raw[2][:], xv[2])
-        runs = gate.rearrange("r n (b t) -> (r n b) t", t=P)
-        nc.gpsimd.dma_start(gate_rows[:16, :], runs[0 : 15 * (N + 1) + 1 : N + 1])
+        runs = gate.rearrange("r n (c t) -> (r n c) t", t=P)
+        nc.gpsimd.dma_start(gate_rows[: TOP * BLOCKS, :], runs[0 : (TOP * BLOCKS - 1) * (N + 1) + 1 : N + 1])
         nc.sync.dma_start(bias[:], b.rearrange("(c p) e -> p c e", p=P))
         v8 = w8_scales.rearrange("e a q n -> q (e a) n")
         v4 = w4_scales.rearrange("e a q n -> q (e a) n")
         w8v = w8_words.rearrange("e a p n r -> p (e a) (n r)")
         w4v = w4_words.rearrange("e a p n -> p (e a) n")
-        for e in range(0, E, 4):
-            nc.sync.dma_start(w8[:, e : e + 4, :].bitcast(I32), w8v[:, e : e + 4, :].bitcast(I32))
-            nc.sync.dma_start(w4[:, 2 * e : 2 * e + 8, :].bitcast(I32), w4v[:, 2 * e : 2 * e + 8, :].bitcast(I32))
-            if e == 0:
-                for q in range(4):
-                    nc.sync.dma_start(s8[q:P:32, :, :].bitcast(I32), v8[q:16:4].bitcast(I32))
+
+        def load_weights(lo, hi):
+            nc.sync.dma_start(w8[:, lo:hi, :].bitcast(I32), w8v[:, lo:hi, :].bitcast(I32))
+            nc.sync.dma_start(w4[:, 2 * lo : 2 * hi, :].bitcast(I32), w4v[:, 2 * lo : 2 * hi, :].bitcast(I32))
+
+        load_weights(0, E // 2)
+        for q in range(4):
+            nc.sync.dma_start(s8[q:P:32, :, :].bitcast(I32), v8[q:16:4].bitcast(I32))
+        load_weights(E // 2, E)
         for r, pos in enumerate((pos1, pos2, pos3, pos4)):
             nc.sync.dma_start(pos_t[r][:], pos)
-
         for q in range(4):
             nc.gpsimd.dma_start(s4[q:P:32, :, :].bitcast(I32), v4[q:16:4].bitcast(I32))
-        nc.vector.memset(planes[:].bitcast(I32), 0)
+        nc.vector.memset(scales[:].bitcast(I32), 0)
         nc.vector.memset(words[:, 3 * T :].bitcast(I32), 0)
-        nc.vector.memset(gp2[:].bitcast(I32), 0)
+        nc.vector.memset(moved_scales[:].bitcast(I32), 0)
 
-        def interleave(a, lo, hi, engine):
-            dst = grp[a][:, lo:hi, :].rearrange("p (c i) j -> p c j i", i=4)
+        def interleave(a, lo, hi, on_vector=False):
+            dst = grouped[a][:, lo:hi, :].rearrange("p (c i) j -> p c j i", i=4)
             src = raw[a][:, :, lo:hi].rearrange("p j (c i) -> p c j i", i=4)
-            if engine == 0:
+            if on_vector:
                 nc.vector.tensor_copy(dst, src)
             else:
                 nc.scalar.activation(dst, src, COPY)
@@ -101,34 +104,39 @@ def tile_moe_tk_lin_bias_kernel(
         def quantise(a, lo, hi):
             nc.vector.quantize_mx(
                 out=words[:, (2 - a) * T + lo : (2 - a) * T + hi].bitcast(FP8X4),
-                scales=planes[ROW[a] :, lo:hi],
-                in_=grp[a][:, lo:hi, :].rearrange("p t j -> p (t j)"),
+                scales=scales[ROW[a] :, lo:hi],
+                in_=grouped[a][:, lo:hi, :].rearrange("p t j -> p (t j)"),
             )
 
-        def slots(a, lo, hi):
-            if a == 1 and lo >= EARLY:
-                return late[0][:, lo - EARLY : hi - EARLY]
-            return gw[a][:, lo:hi]
+        def in_slots(a, lo, hi):
+            if a == 1 and lo >= S // 2:
+                return late_words[:, lo - S // 2 : hi - S // 2]
+            return slot_words[a][:, lo:hi]
 
         def gather_words(a, lo, hi):
-            nc.vector.tensor_copy(slots(a, lo, hi), words[:, (2 - a) * T : (2 - a) * T + WIN].indirect(offs_t[:, lo // 16 : hi // 16]))
+            width = LONG if hi - lo > 3 * C else SHORT
+            window = words[:, (2 - a) * T : (2 - a) * T + width]
+            nc.vector.tensor_copy(in_slots(a, lo, hi), window.indirect(offs_t[:, lo // 16 : hi // 16]))
 
-        def gather_bytes(lo, hi):
-            nc.vector.tensor_copy(gp[:, lo:hi], planes[:].indirect(offs_t[:, lo // 16 : hi // 16]))
-            nc.scalar.dma_start(gp2[: P - 8, lo:hi].bitcast(I32), gp[8:, lo:hi].bitcast(I32))
+        def gather_scales(lo, hi):
+            nc.vector.tensor_copy(slot_scales[:, lo:hi], scales[:].indirect(offs_t[:, lo // 16 : hi // 16]))
+            nc.scalar.dma_start(moved_scales[: P - ROW[2], lo:hi].bitcast(I32), slot_scales[ROW[2] :, lo:hi].bitcast(I32))
 
-        def multiply(e, n, lo=0, hi=C, side=None):
-            if side is None:
+        def named_bank(i, width):
+            return named.tile([P, width], F32, name="bank%d" % i)
+
+        def multiply(e, n, lo=0, hi=C, bank=None):
+            if bank is None:
                 acc = psum.tile([P, hi - lo], F32, name="acc")
             else:
-                acc = held.tile([P, hi - lo], F32, name="side%d" % side)
+                acc = named_bank(bank, hi - lo)
             cols = slice(C * e + lo, C * e + hi)
             nc.tensor.matmul_mx(
                 out=acc[:],
                 lhsT=w8[:, e, 4 * P * n : 4 * P * (n + 1)].bitcast(FP8X4),
                 lhsT_scale=s8[:, e, P * n : P * (n + 1)],
-                rhs=gw[0][:, cols].bitcast(FP8X4),
-                rhs_scale=gp[ROW[0] :, cols],
+                rhs=slot_words[0][:, cols].bitcast(FP8X4),
+                rhs_scale=slot_scales[ROW[0] :, cols],
                 start=True,
                 stop=False,
             )
@@ -139,48 +147,46 @@ def tile_moe_tk_lin_bias_kernel(
                         out=acc[:, c - lo : c - lo + P],
                         lhsT=w4[:, 2 * e + a - 1, 2 * P * n : 2 * P * (n + 1)].bitcast(FP4X4),
                         lhsT_scale=s4[:, 2 * e + a - 1, P * n : P * (n + 1)],
-                        rhs=slots(a, part.start, part.stop).bitcast(FP8X4),
-                        rhs_scale=gp[:, part] if a == 1 else gp2[:, part],
+                        rhs=in_slots(a, part.start, part.stop).bitcast(FP8X4),
+                        rhs_scale=slot_scales[:, part] if a == 1 else moved_scales[:, part],
                         start=False,
                         stop=(a == 2 and c == hi - P),
                     )
             nc.scalar.activation(y[n][:, cols], acc[:], IDENT, bias=bias[:, n, e : e + 1])
 
-        late = []
-        interleave(0, 0, cut, 0)
-        quantise(0, 0, cut)
-        interleave(0, cut, cut + 160, 0)
-        interleave(0, cut + 160, T, 1)
-        quantise(0, cut, T)
-        interleave(1, 0, T, 1)
-        interleave(2, 0, T, 1)
-        for lo in range(0, S, T):
-            gather_words(0, lo, lo + T)
+        interleave(0, 0, HALF)
+        quantise(0, 0, HALF)
+        interleave(0, HALF, HALF + VECTOR_SHARE, on_vector=True)
+        interleave(0, HALF + VECTOR_SHARE, T)
+        quantise(0, HALF, T)
+        interleave(1, 0, T)
+        interleave(2, 0, T)
+        for lo in range(0, S, 3 * C):
+            gather_words(0, lo, min(lo + 3 * C, S))
         quantise(1, 0, T)
-        for lo in range(0, EARLY, T):
-            gather_words(1, lo, lo + T)
+        gather_words(1, 0, S // 2)
         quantise(2, 0, T)
-        gates = keep.tile([P, 4 * T + 16], F32, name="raw2")
-        gate_cols = gates[:, 4 * T :]
-        bank = psum.tile([P, P], F32, name="acc")
-        nc.tensor.transpose(bank[:], gate_rows[:], ident[:])
-        nc.scalar.copy(gate_cols, bank[:, :16])
-        for r in range(4):
-            bank = psum.tile([P, T], F32, name="acc")
-            for c in range(4):
-                column = gates[:, 4 * T + 4 * r + c : 4 * T + 4 * r + c + 1]
-                nc.tensor.transpose(bank[:, P * c : P * (c + 1)], column.to_broadcast([P, P]), ident[:])
-            nc.scalar.copy(gates[:, T * r : T * (r + 1)], bank[:])
-        late.append(keep.tile([P, S - EARLY], U32, name="grp2", align_bytes=64))
-        gather_bytes(0, S // 2)
-        gather_bytes(S // 2, S)
-        gather_words(2, 0, 2 * C)
+
+        gates = keep.tile([P, TOP * T + TOP * BLOCKS], F32, name="raw2")
+        acc = psum.tile([P, P], F32, name="acc")
+        nc.tensor.transpose(acc[:], gate_rows[:], ident[:])
+        nc.scalar.copy(gates[:, TOP * T :], acc[:, : TOP * BLOCKS])
+        for r in range(TOP):
+            acc = psum.tile([P, T], F32, name="acc")
+            for c in range(BLOCKS):
+                at = TOP * T + BLOCKS * r + c
+                nc.tensor.transpose(acc[:, P * c : P * (c + 1)], gates[:, at : at + 1].to_broadcast([P, P]), ident[:])
+            nc.scalar.copy(gates[:, T * r : T * (r + 1)], acc[:])
+
+        late_words = keep.tile([P, S // 2], U32, name="grouped2", align_bytes=64)
+        gather_scales(0, S // 2)
+        gather_scales(S // 2, S)
+        gather_words(2, 0, 4 * C)
         for n in range(NT):
             for e in range(2):
-                multiply(e, n, side=2 + e if n == 2 else None)
-        gather_words(2, 2 * C, 4 * C)
+                multiply(e, n, bank=2 + e if n == NT - 1 else None)
         for e in range(2, 4):
-            multiply(e, 0, side=e % 2)
+            multiply(e, 0, bank=e - 2)
         gather_words(1, 4 * C, 6 * C)
         gather_words(2, 4 * C, 6 * C)
         for e in range(4, 6):
@@ -190,13 +196,13 @@ def tile_moe_tk_lin_bias_kernel(
         multiply(6, 0)
         for lo in range(0, C, P):
             gather_words(2, 7 * C + lo, 7 * C + lo + P)
-            multiply(7, 0, lo, lo + P, side=lo // P)
+            multiply(7, 0, lo, lo + P, bank=lo // P)
         for n in range(1, NT):
-            multiply(7, n, side=n + 1)
+            multiply(7, n, bank=n + 1)
         for e in range(2, 7):
-            multiply(e, 1, side=(e - 2) % 4)
+            multiply(e, 1, bank=(e - 2) % 4)
 
-        prod = [keep.tile([P, 4, T], F32, name="prod%d" % n) for n in range(NT)]
+        prod = [keep.tile([P, TOP, T], F32, name="prod%d" % n) for n in range(NT)]
         turned = [keep.tile([P, T], F32, name="turned%d" % n) for n in range(NT)]
         res = [keep.tile([P, T], F32, name="res%d" % n) for n in range(NT)]
 
@@ -205,10 +211,10 @@ def tile_moe_tk_lin_bias_kernel(
                 prod[n][:, r, lo:hi], y[n][:].indirect(pos_t[r][:, lo // 16 : hi // 16]), gates[:, T * r + lo : T * r + hi], MULT
             )
 
-        def add_turned(bank, n, r, lo, hi, last):
+        def add_turned(total, n, r, lo, hi, last):
             for c in range(lo, hi, P):
                 nc.tensor.matmul(
-                    bank[:, c - lo : c - lo + P],
+                    total[:, c - lo : c - lo + P],
                     lhsT=prod[n][:, r, c : c + P],
                     rhs=ident[:],
                     is_transpose=True,
@@ -216,50 +222,48 @@ def tile_moe_tk_lin_bias_kernel(
                     stop=(r == last and c == hi - P),
                 )
 
-        def turn_back(bank, back, n, lo, hi):
-            nc.scalar.copy(turned[n][:, lo:hi], bank[:])
+        def turn_back(total, back, n, lo, hi):
+            nc.scalar.copy(turned[n][:, lo:hi], total[:])
             for c in range(lo, hi, P):
                 nc.tensor.transpose(back[:, c - lo : c - lo + P], turned[n][:, c : c + P], ident[:])
 
-        def leave(n, bank):
+        def store_sum(n, total):
             back = psum.tile([P, T], F32, name="acc")
-            turn_back(bank, back, n, 0, T)
+            turn_back(total, back, n, 0, T)
             nc.scalar.copy(res[n][:], back[:])
             nc.sync.dma_start(out[P * n : P * (n + 1), :], res[n][:])
 
-        sides = (2, 3, 0)
-        bank = held.tile([P, T], F32, name="side1")
-        for r in range(4):
+        total = named_bank(1, T)
+        for r in range(TOP):
             fetch(0, r, 0, T)
-            add_turned(bank, 0, r, 0, T, 3)
+            add_turned(total, 0, r, 0, T, TOP - 1)
             if r:
-                multiply(r + 1, 2, side=sides[r - 1])
-        multiply(5, 2, side=sides[0])
-        leave(0, bank)
-        multiply(6, 2, side=sides[1])
-        bank = held.tile([P, T], F32, name="side%d" % sides[1])
-        for r in range(4):
+                multiply(r + 1, 2, bank=(r + 1) % 4)
+        multiply(5, 2, bank=2)
+        store_sum(0, total)
+        multiply(6, 2, bank=3)
+        total = named_bank(3, T)
+        for r in range(TOP):
             fetch(1, r, 0, T)
-            add_turned(bank, 1, r, 0, T, 3)
-        leave(1, bank)
+            add_turned(total, 1, r, 0, T, TOP - 1)
+        store_sum(1, total)
 
         n = NT - 1
-        ends = ((0, half), (half, half + P), (half + P, T))
-        banks = [psum.tile([P, hi - lo], F32, name="acc") for lo, hi in ends]
+        pieces = ((0, HALF), (HALF, HALF + P), (HALF + P, T))
+        totals = [psum.tile([P, hi - lo], F32, name="acc") for lo, hi in pieces]
         for r in range(2):
             fetch(n, r, 0, T)
-            for bank, (lo, hi) in zip(banks, ends):
-                add_turned(bank, n, r, lo, hi, 2)
+            for total, (lo, hi) in zip(totals, pieces):
+                add_turned(total, n, r, lo, hi, 2)
         backs = []
-        for bank, (lo, hi) in zip(banks, ends):
+        for i, (lo, hi) in enumerate(pieces):
             fetch(n, 2, lo, hi)
-            add_turned(bank, n, 2, lo, hi, 2)
-            backs.append(psum.tile([P, hi - lo], F32, name="acc"))
-            turn_back(bank, backs[-1], n, lo, hi)
-        for h in range(2):
-            fetch(n, 3, half * h, half * (h + 1))
-        for back, (lo, hi) in zip(backs, ends):
+            add_turned(totals[i], n, 2, lo, hi, 2)
+            backs.append(named_bank(i, hi - lo))
+            turn_back(totals[i], backs[i], n, lo, hi)
+        for lo in range(0, T, HALF):
+            fetch(n, 3, lo, lo + HALF)
+        for back, (lo, hi) in zip(backs, pieces):
             nc.vector.tensor_tensor(res[n][:, lo:hi], back[:], prod[n][:, 3, lo:hi], ADD)
-            if hi != half + P:
-                cols = slice(hi - half, hi)
-                nc.sync.dma_start(out[P * n : P * (n + 1), cols], res[n][:, cols])
+            if hi % HALF == 0:
+                nc.sync.dma_start(out[P * n : P * (n + 1), hi - HALF : hi], res[n][:, hi - HALF : hi])

@@ -30,6 +30,7 @@ LONG = 1376
 SHORT = 1024
 ROW = (4, 0, 8)
 VECTOR_SHARE = 192
+EARLY = 2
 
 
 def tile_moe_tk_lin_bias_kernel(
@@ -51,8 +52,11 @@ def tile_moe_tk_lin_bias_kernel(
         slot_scales = keep.tile([P, S], U8, name="slot_scales", align_bytes=64)
         ident = keep.tile([P, P], F32, name="ident")
         moved_scales = keep.tile([P, S], U8, name="moved_scales", align_bytes=64)
-        w8 = keep.tile([P, E, 4 * N], U8, name="w8", align_bytes=64)
-        w4 = keep.tile([P, 2 * E, 2 * N], U8, name="w4", align_bytes=64)
+        w8_first = keep.tile([P, E, 4 * P], U8, name="w8_first", align_bytes=64)
+        w8_rest = keep.tile([P, E, 8 * P], U8, name="w8_rest", align_bytes=64)
+        w4_first = keep.tile([P, 2 * E, 2 * P], U8, name="w4_first", align_bytes=64)
+        w4_early = keep.tile([P, 2 * EARLY, 4 * P], U8, name="w4_early", align_bytes=64)
+        w4_rest = keep.tile([P, 2 * (E - EARLY), 4 * P], U8, name="w4_rest", align_bytes=64)
         s8 = keep.tile([P, E, N], U8, name="s8", align_bytes=64)
         s4 = keep.tile([P, 2 * E, N], U8, name="s4", align_bytes=64)
         bias = keep.tile([P, NT, E], F32, name="bias")
@@ -77,14 +81,13 @@ def tile_moe_tk_lin_bias_kernel(
         w8v = w8_words.rearrange("e a p n r -> p (e a) (n r)")
         w4v = w4_words.rearrange("e a p n -> p (e a) n")
 
-        def load_weights(lo, hi):
-            nc.sync.dma_start(w8[:, lo:hi, :].bitcast(I32), w8v[:, lo:hi, :].bitcast(I32))
-            nc.sync.dma_start(w4[:, 2 * lo : 2 * hi, :].bitcast(I32), w4v[:, 2 * lo : 2 * hi, :].bitcast(I32))
-
-        load_weights(0, E // 2)
+        nc.sync.dma_start(w8_first[:].bitcast(I32), w8v[:, :, : 4 * P].bitcast(I32))
+        nc.sync.dma_start(w4_first[:].bitcast(I32), w4v[:, :, : 2 * P].bitcast(I32))
         for q in range(4):
             nc.sync.dma_start(s8[q:P:32, :, :].bitcast(I32), v8[q:16:4].bitcast(I32))
-        load_weights(E // 2, E)
+        nc.sync.dma_start(w4_early[:].bitcast(I32), w4v[:, : 2 * EARLY, 2 * P :].bitcast(I32))
+        nc.sync.dma_start(w8_rest[:].bitcast(I32), w8v[:, :, 4 * P :].bitcast(I32))
+        nc.sync.dma_start(w4_rest[:].bitcast(I32), w4v[:, 2 * EARLY :, 2 * P :].bitcast(I32))
         for r, pos in enumerate((pos1, pos2, pos3, pos4)):
             nc.sync.dma_start(pos_t[r][:], pos)
         for q in range(4):
@@ -122,6 +125,15 @@ def tile_moe_tk_lin_bias_kernel(
             nc.vector.tensor_copy(slot_scales[:, lo:hi], scales[:].indirect(offs_t[:, lo // 16 : hi // 16]))
             nc.scalar.dma_start(moved_scales[: P - ROW[2], lo:hi].bitcast(I32), slot_scales[ROW[2] :, lo:hi].bitcast(I32))
 
+        def weights(a, e, n):
+            if a == 0:
+                return w8_first[:, e, :] if n == 0 else w8_rest[:, e, 4 * P * (n - 1) : 4 * P * n]
+            if n == 0:
+                return w4_first[:, 2 * e + a - 1, :]
+            if e < EARLY:
+                return w4_early[:, 2 * e + a - 1, 2 * P * (n - 1) : 2 * P * n]
+            return w4_rest[:, 2 * (e - EARLY) + a - 1, 2 * P * (n - 1) : 2 * P * n]
+
         def named_bank(i, width):
             return named.tile([P, width], F32, name="bank%d" % i)
 
@@ -133,7 +145,7 @@ def tile_moe_tk_lin_bias_kernel(
             cols = slice(C * e + lo, C * e + hi)
             nc.tensor.matmul_mx(
                 out=acc[:],
-                lhsT=w8[:, e, 4 * P * n : 4 * P * (n + 1)].bitcast(FP8X4),
+                lhsT=weights(0, e, n).bitcast(FP8X4),
                 lhsT_scale=s8[:, e, P * n : P * (n + 1)],
                 rhs=slot_words[0][:, cols].bitcast(FP8X4),
                 rhs_scale=slot_scales[ROW[0] :, cols],
@@ -145,7 +157,7 @@ def tile_moe_tk_lin_bias_kernel(
                     part = slice(C * e + c, C * e + c + P)
                     nc.tensor.matmul_mx(
                         out=acc[:, c - lo : c - lo + P],
-                        lhsT=w4[:, 2 * e + a - 1, 2 * P * n : 2 * P * (n + 1)].bitcast(FP4X4),
+                        lhsT=weights(a, e, n).bitcast(FP4X4),
                         lhsT_scale=s4[:, 2 * e + a - 1, P * n : P * (n + 1)],
                         rhs=in_slots(a, part.start, part.stop).bitcast(FP8X4),
                         rhs_scale=slot_scales[:, part] if a == 1 else moved_scales[:, part],
@@ -183,7 +195,7 @@ def tile_moe_tk_lin_bias_kernel(
         gather_scales(S // 2, S)
         gather_words(2, 0, 4 * C)
         for n in range(NT):
-            for e in range(2):
+            for e in range(EARLY):
                 multiply(e, n, bank=2 + e if n == NT - 1 else None)
         for e in range(2, 4):
             multiply(e, 0, bank=e - 2)
@@ -204,7 +216,7 @@ def tile_moe_tk_lin_bias_kernel(
 
         prod = [keep.tile([P, TOP, T], F32, name="prod%d" % n) for n in range(NT)]
         turned = [keep.tile([P, T], F32, name="turned%d" % n) for n in range(NT)]
-        res = [keep.tile([P, T], F32, name="res%d" % n) for n in range(NT)]
+        res = keep.tile([P, NT, T], F32, name="res")
 
         def fetch(n, r, lo, hi):
             nc.vector.tensor_tensor(
@@ -230,8 +242,7 @@ def tile_moe_tk_lin_bias_kernel(
         def store_sum(n, total):
             back = psum.tile([P, T], F32, name="acc")
             turn_back(total, back, n, 0, T)
-            nc.scalar.copy(res[n][:], back[:])
-            nc.sync.dma_start(out[P * n : P * (n + 1), :], res[n][:])
+            nc.scalar.copy(res[:, n, :], back[:])
 
         total = named_bank(1, T)
         for r in range(TOP):
@@ -247,6 +258,7 @@ def tile_moe_tk_lin_bias_kernel(
             fetch(1, r, 0, T)
             add_turned(total, 1, r, 0, T, TOP - 1)
         store_sum(1, total)
+        nc.sync.dma_start(out[: 2 * P, :].rearrange("(n p) t -> p n t", p=P), res[:, :2, :])
 
         n = NT - 1
         pieces = ((0, HALF), (HALF, HALF + P), (HALF + P, T))
@@ -264,6 +276,6 @@ def tile_moe_tk_lin_bias_kernel(
         for lo in range(0, T, HALF):
             fetch(n, 3, lo, lo + HALF)
         for back, (lo, hi) in zip(backs, pieces):
-            nc.vector.tensor_tensor(res[n][:, lo:hi], back[:], prod[n][:, 3, lo:hi], ADD)
+            nc.vector.tensor_tensor(res[:, n, lo:hi], back[:], prod[n][:, 3, lo:hi], ADD)
             if hi % HALF == 0:
-                nc.sync.dma_start(out[P * n : P * (n + 1), hi - HALF : hi], res[n][:, hi - HALF : hi])
+                nc.sync.dma_start(out[P * n : P * (n + 1), hi - HALF : hi], res[:, n, hi - HALF : hi])

@@ -29,7 +29,7 @@ HALF = T // 2
 LONG = 1376
 SHORT = 1024
 ROW = (4, 0, 8)
-VECTOR_SHARE = 192
+VECTOR_SHARE = 160
 EARLY = 2
 
 
@@ -39,14 +39,17 @@ def tile_moe_tk_lin_bias_kernel(
     nc = tc.nc
     with ExitStack() as ctx:
         keep = ctx.enter_context(tc.tile_pool(name="keep", bufs=1))
+        reused = ctx.enter_context(tc.tile_pool(name="reused", bufs=1))
         psum = ctx.enter_context(tc.psum_pool(name="psum", bufs=4))
         named = ctx.enter_context(tc.psum_pool(name="named", bufs=1))
 
         offs_t = keep.tile([P, S // 16], U16, name="offs_t")
         pos_t = [keep.tile([P, T // 16], U16, name="pos_t%d" % r) for r in range(TOP)]
-        raw = [keep.tile([P, 4, T], F32, name="raw%d" % a) for a in range(3)]
-        grouped = [keep.tile([P, T, 4], BF16, name="grouped%d" % a, align_bytes=64) for a in range(3)]
-        words = keep.tile([P, 4 * T], U32, name="words", align_bytes=64)
+        raw = [keep.tile([P, 4, T], F32, name="raw%d" % a) for a in (0, 2)]
+        grouped = [keep.tile([P, T, 4], BF16, name="grouped%d" % a, align_bytes=64) for a in (0, 2)]
+        raw.insert(1, reused.tile([P, 4, T], F32, name="raw1", offset=0, align_bytes=64))
+        grouped.insert(1, reused.tile([P, T, 4], BF16, name="grouped1", offset=16 * T, align_bytes=64))
+        words = keep.tile([P, 2 * T + LONG], U32, name="words", align_bytes=64)
         scales = keep.tile([P, LONG], U8, name="scales", align_bytes=64)
         slot_words = [keep.tile([P, S // 2 if a == 1 else S], U32, name="slot_words%d" % a, align_bytes=64) for a in range(3)]
         slot_scales = keep.tile([P, S], U8, name="slot_scales", align_bytes=64)
@@ -58,14 +61,12 @@ def tile_moe_tk_lin_bias_kernel(
         w4_early = keep.tile([P, 2 * EARLY, 4 * P], U8, name="w4_early", align_bytes=64)
         w4_rest = keep.tile([P, 2 * (E - EARLY), 4 * P], U8, name="w4_rest", align_bytes=64)
         s8 = keep.tile([P, E, N], U8, name="s8", align_bytes=64)
-        s4 = keep.tile([P, 2 * E, N], U8, name="s4", align_bytes=64)
         bias = keep.tile([P, NT, E], F32, name="bias")
         y = [keep.tile([P, S], F32, name="y%d" % n) for n in range(NT)]
         gate_rows = keep.tile([P, P], F32, name="gate_rows")
 
         nc.gpsimd.memset(gate_rows[:], 0.0)
         make_identity(nc, ident[:])
-        nc.vector.memset(s4[:].rearrange("p e n -> p (e n)").bitcast(I32), 0)
         nc.vector.memset(s8[:].rearrange("p e n -> p (e n)").bitcast(I32), 0)
         xv = xT.rearrange("(a p j) t -> a p j t", p=P, j=4)
         nc.sync.dma_start(raw[0][:, :, :HALF], xv[0, :, :, :HALF])
@@ -90,8 +91,6 @@ def tile_moe_tk_lin_bias_kernel(
         nc.sync.dma_start(w4_rest[:].bitcast(I32), w4v[:, 2 * EARLY :, 2 * P :].bitcast(I32))
         for r, pos in enumerate((pos1, pos2, pos3, pos4)):
             nc.sync.dma_start(pos_t[r][:], pos)
-        for q in range(4):
-            nc.gpsimd.dma_start(s4[q:P:32, :, :].bitcast(I32), v4[q:16:4].bitcast(I32))
         nc.vector.memset(scales[:].bitcast(I32), 0)
         nc.vector.memset(words[:, 3 * T :].bitcast(I32), 0)
         nc.vector.memset(moved_scales[:].bitcast(I32), 0)
@@ -166,16 +165,20 @@ def tile_moe_tk_lin_bias_kernel(
                     )
             nc.scalar.activation(y[n][:, cols], acc[:], IDENT, bias=bias[:, n, e : e + 1])
 
-        interleave(0, 0, HALF)
+        interleave(0, 0, P, on_vector=True)
+        interleave(0, P, HALF)
         quantise(0, 0, HALF)
         interleave(0, HALF, HALF + VECTOR_SHARE, on_vector=True)
         interleave(0, HALF + VECTOR_SHARE, T)
         quantise(0, HALF, T)
         interleave(1, 0, T)
         interleave(2, 0, T)
-        for lo in range(0, S, 3 * C):
-            gather_words(0, lo, min(lo + 3 * C, S))
+        for lo in range(0, S, S // 2):
+            gather_words(0, lo, lo + S // 2)
         quantise(1, 0, T)
+        s4 = reused.tile([P, 2 * E, N], U8, name="s4", offset=24 * T - 2 * E * N, align_bytes=64)
+        for q in range(4):
+            nc.gpsimd.dma_start(s4[q:P:32, :, :].bitcast(I32), v4[q:16:4].bitcast(I32))
         gather_words(1, 0, S // 2)
         quantise(2, 0, T)
 

@@ -30,7 +30,8 @@ LONG = 1376
 SHORT = 1024
 ROW = (4, 0, 8)
 VECTOR_SHARE = 160
-EARLY = 2
+OPEN = 4
+EARLY = 3
 
 
 def tile_moe_tk_lin_bias_kernel(
@@ -39,27 +40,20 @@ def tile_moe_tk_lin_bias_kernel(
     nc = tc.nc
     with ExitStack() as ctx:
         keep = ctx.enter_context(tc.tile_pool(name="keep", bufs=1))
-        reused = ctx.enter_context(tc.tile_pool(name="reused", bufs=1))
-        psum = ctx.enter_context(tc.psum_pool(name="psum", bufs=4))
-        named = ctx.enter_context(tc.psum_pool(name="named", bufs=1))
+        experts = ctx.enter_context(tc.psum_pool(name="experts", bufs=OPEN))
 
         offs_t = keep.tile([P, S // 16], U16, name="offs_t")
         pos_t = [keep.tile([P, T // 16], U16, name="pos_t%d" % r) for r in range(TOP)]
-        raw = [keep.tile([P, 4, T], F32, name="raw%d" % a) for a in (0, 2)]
-        grouped = [keep.tile([P, T, 4], BF16, name="grouped%d" % a, align_bytes=64) for a in (0, 2)]
-        raw.insert(1, reused.tile([P, 4, T], F32, name="raw1", offset=0, align_bytes=64))
-        grouped.insert(1, reused.tile([P, T, 4], BF16, name="grouped1", offset=16 * T, align_bytes=64))
+        raw = [keep.tile([P, 4, T], F32, name="raw%d" % a, align_bytes=64) for a in range(3)]
+        grouped = [keep.tile([P, T, 4], BF16, name="grouped%d" % a, align_bytes=64) for a in range(3)]
         words = keep.tile([P, 2 * T + LONG], U32, name="words", align_bytes=64)
         scales = keep.tile([P, LONG], U8, name="scales", align_bytes=64)
-        slot_words = [keep.tile([P, S // 2 if a == 1 else S], U32, name="slot_words%d" % a, align_bytes=64) for a in range(3)]
+        slot_words = [keep.tile([P, EARLY * C if a == 1 else S], U32, name="slot_words%d" % a, align_bytes=64) for a in range(3)]
         slot_scales = keep.tile([P, S], U8, name="slot_scales", align_bytes=64)
         ident = keep.tile([P, P], F32, name="ident")
         moved_scales = keep.tile([P, S], U8, name="moved_scales", align_bytes=64)
-        w8_first = keep.tile([P, E, 4 * P], U8, name="w8_first", align_bytes=64)
-        w8_rest = keep.tile([P, E, 8 * P], U8, name="w8_rest", align_bytes=64)
-        w4_first = keep.tile([P, 2 * E, 2 * P], U8, name="w4_first", align_bytes=64)
-        w4_early = keep.tile([P, 2 * EARLY, 4 * P], U8, name="w4_early", align_bytes=64)
-        w4_rest = keep.tile([P, 2 * (E - EARLY), 4 * P], U8, name="w4_rest", align_bytes=64)
+        w8 = [keep.tile([P, E // 2, 4 * N], U8, name="w8_%d" % h, align_bytes=64) for h in range(2)]
+        w4 = [keep.tile([P, E, 2 * N], U8, name="w4_%d" % h, align_bytes=64) for h in range(2)]
         s8 = keep.tile([P, E, N], U8, name="s8", align_bytes=64)
         bias = keep.tile([P, NT, E], F32, name="bias")
         y = [keep.tile([P, S], F32, name="y%d" % n) for n in range(NT)]
@@ -82,13 +76,12 @@ def tile_moe_tk_lin_bias_kernel(
         w8v = w8_words.rearrange("e a p n r -> p (e a) (n r)")
         w4v = w4_words.rearrange("e a p n -> p (e a) n")
 
-        nc.sync.dma_start(w8_first[:].bitcast(I32), w8v[:, :, : 4 * P].bitcast(I32))
-        nc.sync.dma_start(w4_first[:].bitcast(I32), w4v[:, :, : 2 * P].bitcast(I32))
+        nc.sync.dma_start(w8[0][:].bitcast(I32), w8v[:, : E // 2].bitcast(I32))
+        nc.sync.dma_start(w4[0][:].bitcast(I32), w4v[:, :E].bitcast(I32))
         for q in range(4):
             nc.sync.dma_start(s8[q:P:32, :, :].bitcast(I32), v8[q:16:4].bitcast(I32))
-        nc.sync.dma_start(w4_early[:].bitcast(I32), w4v[:, : 2 * EARLY, 2 * P :].bitcast(I32))
-        nc.sync.dma_start(w8_rest[:].bitcast(I32), w8v[:, :, 4 * P :].bitcast(I32))
-        nc.sync.dma_start(w4_rest[:].bitcast(I32), w4v[:, 2 * EARLY :, 2 * P :].bitcast(I32))
+        nc.sync.dma_start(w8[1][:].bitcast(I32), w8v[:, E // 2 :].bitcast(I32))
+        nc.sync.dma_start(w4[1][:].bitcast(I32), w4v[:, E:].bitcast(I32))
         for r, pos in enumerate((pos1, pos2, pos3, pos4)):
             nc.sync.dma_start(pos_t[r][:], pos)
         nc.vector.memset(scales[:].bitcast(I32), 0)
@@ -111,8 +104,8 @@ def tile_moe_tk_lin_bias_kernel(
             )
 
         def in_slots(a, lo, hi):
-            if a == 1 and lo >= S // 2:
-                return late_words[:, lo - S // 2 : hi - S // 2]
+            if a == 1 and lo >= EARLY * C:
+                return late_words[:, lo - EARLY * C : hi - EARLY * C]
             return slot_words[a][:, lo:hi]
 
         def gather_words(a, lo, hi):
@@ -120,50 +113,45 @@ def tile_moe_tk_lin_bias_kernel(
             window = words[:, (2 - a) * T : (2 - a) * T + width]
             nc.vector.tensor_copy(in_slots(a, lo, hi), window.indirect(offs_t[:, lo // 16 : hi // 16]))
 
-        def gather_scales(lo, hi):
+        def gather_scales(lo, hi, queue):
             nc.vector.tensor_copy(slot_scales[:, lo:hi], scales[:].indirect(offs_t[:, lo // 16 : hi // 16]))
-            nc.scalar.dma_start(moved_scales[: P - ROW[2], lo:hi].bitcast(I32), slot_scales[ROW[2] :, lo:hi].bitcast(I32))
+            queue.dma_start(moved_scales[: P - ROW[2], lo:hi].bitcast(I32), slot_scales[ROW[2] :, lo:hi].bitcast(I32))
 
         def weights(a, e, n):
+            h, i = divmod(e, E // 2)
             if a == 0:
-                return w8_first[:, e, :] if n == 0 else w8_rest[:, e, 4 * P * (n - 1) : 4 * P * n]
-            if n == 0:
-                return w4_first[:, 2 * e + a - 1, :]
-            if e < EARLY:
-                return w4_early[:, 2 * e + a - 1, 2 * P * (n - 1) : 2 * P * n]
-            return w4_rest[:, 2 * (e - EARLY) + a - 1, 2 * P * (n - 1) : 2 * P * n]
+                return w8[h][:, i, 4 * P * n : 4 * P * (n + 1)].bitcast(FP8X4)
+            return w4[h][:, 2 * i + a - 1, 2 * P * n : 2 * P * (n + 1)].bitcast(FP4X4)
 
-        def named_bank(i, width):
-            return named.tile([P, width], F32, name="bank%d" % i)
-
-        def multiply(e, n, lo=0, hi=C, bank=None):
-            if bank is None:
-                acc = psum.tile([P, hi - lo], F32, name="acc")
-            else:
-                acc = named_bank(bank, hi - lo)
+        def multiply(a, e, n, acc, lo=0, hi=C, opens=True, closes=True):
             cols = slice(C * e + lo, C * e + hi)
+            w_scales = s8[:, e, :] if a == 0 else s4[:, 2 * e + a - 1, :]
             nc.tensor.matmul_mx(
-                out=acc[:],
-                lhsT=weights(0, e, n).bitcast(FP8X4),
-                lhsT_scale=s8[:, e, P * n : P * (n + 1)],
-                rhs=slot_words[0][:, cols].bitcast(FP8X4),
-                rhs_scale=slot_scales[ROW[0] :, cols],
-                start=True,
-                stop=False,
+                out=acc,
+                lhsT=weights(a, e, n),
+                lhsT_scale=w_scales[:, P * n : P * (n + 1)],
+                rhs=in_slots(a, cols.start, cols.stop).bitcast(FP8X4),
+                rhs_scale=moved_scales[:, cols] if a == 2 else slot_scales[ROW[a] :, cols],
+                start=(a == 0 and opens),
+                stop=(a == 2 and closes),
             )
-            for a in (1, 2):
-                for c in range(lo, hi, P):
-                    part = slice(C * e + c, C * e + c + P)
-                    nc.tensor.matmul_mx(
-                        out=acc[:, c - lo : c - lo + P],
-                        lhsT=weights(a, e, n).bitcast(FP4X4),
-                        lhsT_scale=s4[:, 2 * e + a - 1, P * n : P * (n + 1)],
-                        rhs=in_slots(a, part.start, part.stop).bitcast(FP8X4),
-                        rhs_scale=slot_scales[:, part] if a == 1 else moved_scales[:, part],
-                        start=False,
-                        stop=(a == 2 and c == hi - P),
-                    )
-            nc.scalar.activation(y[n][:, cols], acc[:], IDENT, bias=bias[:, n, e : e + 1])
+
+        def empty(e, n, acc, lo=0, hi=C):
+            nc.scalar.activation(y[n][:, C * e + lo : C * e + hi], acc, IDENT, bias=bias[:, n, e : e + 1])
+
+        sums = {}
+
+        def expert_pass(a, e):
+            if a == 0:
+                sums[e] = (experts.tile([P, C], F32, name="first"), experts.tile([P, 2, C], F32, name="others"))
+            first, others = sums[e]
+            multiply(a, e, 0, first[:])
+            multiply(a, e, 1, others[:, 0, :], closes=False)
+            multiply(a, e, 2, others[:, 1, :], opens=False)
+            if a == 2:
+                empty(e, 0, first[:])
+                empty(e, 1, others[:, 0, :])
+                empty(e, 2, others[:, 1, :])
 
         interleave(0, 0, P, on_vector=True)
         interleave(0, P, HALF)
@@ -176,65 +164,69 @@ def tile_moe_tk_lin_bias_kernel(
         for lo in range(0, S, S // 2):
             gather_words(0, lo, lo + S // 2)
         quantise(1, 0, T)
-        s4 = reused.tile([P, 2 * E, N], U8, name="s4", offset=24 * T - 2 * E * N, align_bytes=64)
+        s4 = keep.tile([P, 2 * E, N], U8, name="raw0", align_bytes=64)
         for q in range(4):
             nc.gpsimd.dma_start(s4[q:P:32, :, :].bitcast(I32), v4[q:16:4].bitcast(I32))
-        gather_words(1, 0, S // 2)
+        gather_words(1, 0, EARLY * C)
         quantise(2, 0, T)
 
-        gates = keep.tile([P, TOP * T + TOP * BLOCKS], F32, name="raw2")
-        acc = psum.tile([P, P], F32, name="acc")
+        gates = keep.tile([P, TOP * T + TOP * BLOCKS], F32, name="raw2", align_bytes=64)
+        acc = experts.tile([P, P], F32, name="first")
         nc.tensor.transpose(acc[:], gate_rows[:], ident[:])
         nc.scalar.copy(gates[:, TOP * T :], acc[:, : TOP * BLOCKS])
         for r in range(TOP):
-            acc = psum.tile([P, T], F32, name="acc")
+            acc = experts.tile([P, T], F32, name="others")
             for c in range(BLOCKS):
                 at = TOP * T + BLOCKS * r + c
                 nc.tensor.transpose(acc[:, P * c : P * (c + 1)], gates[:, at : at + 1].to_broadcast([P, P]), ident[:])
             nc.scalar.copy(gates[:, T * r : T * (r + 1)], acc[:])
 
-        late_words = keep.tile([P, S // 2], U32, name="grouped2", align_bytes=64)
-        gather_scales(0, S // 2)
-        gather_scales(S // 2, S)
-        gather_words(2, 0, 4 * C)
-        for n in range(NT):
-            for e in range(EARLY):
-                multiply(e, n, bank=2 + e if n == NT - 1 else None)
-        for e in range(2, 4):
-            multiply(e, 0, bank=e - 2)
-        gather_words(1, 4 * C, 6 * C)
-        gather_words(2, 4 * C, 6 * C)
-        for e in range(4, 6):
-            multiply(e, 0)
-        gather_words(1, 6 * C, 8 * C)
-        gather_words(2, 6 * C, 7 * C)
-        multiply(6, 0)
-        for lo in range(0, C, P):
-            gather_words(2, 7 * C + lo, 7 * C + lo + P)
-            multiply(7, 0, lo, lo + P, bank=lo // P)
-        for n in range(1, NT):
-            multiply(7, n, bank=n + 1)
-        for e in range(2, 7):
-            multiply(e, 1, bank=(e - 2) % 4)
+        late_words = keep.tile([P, S - EARLY * C], U32, name="grouped2", align_bytes=64)
+        gather_scales(0, 2 * C, nc.scalar)
+        gather_scales(2 * C, 6 * C, nc.scalar)
+        gather_words(1, EARLY * C, OPEN * C)
+        for lo in range(0, OPEN * C, 2 * C):
+            gather_words(2, lo, lo + 2 * C)
+        gather_scales(6 * C, S, nc.sync)
+        for e in range(OPEN):
+            for a in range(2):
+                expert_pass(a, e)
+        for e in range(OPEN):
+            expert_pass(2, e)
+        expert_pass(0, OPEN)
+        for e in range(OPEN, E):
+            gather_words(1, C * e, C * (e + 1))
+            gather_words(2, C * e, C * (e + 1))
+            expert_pass(1, e)
+            if e + 1 < E:
+                expert_pass(0, e + 1)
+            expert_pass(2, e)
 
         prod = [keep.tile([P, TOP, T], F32, name="prod%d" % n) for n in range(NT)]
         turned = [keep.tile([P, T], F32, name="turned%d" % n) for n in range(NT)]
-        res = keep.tile([P, NT, T], F32, name="res")
+        final = keep.tile([P, T], F32, name="final")
+        last_list = keep.tile([P, T], F32, name="last_list")
 
-        def fetch(n, r, lo, hi):
+        def fetch(dst, n, r, lo=0, hi=T):
             nc.vector.tensor_tensor(
-                prod[n][:, r, lo:hi], y[n][:].indirect(pos_t[r][:, lo // 16 : hi // 16]), gates[:, T * r + lo : T * r + hi], MULT
+                dst[:, lo:hi], y[n][:].indirect(pos_t[r][:, lo // 16 : hi // 16]), gates[:, T * r + lo : T * r + hi], MULT
             )
 
-        def add_turned(total, n, r, lo, hi, last):
+        def fetch_plain(n, r):
+            nc.scalar.activation(prod[n][:, r, :], y[n][:].indirect(pos_t[r][:]), COPY)
+
+        def times_gate(n, r, lo=0, hi=T):
+            nc.vector.tensor_tensor(prod[n][:, r, lo:hi], prod[n][:, r, lo:hi], gates[:, T * r + lo : T * r + hi], MULT)
+
+        def add_turned(total, n, r, lo, hi, first, final):
             for c in range(lo, hi, P):
                 nc.tensor.matmul(
                     total[:, c - lo : c - lo + P],
                     lhsT=prod[n][:, r, c : c + P],
                     rhs=ident[:],
                     is_transpose=True,
-                    start=(r == 0 and c == lo),
-                    stop=(r == last and c == hi - P),
+                    start=(r == first and c == lo),
+                    stop=(r == final and c == hi - P),
                 )
 
         def turn_back(total, back, n, lo, hi):
@@ -242,43 +234,44 @@ def tile_moe_tk_lin_bias_kernel(
             for c in range(lo, hi, P):
                 nc.tensor.transpose(back[:, c - lo : c - lo + P], turned[n][:, c : c + P], ident[:])
 
-        def store_sum(n, total):
-            back = psum.tile([P, T], F32, name="acc")
-            turn_back(total, back, n, 0, T)
-            nc.scalar.copy(res[:, n, :], back[:])
+        def store(n, back):
+            res = keep.tile([P, T], F32, name="prod%d" % (n + 1))
+            nc.scalar.copy(res[:], back[:])
+            nc.sync.dma_start(out[P * n : P * (n + 1), :], res[:])
 
-        total = named_bank(1, T)
-        for r in range(TOP):
-            fetch(0, r, 0, T)
-            add_turned(total, 0, r, 0, T, TOP - 1)
-            if r:
-                multiply(r + 1, 2, bank=(r + 1) % 4)
-        multiply(5, 2, bank=2)
-        store_sum(0, total)
-        multiply(6, 2, bank=3)
-        total = named_bank(3, T)
-        for r in range(TOP):
-            fetch(1, r, 0, T)
-            add_turned(total, 1, r, 0, T, TOP - 1)
-        store_sum(1, total)
-        nc.sync.dma_start(out[: 2 * P, :].rearrange("(n p) t -> p n t", p=P), res[:, :2, :])
-
+        totals = [experts.tile([P, T], F32, name="first") for n in range(2)]
+        backs = [experts.tile([P, T], F32, name="others") for n in range(2)]
+        for n in range(2):
+            for r in range(2):
+                fetch(prod[n][:, r, :], n, r)
+                fetch_plain(n, r + 2)
+            for r in range(2, TOP):
+                times_gate(n, r)
+            for r in range(TOP):
+                add_turned(totals[n], n, r, 0, T, 0, 3)
         n = NT - 1
-        pieces = ((0, HALF), (HALF, HALF + P), (HALF + P, T))
-        totals = [psum.tile([P, hi - lo], F32, name="acc") for lo, hi in pieces]
-        for r in range(2):
-            fetch(n, r, 0, T)
+        fetch_plain(n, 2)
+        turn_back(totals[0], backs[0], 0, 0, T)
+        fetch_plain(n, 3)
+        turn_back(totals[1], backs[1], 1, 0, T)
+        store(0, backs[0])
+
+        pieces = ((0, HALF), (HALF, T))
+        totals = [experts.tile([P, hi - lo], F32, name="first") for lo, hi in pieces]
+        times_gate(n, 2)
+        fetch(prod[n][:, 0, :], n, 0)
+        for r in (2, 0):
             for total, (lo, hi) in zip(totals, pieces):
-                add_turned(total, n, r, lo, hi, 2)
-        backs = []
+                add_turned(total, n, r, lo, hi, 2, 3)
+        ends = []
         for i, (lo, hi) in enumerate(pieces):
-            fetch(n, 2, lo, hi)
-            add_turned(totals[i], n, 2, lo, hi, 2)
-            backs.append(named_bank(i, hi - lo))
-            turn_back(totals[i], backs[i], n, lo, hi)
-        for lo in range(0, T, HALF):
-            fetch(n, 3, lo, lo + HALF)
-        for back, (lo, hi) in zip(backs, pieces):
-            nc.vector.tensor_tensor(res[:, n, lo:hi], back[:], prod[n][:, 3, lo:hi], ADD)
-            if hi % HALF == 0:
-                nc.sync.dma_start(out[P * n : P * (n + 1), hi - HALF : hi], res[:, n, hi - HALF : hi])
+            times_gate(n, 3, lo, hi)
+            add_turned(totals[i], n, 3, lo, hi, 2, 3)
+            ends.append(experts.tile([P, hi - lo], F32, name="others"))
+            turn_back(totals[i], ends[i], n, lo, hi)
+        store(1, backs[1])
+        for lo, hi in pieces:
+            fetch(last_list, n, 1, lo, hi)
+        for end, (lo, hi) in zip(ends, pieces):
+            nc.vector.tensor_tensor(final[:, lo:hi], end[:], last_list[:, lo:hi], ADD)
+            nc.sync.dma_start(out[P * n : P * (n + 1), lo:hi], final[:, lo:hi])

@@ -70,7 +70,7 @@ def tile_moe_tk_lin_bias_kernel(
         nc.sync.dma_start(raw[2][:], xv[2])
         runs = gate.rearrange("r n (c t) -> (r n c) t", t=P)
         nc.gpsimd.dma_start(gate_rows[: TOP * BLOCKS, :], runs[0 : (TOP * BLOCKS - 1) * (N + 1) + 1 : N + 1])
-        nc.sync.dma_start(bias[:], b.rearrange("(c p) e -> p c e", p=P))
+        nc.gpsimd.dma_start(bias[:], b.rearrange("(c p) e -> p c e", p=P))
         v8 = w8_scales.rearrange("e a q n -> q (e a) n")
         v4 = w4_scales.rearrange("e a q n -> q (e a) n")
         w8v = w8_words.rearrange("e a p n r -> p (e a) (n r)")
@@ -252,21 +252,20 @@ def tile_moe_tk_lin_bias_kernel(
         n = NT - 1
         fetch_plain(n, 2)
         turn_back(totals[0], backs[0], 0, 0, T)
-        fetch_plain(n, 3)
         turn_back(totals[1], backs[1], 1, 0, T)
         store(0, backs[0])
 
         pieces = ((0, HALF), (HALF, T))
         totals = [experts.tile([P, hi - lo], F32, name="first") for lo, hi in pieces]
-        times_gate(n, 2)
         fetch(prod[n][:, 0, :], n, 0)
-        for r in (2, 0):
+        times_gate(n, 2)
+        for r in (0, 2):
             for total, (lo, hi) in zip(totals, pieces):
-                add_turned(total, n, r, lo, hi, 2, 3)
+                add_turned(total, n, r, lo, hi, 0, 3)
         ends = []
         for i, (lo, hi) in enumerate(pieces):
-            times_gate(n, 3, lo, hi)
-            add_turned(totals[i], n, 3, lo, hi, 2, 3)
+            fetch(prod[n][:, 3, :], n, 3, lo, hi)
+            add_turned(totals[i], n, 3, lo, hi, 0, 3)
             ends.append(experts.tile([P, hi - lo], F32, name="others"))
             turn_back(totals[i], ends[i], n, lo, hi)
         store(1, backs[1])

@@ -31,7 +31,7 @@ SHORT = 1024
 ROW = (4, 0, 8)
 VECTOR_SHARE = 160
 OPEN = 4
-EARLY = 3
+EARLY = 2
 
 
 def tile_moe_tk_lin_bias_kernel(
@@ -40,7 +40,7 @@ def tile_moe_tk_lin_bias_kernel(
     nc = tc.nc
     with ExitStack() as ctx:
         keep = ctx.enter_context(tc.tile_pool(name="keep", bufs=1))
-        experts = ctx.enter_context(tc.psum_pool(name="experts", bufs=OPEN))
+        psum = ctx.enter_context(tc.psum_pool(name="psum", bufs=1))
 
         offs_t = keep.tile([P, S // 16], U16, name="offs_t")
         pos_t = [keep.tile([P, T // 16], U16, name="pos_t%d" % r) for r in range(TOP)]
@@ -77,9 +77,9 @@ def tile_moe_tk_lin_bias_kernel(
         w4v = w4_words.rearrange("e a p n -> p (e a) n")
 
         nc.sync.dma_start(w8[0][:].bitcast(I32), w8v[:, : E // 2].bitcast(I32))
-        nc.sync.dma_start(w4[0][:].bitcast(I32), w4v[:, :E].bitcast(I32))
         for q in range(4):
             nc.sync.dma_start(s8[q:P:32, :, :].bitcast(I32), v8[q:16:4].bitcast(I32))
+        nc.sync.dma_start(w4[0][:].bitcast(I32), w4v[:, :E].bitcast(I32))
         nc.sync.dma_start(w8[1][:].bitcast(I32), w8v[:, E // 2 :].bitcast(I32))
         nc.sync.dma_start(w4[1][:].bitcast(I32), w4v[:, E:].bitcast(I32))
         for r, pos in enumerate((pos1, pos2, pos3, pos4)):
@@ -113,8 +113,10 @@ def tile_moe_tk_lin_bias_kernel(
             window = words[:, (2 - a) * T : (2 - a) * T + width]
             nc.vector.tensor_copy(in_slots(a, lo, hi), window.indirect(offs_t[:, lo // 16 : hi // 16]))
 
-        def gather_scales(lo, hi, queue):
+        def gather_scales(lo, hi):
             nc.vector.tensor_copy(slot_scales[:, lo:hi], scales[:].indirect(offs_t[:, lo // 16 : hi // 16]))
+
+        def move_scales(lo, hi, queue):
             queue.dma_start(moved_scales[: P - ROW[2], lo:hi].bitcast(I32), slot_scales[ROW[2] :, lo:hi].bitcast(I32))
 
         def weights(a, e, n):
@@ -139,19 +141,40 @@ def tile_moe_tk_lin_bias_kernel(
         def empty(e, n, acc, lo=0, hi=C):
             nc.scalar.activation(y[n][:, C * e + lo : C * e + hi], acc, IDENT, bias=bias[:, n, e : e + 1])
 
+        def bank(i, *shape):
+            return psum.tile([P, *shape], F32, name="bank%d" % i)
+
         sums = {}
 
         def expert_pass(a, e):
+            rows = range(1, min(NT, E - e))
             if a == 0:
-                sums[e] = (experts.tile([P, C], F32, name="first"), experts.tile([P, 2, C], F32, name="others"))
+                sums[e] = (bank(2 * (e % OPEN), C), bank(2 * (e % OPEN) + 1, len(rows), C))
             first, others = sums[e]
             multiply(a, e, 0, first[:])
-            multiply(a, e, 1, others[:, 0, :], closes=False)
-            multiply(a, e, 2, others[:, 1, :], opens=False)
+            for n in rows:
+                multiply(a, e, n, others[:, n - 1, :], opens=(n == rows[0]), closes=(n == rows[-1]))
             if a == 2:
                 empty(e, 0, first[:])
-                empty(e, 1, others[:, 0, :])
-                empty(e, 2, others[:, 1, :])
+                for n in rows:
+                    empty(e, n, others[:, n - 1, :])
+
+        def last_expert_pass(a):
+            e = E - 1
+            if a == 0:
+                sums[e] = (bank(6, P), bank(7, P))
+            for half, lo in zip(sums[e], (0, P)):
+                if a == 2:
+                    gather_words(2, C * e + lo, C * e + lo + P)
+                multiply(a, e, 0, half[:], lo, lo + P)
+                if a == 2:
+                    empty(e, 0, half[:], lo, lo + P)
+
+        def late_product(e, n, i):
+            acc = bank(i, C)
+            for a in range(3):
+                multiply(a, e, n, acc[:])
+            empty(e, n, acc[:])
 
         interleave(0, 0, P, on_vector=True)
         interleave(0, P, HALF)
@@ -171,36 +194,47 @@ def tile_moe_tk_lin_bias_kernel(
         quantise(2, 0, T)
 
         gates = keep.tile([P, TOP * T + TOP * BLOCKS], F32, name="raw2", align_bytes=64)
-        acc = experts.tile([P, P], F32, name="first")
+        acc = bank(0, P)
         nc.tensor.transpose(acc[:], gate_rows[:], ident[:])
         nc.scalar.copy(gates[:, TOP * T :], acc[:, : TOP * BLOCKS])
         for r in range(TOP):
-            acc = experts.tile([P, T], F32, name="others")
+            acc = bank(r + 1, T)
             for c in range(BLOCKS):
                 at = TOP * T + BLOCKS * r + c
                 nc.tensor.transpose(acc[:, P * c : P * (c + 1)], gates[:, at : at + 1].to_broadcast([P, P]), ident[:])
             nc.scalar.copy(gates[:, T * r : T * (r + 1)], acc[:])
 
         late_words = keep.tile([P, S - EARLY * C], U32, name="grouped2", align_bytes=64)
-        gather_scales(0, 2 * C, nc.scalar)
-        gather_scales(2 * C, 6 * C, nc.scalar)
+        gather_scales(0, C)
+        gather_scales(C, 2 * C)
+        move_scales(0, 2 * C, nc.scalar)
+        gather_scales(2 * C, 6 * C)
+        move_scales(2 * C, 6 * C, nc.scalar)
         gather_words(1, EARLY * C, OPEN * C)
         for lo in range(0, OPEN * C, 2 * C):
             gather_words(2, lo, lo + 2 * C)
-        gather_scales(6 * C, S, nc.sync)
-        for e in range(OPEN):
+        gather_scales(6 * C, S)
+        move_scales(6 * C, S, nc.sync)
+        for first in range(0, OPEN, 2):
             for a in range(2):
-                expert_pass(a, e)
+                for e in (first, first + 1):
+                    expert_pass(a, e)
         for e in range(OPEN):
             expert_pass(2, e)
-        expert_pass(0, OPEN)
-        for e in range(OPEN, E):
+        for e in range(OPEN, OPEN + 2):
+            expert_pass(0, e)
+        for e in range(OPEN, E - 1):
             gather_words(1, C * e, C * (e + 1))
             gather_words(2, C * e, C * (e + 1))
             expert_pass(1, e)
-            if e + 1 < E:
-                expert_pass(0, e + 1)
             expert_pass(2, e)
+            if e + 2 < E - 1:
+                expert_pass(0, e + 2)
+            if e + 2 == E - 1:
+                last_expert_pass(0)
+        gather_words(1, S - C, S)
+        last_expert_pass(1)
+        last_expert_pass(2)
 
         prod = [keep.tile([P, TOP, T], F32, name="prod%d" % n) for n in range(NT)]
         turned = [keep.tile([P, T], F32, name="turned%d" % n) for n in range(NT)]
@@ -239,12 +273,17 @@ def tile_moe_tk_lin_bias_kernel(
             nc.scalar.copy(res[:], back[:])
             nc.sync.dma_start(out[P * n : P * (n + 1), :], res[:])
 
-        totals = [experts.tile([P, T], F32, name="first") for n in range(2)]
-        backs = [experts.tile([P, T], F32, name="others") for n in range(2)]
+        totals = [bank(0, T), bank(2, T)]
+        backs = [bank(1, T), bank(3, T)]
         for n in range(2):
             for r in range(2):
                 fetch(prod[n][:, r, :], n, r)
                 fetch_plain(n, r + 2)
+                if (n, r) == (0, 0):
+                    late_product(E - 1, 1, 4)
+                if (n, r) == (0, 1):
+                    late_product(E - 2, 2, 5)
+                    late_product(E - 1, 2, 6)
             for r in range(2, TOP):
                 times_gate(n, r)
             for r in range(TOP):
@@ -256,7 +295,7 @@ def tile_moe_tk_lin_bias_kernel(
         store(0, backs[0])
 
         pieces = ((0, HALF), (HALF, T))
-        totals = [experts.tile([P, hi - lo], F32, name="first") for lo, hi in pieces]
+        totals = [bank(7, HALF), bank(4, HALF)]
         fetch(prod[n][:, 0, :], n, 0)
         times_gate(n, 2)
         for r in (0, 2):
@@ -266,7 +305,7 @@ def tile_moe_tk_lin_bias_kernel(
         for i, (lo, hi) in enumerate(pieces):
             fetch(prod[n][:, 3, :], n, 3, lo, hi)
             add_turned(totals[i], n, 3, lo, hi, 0, 3)
-            ends.append(experts.tile([P, hi - lo], F32, name="others"))
+            ends.append(bank(5 + i, hi - lo))
             turn_back(totals[i], ends[i], n, lo, hi)
         store(1, backs[1])
         for lo, hi in pieces:

@@ -157,7 +157,8 @@ def tile_moe_tk_lin_bias_kernel(
             if a == 2:
                 empty(e, 0, first[:])
                 for n in rows:
-                    empty(e, n, others[:, n - 1, :])
+                    if e < E - 2:
+                        empty(e, n, others[:, n - 1, :])
 
         def last_expert_pass(a):
             e = E - 1
@@ -224,7 +225,8 @@ def tile_moe_tk_lin_bias_kernel(
         for e in range(OPEN, OPEN + 2):
             expert_pass(0, e)
         for e in range(OPEN, E - 1):
-            gather_words(1, C * e, C * (e + 1))
+            if e % 2 == 0:
+                gather_words(1, C * e, C * (e + 2))
             gather_words(2, C * e, C * (e + 1))
             expert_pass(1, e)
             expert_pass(2, e)
@@ -232,9 +234,9 @@ def tile_moe_tk_lin_bias_kernel(
                 expert_pass(0, e + 2)
             if e + 2 == E - 1:
                 last_expert_pass(0)
-        gather_words(1, S - C, S)
         last_expert_pass(1)
         last_expert_pass(2)
+        nc.vector.tensor_scalar_add(y[1][:, S - 2 * C : S - C], sums[E - 2][1][:, 0, :], bias[:, 1, E - 2 : E - 1])
 
         prod = [keep.tile([P, TOP, T], F32, name="prod%d" % n) for n in range(NT)]
         turned = [keep.tile([P, T], F32, name="turned%d" % n) for n in range(NT)]
@@ -246,8 +248,8 @@ def tile_moe_tk_lin_bias_kernel(
                 dst[:, lo:hi], y[n][:].indirect(pos_t[r][:, lo // 16 : hi // 16]), gates[:, T * r + lo : T * r + hi], MULT
             )
 
-        def fetch_plain(n, r):
-            nc.scalar.activation(prod[n][:, r, :], y[n][:].indirect(pos_t[r][:]), COPY)
+        def fetch_plain(n, r, hi=T):
+            nc.scalar.activation(prod[n][:, r, :hi], y[n][:].indirect(pos_t[r][:, : hi // 16]), COPY)
 
         def times_gate(n, r, lo=0, hi=T):
             nc.vector.tensor_tensor(prod[n][:, r, lo:hi], prod[n][:, r, lo:hi], gates[:, T * r + lo : T * r + hi], MULT)
@@ -291,6 +293,7 @@ def tile_moe_tk_lin_bias_kernel(
         n = NT - 1
         fetch_plain(n, 2)
         turn_back(totals[0], backs[0], 0, 0, T)
+        fetch_plain(n, 3, HALF)
         turn_back(totals[1], backs[1], 1, 0, T)
         store(0, backs[0])
 
@@ -303,7 +306,10 @@ def tile_moe_tk_lin_bias_kernel(
                 add_turned(total, n, r, lo, hi, 0, 3)
         ends = []
         for i, (lo, hi) in enumerate(pieces):
-            fetch(prod[n][:, 3, :], n, 3, lo, hi)
+            if i == 0:
+                times_gate(n, 3, lo, hi)
+            else:
+                fetch(prod[n][:, 3, :], n, 3, lo, hi)
             add_turned(totals[i], n, 3, lo, hi, 0, 3)
             ends.append(bank(5 + i, hi - lo))
             turn_back(totals[i], ends[i], n, lo, hi)

@@ -53,7 +53,7 @@ def tile_moe_tk_lin_bias_kernel(
         ident = keep.tile([P, P], F32, name="ident")
         moved_scales = keep.tile([P, S], U8, name="moved_scales", align_bytes=64)
         w8 = [keep.tile([P, E // 2, 4 * N], U8, name="w8_%d" % h, align_bytes=64) for h in range(2)]
-        w4 = [keep.tile([P, E, 2 * N], U8, name="w4_%d" % h, align_bytes=64) for h in range(2)]
+        w4 = [keep.tile([P, 2 * n, 2 * N], U8, name="w4_%d" % h, align_bytes=64) for h, n in enumerate((EARLY, E - EARLY))]
         s8 = keep.tile([P, E, N], U8, name="s8", align_bytes=64)
         bias = keep.tile([P, NT, E], F32, name="bias")
         y = [keep.tile([P, S], F32, name="y%d" % n) for n in range(NT)]
@@ -79,9 +79,9 @@ def tile_moe_tk_lin_bias_kernel(
         nc.sync.dma_start(w8[0][:].bitcast(I32), w8v[:, : E // 2].bitcast(I32))
         for q in range(4):
             nc.sync.dma_start(s8[q:P:32, :, :].bitcast(I32), v8[q:16:4].bitcast(I32))
-        nc.sync.dma_start(w4[0][:].bitcast(I32), w4v[:, :E].bitcast(I32))
+        nc.sync.dma_start(w4[0][:].bitcast(I32), w4v[:, : 2 * EARLY].bitcast(I32))
         nc.sync.dma_start(w8[1][:].bitcast(I32), w8v[:, E // 2 :].bitcast(I32))
-        nc.sync.dma_start(w4[1][:].bitcast(I32), w4v[:, E:].bitcast(I32))
+        nc.sync.dma_start(w4[1][:].bitcast(I32), w4v[:, 2 * EARLY :].bitcast(I32))
         for r, pos in enumerate((pos1, pos2, pos3, pos4)):
             nc.sync.dma_start(pos_t[r][:], pos)
         nc.vector.memset(scales[:].bitcast(I32), 0)
@@ -113,16 +113,15 @@ def tile_moe_tk_lin_bias_kernel(
             window = words[:, (2 - a) * T : (2 - a) * T + width]
             nc.vector.tensor_copy(in_slots(a, lo, hi), window.indirect(offs_t[:, lo // 16 : hi // 16]))
 
-        def gather_scales(lo, hi):
+        def gather_scales(lo, hi, queue):
             nc.vector.tensor_copy(slot_scales[:, lo:hi], scales[:].indirect(offs_t[:, lo // 16 : hi // 16]))
-
-        def move_scales(lo, hi, queue):
             queue.dma_start(moved_scales[: P - ROW[2], lo:hi].bitcast(I32), slot_scales[ROW[2] :, lo:hi].bitcast(I32))
 
         def weights(a, e, n):
-            h, i = divmod(e, E // 2)
             if a == 0:
+                h, i = divmod(e, E // 2)
                 return w8[h][:, i, 4 * P * n : 4 * P * (n + 1)].bitcast(FP8X4)
+            h, i = (0, e) if e < EARLY else (1, e - EARLY)
             return w4[h][:, 2 * i + a - 1, 2 * P * n : 2 * P * (n + 1)].bitcast(FP4X4)
 
         def multiply(a, e, n, acc, lo=0, hi=C, opens=True, closes=True):
@@ -147,35 +146,24 @@ def tile_moe_tk_lin_bias_kernel(
         sums = {}
 
         def expert_pass(a, e):
-            rows = range(1, min(NT, E - e))
+            last = e == E - 1
             if a == 0:
-                sums[e] = (bank(2 * (e % OPEN), C), bank(2 * (e % OPEN) + 1, len(rows), C))
+                first = [bank(6, P), bank(0, P)] if last else [bank(2 * (e % OPEN), C)]
+                sums[e] = (first, bank(2 * (e % OPEN) + 1, NT - 1, C))
             first, others = sums[e]
-            multiply(a, e, 0, first[:])
-            for n in rows:
-                multiply(a, e, n, others[:, n - 1, :], opens=(n == rows[0]), closes=(n == rows[-1]))
+            width = C // len(first)
+            for i, acc in enumerate(first):
+                multiply(a, e, 0, acc[:], i * width, (i + 1) * width)
+                if a == 2:
+                    empty(e, 0, acc[:], i * width, (i + 1) * width)
+            for n in range(1, NT):
+                multiply(a, e, n, others[:, n - 1, :], opens=(n == 1), closes=(n == NT - 1))
             if a == 2:
-                empty(e, 0, first[:])
-                for n in rows:
+                for n in range(1, NT):
                     if e < E - 2:
                         empty(e, n, others[:, n - 1, :])
-
-        def last_expert_pass(a):
-            e = E - 1
-            if a == 0:
-                sums[e] = (bank(6, P), bank(7, P))
-            for half, lo in zip(sums[e], (0, P)):
-                if a == 2:
-                    gather_words(2, C * e + lo, C * e + lo + P)
-                multiply(a, e, 0, half[:], lo, lo + P)
-                if a == 2:
-                    empty(e, 0, half[:], lo, lo + P)
-
-        def late_product(e, n, i):
-            acc = bank(i, C)
-            for a in range(3):
-                multiply(a, e, n, acc[:])
-            empty(e, n, acc[:])
+                    elif (e, n) != (E - 1, NT - 1):
+                        nc.vector.tensor_scalar_add(y[n][:, C * e : C * (e + 1)], others[:, n - 1, :], bias[:, n, e : e + 1])
 
         interleave(0, 0, P, on_vector=True)
         interleave(0, P, HALF)
@@ -194,128 +182,123 @@ def tile_moe_tk_lin_bias_kernel(
         gather_words(1, 0, EARLY * C)
         quantise(2, 0, T)
 
-        gates = keep.tile([P, TOP * T + TOP * BLOCKS], F32, name="raw2", align_bytes=64)
-        acc = bank(0, P)
+        gates = keep.tile([P, (TOP - 1) * T + TOP * BLOCKS], F32, name="raw2", align_bytes=64)
+        gate_cols = gates[:, (TOP - 1) * T :]
+        acc = bank(4, P)
         nc.tensor.transpose(acc[:], gate_rows[:], ident[:])
-        nc.scalar.copy(gates[:, TOP * T :], acc[:, : TOP * BLOCKS])
-        for r in range(TOP):
-            acc = bank(r + 1, T)
+        nc.scalar.copy(gate_cols, acc[:, : TOP * BLOCKS])
+        for r in range(TOP - 1):
+            acc = bank(r + 5, T)
             for c in range(BLOCKS):
-                at = TOP * T + BLOCKS * r + c
-                nc.tensor.transpose(acc[:, P * c : P * (c + 1)], gates[:, at : at + 1].to_broadcast([P, P]), ident[:])
+                at = BLOCKS * r + c
+                nc.tensor.transpose(acc[:, P * c : P * (c + 1)], gate_cols[:, at : at + 1].to_broadcast([P, P]), ident[:])
             nc.scalar.copy(gates[:, T * r : T * (r + 1)], acc[:])
 
         late_words = keep.tile([P, S - EARLY * C], U32, name="grouped2", align_bytes=64)
-        gather_scales(0, C)
-        gather_scales(C, 2 * C)
-        move_scales(0, 2 * C, nc.scalar)
-        gather_scales(2 * C, 6 * C)
-        move_scales(2 * C, 6 * C, nc.scalar)
-        gather_words(1, EARLY * C, OPEN * C)
-        for lo in range(0, OPEN * C, 2 * C):
-            gather_words(2, lo, lo + 2 * C)
-        gather_scales(6 * C, S)
-        move_scales(6 * C, S, nc.sync)
-        for first in range(0, OPEN, 2):
-            for a in range(2):
-                for e in (first, first + 1):
-                    expert_pass(a, e)
-        for e in range(OPEN):
-            expert_pass(2, e)
-        for e in range(OPEN, OPEN + 2):
-            expert_pass(0, e)
-        for e in range(OPEN, E - 1):
-            if e % 2 == 0:
-                gather_words(1, C * e, C * (e + 2))
-            gather_words(2, C * e, C * (e + 1))
-            expert_pass(1, e)
-            expert_pass(2, e)
-            if e + 2 < E - 1:
-                expert_pass(0, e + 2)
-            if e + 2 == E - 1:
-                last_expert_pass(0)
-        last_expert_pass(1)
-        last_expert_pass(2)
-        nc.vector.tensor_scalar_add(y[1][:, S - 2 * C : S - C], sums[E - 2][1][:, 0, :], bias[:, 1, E - 2 : E - 1])
+        gather_scales(0, S // 2, nc.scalar)
+        gather_words(2, 0, 2 * C)
+        gather_scales(S // 2, S, nc.sync)
+        gather_words(1, 2 * C, 4 * C)
+        gather_words(2, 2 * C, 4 * C)
+        gather_words(1, 4 * C, 6 * C)
+        gather_words(2, 4 * C, 5 * C)
+        gather_words(2, 5 * C, 6 * C)
+        gather_words(1, 6 * C, S)
+        gather_words(2, 6 * C, 7 * C)
+        gather_words(2, 7 * C, 7 * C + P)
+        gather_words(2, 7 * C + P, S)
+        for a, e in ((0, 0), (0, 1), (1, 0), (1, 1), (0, 2), (0, 3), (2, 0), (2, 1), (1, 2), (1, 3), (2, 2), (0, 4), (2, 3), (0, 5),
+                     (1, 4), (2, 4), (1, 5), (0, 6), (2, 5), (0, 7), (1, 6), (2, 6), (1, 7), (2, 7)):
+            expert_pass(a, e)
 
-        prod = [keep.tile([P, TOP, T], F32, name="prod%d" % n) for n in range(NT)]
-        turned = [keep.tile([P, T], F32, name="turned%d" % n) for n in range(NT)]
-        final = keep.tile([P, T], F32, name="final")
-        last_list = keep.tile([P, T], F32, name="last_list")
+        def piece(name):
+            return keep.tile([P, T], F32, name=name)
 
-        def fetch(dst, n, r, lo=0, hi=T):
-            nc.vector.tensor_tensor(
-                dst[:, lo:hi], y[n][:].indirect(pos_t[r][:, lo // 16 : hi // 16]), gates[:, T * r + lo : T * r + hi], MULT
-            )
+        def fetch(n, r, name):
+            dst = piece(name)
+            nc.vector.tensor_tensor(dst[:], y[n][:].indirect(pos_t[r][:]), gates[:, T * r : T * (r + 1)], MULT)
+            return dst
 
-        def fetch_plain(n, r, hi=T):
-            nc.scalar.activation(prod[n][:, r, :hi], y[n][:].indirect(pos_t[r][:, : hi // 16]), COPY)
+        def fetch_plain(n, r):
+            dst = piece("plain%d%d" % (n, r))
+            nc.scalar.activation(dst[:], y[n][:].indirect(pos_t[r][:]), COPY)
+            return dst
 
-        def times_gate(n, r, lo=0, hi=T):
-            nc.vector.tensor_tensor(prod[n][:, r, lo:hi], prod[n][:, r, lo:hi], gates[:, T * r + lo : T * r + hi], MULT)
+        def turn(dst, src, opens=True, closes=True):
+            for c in range(BLOCKS):
+                nc.tensor.matmul(dst(c), lhsT=src(c), rhs=ident[:], is_transpose=True,
+                                 start=(opens and c == 0), stop=(closes and c == BLOCKS - 1))
 
-        def add_turned(total, n, r, lo, hi, first, final):
-            for c in range(lo, hi, P):
-                nc.tensor.matmul(
-                    total[:, c - lo : c - lo + P],
-                    lhsT=prod[n][:, r, c : c + P],
-                    rhs=ident[:],
-                    is_transpose=True,
-                    start=(r == first and c == lo),
-                    stop=(r == final and c == hi - P),
-                )
+        def blocks(t):
+            return lambda c: t[:, P * c : P * (c + 1)]
 
-        def turn_back(total, back, n, lo, hi):
-            nc.scalar.copy(turned[n][:, lo:hi], total[:])
-            for c in range(lo, hi, P):
-                nc.tensor.transpose(back[:, c - lo : c - lo + P], turned[n][:, c : c + P], ident[:])
+        def turn_one(dst, src, opens, closes):
+            nc.tensor.matmul(dst, lhsT=src, rhs=ident[:], is_transpose=True, start=opens, stop=closes)
 
-        def store(n, back):
-            res = keep.tile([P, T], F32, name="prod%d" % (n + 1))
-            nc.scalar.copy(res[:], back[:])
-            nc.sync.dma_start(out[P * n : P * (n + 1), :], res[:])
+        def gate_blocks(dst, turned, r, first=0, count=BLOCKS):
+            for c in range(first, first + count):
+                at = BLOCKS * r + c
+                nc.scalar.activation(blocks(dst)(c), blocks(turned)(c - first), COPY, scale=gate_cols[:, at : at + 1])
 
-        totals = [bank(0, T), bank(2, T)]
-        backs = [bank(1, T), bank(3, T)]
+        last = E - 1
+        f0 = [fetch(0, r, "f0%d" % r) for r in range(3)]
+        p3 = [fetch_plain(n, 3) for n in range(2)]
+        empty(last, 2, sums[last][1][:, 1, :])
+        p12 = fetch_plain(1, 2)
+        pair = [bank(1, 2, 2, P), bank(2, 2, 2, P)]
+        own = bank(3, T)
         for n in range(2):
-            for r in range(2):
-                fetch(prod[n][:, r, :], n, r)
-                fetch_plain(n, r + 2)
-                if (n, r) == (0, 0):
-                    late_product(E - 1, 1, 4)
-                if (n, r) == (0, 1):
-                    late_product(E - 2, 2, 5)
-                    late_product(E - 1, 2, 6)
-            for r in range(2, TOP):
-                times_gate(n, r)
-            for r in range(TOP):
-                add_turned(totals[n], n, r, 0, T, 0, 3)
-        n = NT - 1
-        fetch_plain(n, 2)
-        turn_back(totals[0], backs[0], 0, 0, T)
-        fetch_plain(n, 3, HALF)
-        turn_back(totals[1], backs[1], 1, 0, T)
-        store(0, backs[0])
+            for c in range(BLOCKS):
+                turn_one(pair[c // 2][:, c % 2, n, :], blocks(p3[n])(c), n == 0 and c % 2 == 0, n == 1 and c % 2 == 1)
+            turn(blocks(own), blocks(f0[n]), opens=(n == 0), closes=False)
+        turn(blocks(own), blocks(f0[2]), opens=False)
+        t12 = bank(4, T)
+        turn(blocks(t12), blocks(p12))
+        f1 = [fetch(1, r, "f1%d" % r) for r in range(2)]
+        nc.vector.tensor_tensor(f1[0][:], f1[0][:], f1[1][:], ADD)
+        f2 = keep.tile([P, 2, T], F32, name="f2")
+        for r in range(2):
+            nc.vector.tensor_tensor(f2[:, r, :], y[2][:].indirect(pos_t[r][:]), gates[:, T * r : T * (r + 1)], MULT)
 
-        pieces = ((0, HALF), (HALF, T))
-        totals = [bank(7, HALF), bank(4, HALF)]
-        fetch(prod[n][:, 0, :], n, 0)
-        times_gate(n, 2)
-        for r in (0, 2):
-            for total, (lo, hi) in zip(totals, pieces):
-                add_turned(total, n, r, lo, hi, 0, 3)
-        ends = []
-        for i, (lo, hi) in enumerate(pieces):
-            if i == 0:
-                times_gate(n, 3, lo, hi)
-            else:
-                fetch(prod[n][:, 3, :], n, 3, lo, hi)
-            add_turned(totals[i], n, 3, lo, hi, 0, 3)
-            ends.append(bank(5 + i, hi - lo))
-            turn_back(totals[i], ends[i], n, lo, hi)
-        store(1, backs[1])
-        for lo, hi in pieces:
-            fetch(last_list, n, 1, lo, hi)
-        for end, (lo, hi) in zip(ends, pieces):
-            nc.vector.tensor_tensor(final[:, lo:hi], end[:], last_list[:, lo:hi], ADD)
-            nc.sync.dma_start(out[P * n : P * (n + 1), lo:hi], final[:, lo:hi])
+        g3 = keep.tile([P, BLOCKS, 2, P], F32, name="g3")
+        back = [bank(5, T), bank(6, T)]
+        for c in range(BLOCKS):
+            at = BLOCKS * 3 + c
+            nc.scalar.activation(g3[:, c], pair[c // 2][:, c % 2], COPY, scale=gate_cols[:, at : at + 1])
+            for n in range(2):
+                turn_one(blocks(back[n])(c), g3[:, c, n, :], c == 0, False)
+        own_sum = piece("own_sum")
+        nc.scalar.copy(own_sum[:], own[:])
+        p22 = fetch_plain(2, 2)
+        t22 = bank(0, T)
+        turn(blocks(t22), blocks(p22))
+        turn(blocks(back[0]), blocks(own_sum), opens=False)
+        g12 = piece("g12")
+        gate_blocks(g12, t12, 2)
+        turn(blocks(back[1]), blocks(g12), opens=False)
+        p23 = piece("p23")
+        t23 = [bank(7, HALF), bank(3, HALF)]
+        for h in range(2):
+            nc.scalar.activation(p23[:, HALF * h : HALF * (h + 1)], y[2][:].indirect(pos_t[3][:, HALF * h // 16 : HALF * (h + 1) // 16]), COPY)
+            for c in range(2):
+                turn_one(blocks(t23[h])(c), blocks(p23)(2 * h + c), c == 0, c == 1)
+        g22 = piece("g22")
+        gate_blocks(g22, t22, 2)
+        ends = [bank(1, HALF), bank(2, HALF)]
+        for c in range(BLOCKS):
+            turn_one(blocks(ends[c // 2])(c % 2), blocks(g22)(c), c % 2 == 0, False)
+        g23 = piece("g23")
+        for h in range(2):
+            gate_blocks(g23, t23[h], 3, 2 * h, 2)
+            for c in range(2):
+                turn_one(blocks(ends[h])(c), blocks(g23)(2 * h + c), False, c == 1)
+        res = [piece("res%d" % n) for n in range(NT)]
+        nc.vector.tensor_tensor(res[1][:], back[1][:], f1[0][:], ADD)
+        nc.sync.dma_start(out[P : 2 * P, :], res[1][:])
+        nc.vector.tensor_tensor(f2[:, 0, :], f2[:, 0, :], f2[:, 1, :], ADD)
+        nc.scalar.copy(res[0][:], back[0][:])
+        nc.sync.dma_start(out[:P, :], res[0][:])
+        for h in range(2):
+            cols = slice(HALF * h, HALF * (h + 1))
+            nc.vector.tensor_tensor(res[2][:, cols], ends[h][:], f2[:, 0, cols], ADD)
+            nc.sync.dma_start(out[2 * P :, cols], res[2][:, cols])

@@ -31,7 +31,8 @@ SHORT = 1024
 ROW = (4, 0, 8)
 VECTOR_SHARE = 160
 OPEN = 4
-EARLY = 2
+GROUPS = ((0, 2), (2, 4), (4, 8))
+W8_ROW = 8
 
 
 def tile_moe_tk_lin_bias_kernel(
@@ -48,12 +49,12 @@ def tile_moe_tk_lin_bias_kernel(
         grouped = [keep.tile([P, T, 4], BF16, name="grouped%d" % a, align_bytes=64) for a in range(3)]
         words = keep.tile([P, 2 * T + LONG], U32, name="words", align_bytes=64)
         scales = keep.tile([P, LONG], U8, name="scales", align_bytes=64)
-        slot_words = [keep.tile([P, EARLY * C if a == 1 else S], U32, name="slot_words%d" % a, align_bytes=64) for a in range(3)]
+        slot_words = [keep.tile([P, S if a == 2 else S // 2], U32, name="slot_words%d" % a, align_bytes=64) for a in range(3)]
         slot_scales = keep.tile([P, S], U8, name="slot_scales", align_bytes=64)
         ident = keep.tile([P, P], F32, name="ident")
         moved_scales = keep.tile([P, S], U8, name="moved_scales", align_bytes=64)
-        w8 = [keep.tile([P, E // 2, 4 * N], U8, name="w8_%d" % h, align_bytes=64) for h in range(2)]
-        w4 = [keep.tile([P, 2 * n, 2 * N], U8, name="w4_%d" % h, align_bytes=64) for h, n in enumerate((EARLY, E - EARLY))]
+        w8 = [keep.tile([P, hi - lo, 4 * N], U8, name="w8_%d" % lo, align_bytes=64) for lo, hi in GROUPS]
+        w4 = [keep.tile([P, 2 * (hi - lo), 2 * N], U8, name="w4_%d" % lo, align_bytes=64) for lo, hi in GROUPS]
         s8 = keep.tile([P, E, N], U8, name="s8", align_bytes=64)
         bias = keep.tile([P, NT, E], F32, name="bias")
         y = [keep.tile([P, S], F32, name="y%d" % n) for n in range(NT)]
@@ -66,22 +67,23 @@ def tile_moe_tk_lin_bias_kernel(
         nc.sync.dma_start(raw[0][:, :, :HALF], xv[0, :, :, :HALF])
         nc.sync.dma_start(raw[0][:, :, HALF:], xv[0, :, :, HALF:])
         nc.sync.dma_start(offs_t[:], offs)
-        nc.sync.dma_start(raw[1][:], xv[1])
-        nc.sync.dma_start(raw[2][:], xv[2])
+        for a in (1, 2):
+            for lo in (0, HALF):
+                nc.sync.dma_start(raw[a][:, :, lo : lo + HALF], xv[a, :, :, lo : lo + HALF])
         runs = gate.rearrange("r n (c t) -> (r n c) t", t=P)
-        nc.gpsimd.dma_start(gate_rows[: TOP * BLOCKS, :], runs[0 : (TOP * BLOCKS - 1) * (N + 1) + 1 : N + 1])
+        nc.gpsimd.dma_start(gate_rows[: 2 * BLOCKS, :], runs[2 * BLOCKS * (N + 1) : (TOP * BLOCKS - 1) * (N + 1) + 1 : N + 1])
         nc.gpsimd.dma_start(bias[:], b.rearrange("(c p) e -> p c e", p=P))
         v8 = w8_scales.rearrange("e a q n -> q (e a) n")
         v4 = w4_scales.rearrange("e a q n -> q (e a) n")
         w8v = w8_words.rearrange("e a p n r -> p (e a) (n r)")
         w4v = w4_words.rearrange("e a p n -> p (e a) n")
 
-        nc.sync.dma_start(w8[0][:].bitcast(I32), w8v[:, : E // 2].bitcast(I32))
-        for q in range(4):
-            nc.sync.dma_start(s8[q:P:32, :, :].bitcast(I32), v8[q:16:4].bitcast(I32))
-        nc.sync.dma_start(w4[0][:].bitcast(I32), w4v[:, : 2 * EARLY].bitcast(I32))
-        nc.sync.dma_start(w8[1][:].bitcast(I32), w8v[:, E // 2 :].bitcast(I32))
-        nc.sync.dma_start(w4[1][:].bitcast(I32), w4v[:, 2 * EARLY :].bitcast(I32))
+        for g, (lo, hi) in enumerate(GROUPS):
+            nc.sync.dma_start(w8[g][:].bitcast(I32), w8v[:, lo:hi].bitcast(I32))
+            if g == 0:
+                for q in range(4):
+                    nc.sync.dma_start(s8[W8_ROW + q : P : 32, :, :].bitcast(I32), v8[q:16:4].bitcast(I32))
+            nc.sync.dma_start(w4[g][:].bitcast(I32), w4v[:, 2 * lo : 2 * hi].bitcast(I32))
         for r, pos in enumerate((pos1, pos2, pos3, pos4)):
             nc.sync.dma_start(pos_t[r][:], pos)
         nc.vector.memset(scales[:].bitcast(I32), 0)
@@ -104,8 +106,8 @@ def tile_moe_tk_lin_bias_kernel(
             )
 
         def in_slots(a, lo, hi):
-            if a == 1 and lo >= EARLY * C:
-                return late_words[:, lo - EARLY * C : hi - EARLY * C]
+            if a < 2 and lo >= S // 2:
+                return late_words[:, a, lo - S // 2 : hi - S // 2]
             return slot_words[a][:, lo:hi]
 
         def gather_words(a, lo, hi):
@@ -113,20 +115,22 @@ def tile_moe_tk_lin_bias_kernel(
             window = words[:, (2 - a) * T : (2 - a) * T + width]
             nc.vector.tensor_copy(in_slots(a, lo, hi), window.indirect(offs_t[:, lo // 16 : hi // 16]))
 
-        def gather_scales(lo, hi, queue):
+        def gather_scales(lo, hi):
             nc.vector.tensor_copy(slot_scales[:, lo:hi], scales[:].indirect(offs_t[:, lo // 16 : hi // 16]))
+
+        def move_scales(lo, hi, queue):
             queue.dma_start(moved_scales[: P - ROW[2], lo:hi].bitcast(I32), slot_scales[ROW[2] :, lo:hi].bitcast(I32))
 
         def weights(a, e, n):
+            g = max(g for g, (lo, hi) in enumerate(GROUPS) if lo <= e)
+            i = e - GROUPS[g][0]
             if a == 0:
-                h, i = divmod(e, E // 2)
-                return w8[h][:, i, 4 * P * n : 4 * P * (n + 1)].bitcast(FP8X4)
-            h, i = (0, e) if e < EARLY else (1, e - EARLY)
-            return w4[h][:, 2 * i + a - 1, 2 * P * n : 2 * P * (n + 1)].bitcast(FP4X4)
+                return w8[g][:, i, 4 * P * n : 4 * P * (n + 1)].bitcast(FP8X4)
+            return w4[g][:, 2 * i + a - 1, 2 * P * n : 2 * P * (n + 1)].bitcast(FP4X4)
 
         def multiply(a, e, n, acc, lo=0, hi=C, opens=True, closes=True):
             cols = slice(C * e + lo, C * e + hi)
-            w_scales = s8[:, e, :] if a == 0 else s4[:, 2 * e + a - 1, :]
+            w_scales = s8[W8_ROW:, e, :] if a == 0 else s4[:, 2 * e + a - 1, :]
             nc.tensor.matmul_mx(
                 out=acc,
                 lhsT=weights(a, e, n),
@@ -171,44 +175,48 @@ def tile_moe_tk_lin_bias_kernel(
         interleave(0, HALF, HALF + VECTOR_SHARE, on_vector=True)
         interleave(0, HALF + VECTOR_SHARE, T)
         quantise(0, HALF, T)
-        interleave(1, 0, T)
-        interleave(2, 0, T)
-        for lo in range(0, S, S // 2):
-            gather_words(0, lo, lo + S // 2)
+        for a in (1, 2):
+            for lo in (0, HALF):
+                interleave(a, lo, lo + HALF)
+        gather_words(0, 0, S // 2)
         quantise(1, 0, T)
-        s4 = keep.tile([P, 2 * E, N], U8, name="raw0", align_bytes=64)
+        s4 = keep.tile([P, 2 * E, N], U8, name="raw1", align_bytes=64)
         for q in range(4):
             nc.gpsimd.dma_start(s4[q:P:32, :, :].bitcast(I32), v4[q:16:4].bitcast(I32))
-        gather_words(1, 0, EARLY * C)
+        gather_words(1, 0, S // 2)
         quantise(2, 0, T)
 
-        gates = keep.tile([P, (TOP - 1) * T + TOP * BLOCKS], F32, name="raw2", align_bytes=64)
-        gate_cols = gates[:, (TOP - 1) * T :]
-        acc = bank(4, P)
+        gate_cols = keep.tile([P, 2 * BLOCKS], F32, name="raw2", align_bytes=64)
+        acc = bank(7, P)
         nc.tensor.transpose(acc[:], gate_rows[:], ident[:])
-        nc.scalar.copy(gate_cols, acc[:, : TOP * BLOCKS])
-        for r in range(TOP - 1):
-            acc = bank(r + 5, T)
-            for c in range(BLOCKS):
-                at = BLOCKS * r + c
-                nc.tensor.transpose(acc[:, P * c : P * (c + 1)], gate_cols[:, at : at + 1].to_broadcast([P, P]), ident[:])
-            nc.scalar.copy(gates[:, T * r : T * (r + 1)], acc[:])
+        nc.scalar.copy(gate_cols[:], acc[:, : 2 * BLOCKS])
 
-        late_words = keep.tile([P, S - EARLY * C], U32, name="grouped2", align_bytes=64)
-        gather_scales(0, S // 2, nc.scalar)
+        late_words = keep.tile([P, 2, S // 2], U32, name="grouped2", align_bytes=64)
+        gather_scales(0, C)
+        gather_scales(C, S // 2)
+        move_scales(0, S // 2, nc.scalar)
         gather_words(2, 0, 2 * C)
-        gather_scales(S // 2, S, nc.sync)
-        gather_words(1, 2 * C, 4 * C)
+        gather_scales(S // 2, S)
+        move_scales(S // 2, S, nc.sync)
         gather_words(2, 2 * C, 4 * C)
+        gather_words(0, 4 * C, 6 * C)
         gather_words(1, 4 * C, 6 * C)
         gather_words(2, 4 * C, 5 * C)
+        gather_words(0, 6 * C, S)
         gather_words(2, 5 * C, 6 * C)
         gather_words(1, 6 * C, S)
         gather_words(2, 6 * C, 7 * C)
         gather_words(2, 7 * C, 7 * C + P)
         gather_words(2, 7 * C + P, S)
-        for a, e in ((0, 0), (0, 1), (1, 0), (1, 1), (0, 2), (0, 3), (2, 0), (2, 1), (1, 2), (1, 3), (2, 2), (0, 4), (2, 3), (0, 5),
-                     (1, 4), (2, 4), (1, 5), (0, 6), (2, 5), (0, 7), (1, 6), (2, 6), (1, 7), (2, 7)):
+        for e in range(OPEN):
+            expert_pass(0, e)
+            expert_pass(1, e)
+        for e in range(OPEN):
+            expert_pass(2, e)
+            if e == 1:
+                gates = keep.tile([P, TOP - 1, T], F32, name="w4_0", align_bytes=64)
+                nc.sync.dma_start(gates[:], gate[: TOP - 1, :P, :].rearrange("r p t -> p r t"))
+        for a, e in ((0, 4), (0, 5), (1, 4), (1, 5), (2, 4), (0, 6), (0, 7), (2, 5), (1, 6), (1, 7), (2, 6), (2, 7)):
             expert_pass(a, e)
 
         def piece(name):
@@ -216,7 +224,7 @@ def tile_moe_tk_lin_bias_kernel(
 
         def fetch(n, r, name):
             dst = piece(name)
-            nc.vector.tensor_tensor(dst[:], y[n][:].indirect(pos_t[r][:]), gates[:, T * r : T * (r + 1)], MULT)
+            nc.vector.tensor_tensor(dst[:], y[n][:].indirect(pos_t[r][:]), gates[:, r, :], MULT)
             return dst
 
         def fetch_plain(n, r):
@@ -237,7 +245,7 @@ def tile_moe_tk_lin_bias_kernel(
 
         def gate_blocks(dst, turned, r, first=0, count=BLOCKS):
             for c in range(first, first + count):
-                at = BLOCKS * r + c
+                at = BLOCKS * (r - 2) + c
                 nc.scalar.activation(blocks(dst)(c), blocks(turned)(c - first), COPY, scale=gate_cols[:, at : at + 1])
 
         last = E - 1
@@ -258,12 +266,12 @@ def tile_moe_tk_lin_bias_kernel(
         nc.vector.tensor_tensor(f1[0][:], f1[0][:], f1[1][:], ADD)
         f2 = keep.tile([P, 2, T], F32, name="f2")
         for r in range(2):
-            nc.vector.tensor_tensor(f2[:, r, :], y[2][:].indirect(pos_t[r][:]), gates[:, T * r : T * (r + 1)], MULT)
+            nc.vector.tensor_tensor(f2[:, r, :], y[2][:].indirect(pos_t[r][:]), gates[:, r, :], MULT)
 
         g3 = keep.tile([P, BLOCKS, 2, P], F32, name="g3")
         back = [bank(5, T), bank(6, T)]
         for c in range(BLOCKS):
-            at = BLOCKS * 3 + c
+            at = BLOCKS + c
             nc.scalar.activation(g3[:, c], pair[c // 2][:, c % 2], COPY, scale=gate_cols[:, at : at + 1])
             for n in range(2):
                 turn_one(blocks(back[n])(c), g3[:, c, n, :], c == 0, False)

@@ -58,9 +58,7 @@ def tile_moe_tk_lin_bias_kernel(
         s8 = keep.tile([P, E, N], U8, name="s8", align_bytes=64)
         bias = keep.tile([P, NT, E], F32, name="bias")
         y = [keep.tile([P, S], F32, name="y%d" % n) for n in range(NT)]
-        gate_rows = keep.tile([P, P], F32, name="gate_rows")
 
-        nc.gpsimd.memset(gate_rows[:], 0.0)
         make_identity(nc, ident[:])
         nc.vector.memset(s8[:].rearrange("p e n -> p (e n)").bitcast(I32), 0)
         xv = xT.rearrange("(a p j) t -> a p j t", p=P, j=4)
@@ -70,8 +68,6 @@ def tile_moe_tk_lin_bias_kernel(
         for a in (1, 2):
             for lo in (0, HALF):
                 nc.sync.dma_start(raw[a][:, :, lo : lo + HALF], xv[a, :, :, lo : lo + HALF])
-        runs = gate.rearrange("r n (c t) -> (r n c) t", t=P)
-        nc.gpsimd.dma_start(gate_rows[: 2 * BLOCKS, :], runs[2 * BLOCKS * (N + 1) : (TOP * BLOCKS - 1) * (N + 1) + 1 : N + 1])
         nc.gpsimd.dma_start(bias[:], b.rearrange("(c p) e -> p c e", p=P))
         v8 = w8_scales.rearrange("e a q n -> q (e a) n")
         v4 = w4_scales.rearrange("e a q n -> q (e a) n")
@@ -186,11 +182,6 @@ def tile_moe_tk_lin_bias_kernel(
         gather_words(1, 0, S // 2)
         quantise(2, 0, T)
 
-        gate_cols = keep.tile([P, 2 * BLOCKS], F32, name="raw2", align_bytes=64)
-        acc = bank(7, P)
-        nc.tensor.transpose(acc[:], gate_rows[:], ident[:])
-        nc.scalar.copy(gate_cols[:], acc[:, : 2 * BLOCKS])
-
         late_words = keep.tile([P, 2, S // 2], U32, name="grouped2", align_bytes=64)
         gather_scales(0, C)
         gather_scales(C, S // 2)
@@ -214,99 +205,86 @@ def tile_moe_tk_lin_bias_kernel(
         for e in range(OPEN):
             expert_pass(2, e)
             if e == 1:
-                gates = keep.tile([P, TOP - 1, T], F32, name="w4_0", align_bytes=64)
-                nc.sync.dma_start(gates[:], gate[: TOP - 1, :P, :].rearrange("r p t -> p r t"))
+                gates = keep.tile([P, TOP, T], F32, name="w4_0", align_bytes=64)
+                nc.sync.dma_start(gates[:], gate[:, :P, :].rearrange("r p t -> p r t"))
         for a, e in ((0, 4), (0, 5), (1, 4), (1, 5), (2, 4), (0, 6), (0, 7), (2, 5), (1, 6), (1, 7), (2, 6), (2, 7)):
             expert_pass(a, e)
 
-        def piece(name):
-            return keep.tile([P, T], F32, name=name)
+        prod = [keep.tile([P, TOP, T], F32, name="prod%d" % n) for n in range(NT)]
+        turned = [keep.tile([P, T], F32, name="turned%d" % n) for n in range(NT)]
+        final = keep.tile([P, T], F32, name="final")
+        last_list = keep.tile([P, T], F32, name="last_list")
 
-        def fetch(n, r, name):
-            dst = piece(name)
-            nc.vector.tensor_tensor(dst[:], y[n][:].indirect(pos_t[r][:]), gates[:, r, :], MULT)
-            return dst
+        def fetch(dst, n, r, lo=0, hi=T):
+            nc.vector.tensor_tensor(
+                dst[:, lo:hi], y[n][:].indirect(pos_t[r][:, lo // 16 : hi // 16]), gates[:, r, lo:hi], MULT
+            )
 
-        def fetch_plain(n, r):
-            dst = piece("plain%d%d" % (n, r))
-            nc.scalar.activation(dst[:], y[n][:].indirect(pos_t[r][:]), COPY)
-            return dst
+        def fetch_plain(n, r, hi=T):
+            nc.scalar.activation(prod[n][:, r, :hi], y[n][:].indirect(pos_t[r][:, : hi // 16]), COPY)
 
-        def turn(dst, src, opens=True, closes=True):
-            for c in range(BLOCKS):
-                nc.tensor.matmul(dst(c), lhsT=src(c), rhs=ident[:], is_transpose=True,
-                                 start=(opens and c == 0), stop=(closes and c == BLOCKS - 1))
+        def times_gate(n, r, lo=0, hi=T):
+            nc.vector.tensor_tensor(prod[n][:, r, lo:hi], prod[n][:, r, lo:hi], gates[:, r, lo:hi], MULT)
 
-        def blocks(t):
-            return lambda c: t[:, P * c : P * (c + 1)]
+        def add_turned(total, n, r, lo, hi, first, final):
+            for c in range(lo, hi, P):
+                nc.tensor.matmul(
+                    total[:, c - lo : c - lo + P],
+                    lhsT=prod[n][:, r, c : c + P],
+                    rhs=ident[:],
+                    is_transpose=True,
+                    start=(r == first and c == lo),
+                    stop=(r == final and c == hi - P),
+                )
 
-        def turn_one(dst, src, opens, closes):
-            nc.tensor.matmul(dst, lhsT=src, rhs=ident[:], is_transpose=True, start=opens, stop=closes)
+        def turn_back(total, back, n, lo, hi):
+            nc.scalar.copy(turned[n][:, lo:hi], total[:])
+            for c in range(lo, hi, P):
+                nc.tensor.transpose(back[:, c - lo : c - lo + P], turned[n][:, c : c + P], ident[:])
 
-        def gate_blocks(dst, turned, r, first=0, count=BLOCKS):
-            for c in range(first, first + count):
-                at = BLOCKS * (r - 2) + c
-                nc.scalar.activation(blocks(dst)(c), blocks(turned)(c - first), COPY, scale=gate_cols[:, at : at + 1])
+        def store(n, back):
+            res = keep.tile([P, T], F32, name="prod%d" % (n + 1))
+            nc.scalar.copy(res[:], back[:])
+            nc.sync.dma_start(out[P * n : P * (n + 1), :], res[:])
 
-        last = E - 1
-        f0 = [fetch(0, r, "f0%d" % r) for r in range(3)]
-        p3 = [fetch_plain(n, 3) for n in range(2)]
-        empty(last, 2, sums[last][1][:, 1, :])
-        p12 = fetch_plain(1, 2)
-        pair = [bank(1, 2, 2, P), bank(2, 2, 2, P)]
-        own = bank(3, T)
+        totals = [bank(0, T), bank(2, T)]
+        backs = [bank(1, T), bank(3, T)]
         for n in range(2):
-            for c in range(BLOCKS):
-                turn_one(pair[c // 2][:, c % 2, n, :], blocks(p3[n])(c), n == 0 and c % 2 == 0, n == 1 and c % 2 == 1)
-            turn(blocks(own), blocks(f0[n]), opens=(n == 0), closes=False)
-        turn(blocks(own), blocks(f0[2]), opens=False)
-        t12 = bank(4, T)
-        turn(blocks(t12), blocks(p12))
-        f1 = [fetch(1, r, "f1%d" % r) for r in range(2)]
-        nc.vector.tensor_tensor(f1[0][:], f1[0][:], f1[1][:], ADD)
-        f2 = keep.tile([P, 2, T], F32, name="f2")
-        for r in range(2):
-            nc.vector.tensor_tensor(f2[:, r, :], y[2][:].indirect(pos_t[r][:]), gates[:, r, :], MULT)
+            for r in range(2):
+                fetch(prod[n][:, r, :], n, r)
+                fetch_plain(n, r + 2)
+                if (n, r) == (0, 0):
+                    empty(E - 1, 2, sums[E - 1][1][:, 1, :])
+            for r in range(2, TOP):
+                times_gate(n, r)
+            for r in range(TOP):
+                add_turned(totals[n], n, r, 0, T, 0, 3)
+        n = NT - 1
+        fetch_plain(n, 2)
+        turn_back(totals[0], backs[0], 0, 0, T)
+        fetch_plain(n, 3, HALF)
+        turn_back(totals[1], backs[1], 1, 0, T)
+        store(0, backs[0])
 
-        g3 = keep.tile([P, BLOCKS, 2, P], F32, name="g3")
-        back = [bank(5, T), bank(6, T)]
-        for c in range(BLOCKS):
-            at = BLOCKS + c
-            nc.scalar.activation(g3[:, c], pair[c // 2][:, c % 2], COPY, scale=gate_cols[:, at : at + 1])
-            for n in range(2):
-                turn_one(blocks(back[n])(c), g3[:, c, n, :], c == 0, False)
-        own_sum = piece("own_sum")
-        nc.scalar.copy(own_sum[:], own[:])
-        p22 = fetch_plain(2, 2)
-        t22 = bank(0, T)
-        turn(blocks(t22), blocks(p22))
-        turn(blocks(back[0]), blocks(own_sum), opens=False)
-        g12 = piece("g12")
-        gate_blocks(g12, t12, 2)
-        turn(blocks(back[1]), blocks(g12), opens=False)
-        p23 = piece("p23")
-        t23 = [bank(7, HALF), bank(3, HALF)]
-        for h in range(2):
-            nc.scalar.activation(p23[:, HALF * h : HALF * (h + 1)], y[2][:].indirect(pos_t[3][:, HALF * h // 16 : HALF * (h + 1) // 16]), COPY)
-            for c in range(2):
-                turn_one(blocks(t23[h])(c), blocks(p23)(2 * h + c), c == 0, c == 1)
-        g22 = piece("g22")
-        gate_blocks(g22, t22, 2)
-        ends = [bank(1, HALF), bank(2, HALF)]
-        for c in range(BLOCKS):
-            turn_one(blocks(ends[c // 2])(c % 2), blocks(g22)(c), c % 2 == 0, False)
-        g23 = piece("g23")
-        for h in range(2):
-            gate_blocks(g23, t23[h], 3, 2 * h, 2)
-            for c in range(2):
-                turn_one(blocks(ends[h])(c), blocks(g23)(2 * h + c), False, c == 1)
-        res = [piece("res%d" % n) for n in range(NT)]
-        nc.vector.tensor_tensor(res[1][:], back[1][:], f1[0][:], ADD)
-        nc.sync.dma_start(out[P : 2 * P, :], res[1][:])
-        nc.vector.tensor_tensor(f2[:, 0, :], f2[:, 0, :], f2[:, 1, :], ADD)
-        nc.scalar.copy(res[0][:], back[0][:])
-        nc.sync.dma_start(out[:P, :], res[0][:])
-        for h in range(2):
-            cols = slice(HALF * h, HALF * (h + 1))
-            nc.vector.tensor_tensor(res[2][:, cols], ends[h][:], f2[:, 0, cols], ADD)
-            nc.sync.dma_start(out[2 * P :, cols], res[2][:, cols])
+        pieces = ((0, HALF), (HALF, T))
+        totals = [bank(7, HALF), bank(4, HALF)]
+        fetch(prod[n][:, 0, :], n, 0)
+        times_gate(n, 2)
+        for r in (0, 2):
+            for total, (lo, hi) in zip(totals, pieces):
+                add_turned(total, n, r, lo, hi, 0, 3)
+        ends = []
+        for i, (lo, hi) in enumerate(pieces):
+            if i == 0:
+                times_gate(n, 3, lo, hi)
+            else:
+                fetch(prod[n][:, 3, :], n, 3, lo, hi)
+            add_turned(totals[i], n, 3, lo, hi, 0, 3)
+            ends.append(bank(5 + i, hi - lo))
+            turn_back(totals[i], ends[i], n, lo, hi)
+        store(1, backs[1])
+        for lo, hi in pieces:
+            fetch(last_list, n, 1, lo, hi)
+        for end, (lo, hi) in zip(ends, pieces):
+            nc.vector.tensor_tensor(final[:, lo:hi], end[:], last_list[:, lo:hi], ADD)
+            nc.sync.dma_start(out[P * n : P * (n + 1), lo:hi], final[:, lo:hi])

@@ -31,8 +31,7 @@ SHORT = 1024
 ROW = (4, 0, 8)
 VECTOR_SHARE = 160
 OPEN = 4
-GROUPS = ((0, 2), (2, 4), (4, 8))
-W8_ROW = 8
+EARLY = 2
 
 
 def tile_moe_tk_lin_bias_kernel(
@@ -49,37 +48,40 @@ def tile_moe_tk_lin_bias_kernel(
         grouped = [keep.tile([P, T, 4], BF16, name="grouped%d" % a, align_bytes=64) for a in range(3)]
         words = keep.tile([P, 2 * T + LONG], U32, name="words", align_bytes=64)
         scales = keep.tile([P, LONG], U8, name="scales", align_bytes=64)
-        slot_words = [keep.tile([P, S if a == 2 else S // 2], U32, name="slot_words%d" % a, align_bytes=64) for a in range(3)]
+        slot_words = [keep.tile([P, EARLY * C if a == 1 else S], U32, name="slot_words%d" % a, align_bytes=64) for a in range(3)]
         slot_scales = keep.tile([P, S], U8, name="slot_scales", align_bytes=64)
         ident = keep.tile([P, P], F32, name="ident")
         moved_scales = keep.tile([P, S], U8, name="moved_scales", align_bytes=64)
-        w8 = [keep.tile([P, hi - lo, 4 * N], U8, name="w8_%d" % lo, align_bytes=64) for lo, hi in GROUPS]
-        w4 = [keep.tile([P, 2 * (hi - lo), 2 * N], U8, name="w4_%d" % lo, align_bytes=64) for lo, hi in GROUPS]
+        w8 = [keep.tile([P, E // 2, 4 * N], U8, name="w8_%d" % h, align_bytes=64) for h in range(2)]
+        w4 = [keep.tile([P, E, 2 * N], U8, name="w4_%d" % h, align_bytes=64) for h in range(2)]
         s8 = keep.tile([P, E, N], U8, name="s8", align_bytes=64)
         bias = keep.tile([P, NT, E], F32, name="bias")
         y = [keep.tile([P, S], F32, name="y%d" % n) for n in range(NT)]
+        gate_rows = keep.tile([P, P], F32, name="gate_rows")
 
+        nc.gpsimd.memset(gate_rows[:], 0.0)
         make_identity(nc, ident[:])
         nc.vector.memset(s8[:].rearrange("p e n -> p (e n)").bitcast(I32), 0)
         xv = xT.rearrange("(a p j) t -> a p j t", p=P, j=4)
         nc.sync.dma_start(raw[0][:, :, :HALF], xv[0, :, :, :HALF])
         nc.sync.dma_start(raw[0][:, :, HALF:], xv[0, :, :, HALF:])
         nc.sync.dma_start(offs_t[:], offs)
-        for a in (1, 2):
-            for lo in (0, HALF):
-                nc.sync.dma_start(raw[a][:, :, lo : lo + HALF], xv[a, :, :, lo : lo + HALF])
+        nc.sync.dma_start(raw[1][:], xv[1])
+        nc.sync.dma_start(raw[2][:], xv[2])
+        runs = gate.rearrange("r n (c t) -> (r n c) t", t=P)
+        nc.gpsimd.dma_start(gate_rows[: TOP * BLOCKS, :], runs[0 : (TOP * BLOCKS - 1) * (N + 1) + 1 : N + 1])
         nc.gpsimd.dma_start(bias[:], b.rearrange("(c p) e -> p c e", p=P))
         v8 = w8_scales.rearrange("e a q n -> q (e a) n")
         v4 = w4_scales.rearrange("e a q n -> q (e a) n")
         w8v = w8_words.rearrange("e a p n r -> p (e a) (n r)")
         w4v = w4_words.rearrange("e a p n -> p (e a) n")
 
-        for g, (lo, hi) in enumerate(GROUPS):
-            nc.sync.dma_start(w8[g][:].bitcast(I32), w8v[:, lo:hi].bitcast(I32))
-            if g == 0:
-                for q in range(4):
-                    nc.sync.dma_start(s8[W8_ROW + q : P : 32, :, :].bitcast(I32), v8[q:16:4].bitcast(I32))
-            nc.sync.dma_start(w4[g][:].bitcast(I32), w4v[:, 2 * lo : 2 * hi].bitcast(I32))
+        nc.sync.dma_start(w8[0][:].bitcast(I32), w8v[:, : E // 2].bitcast(I32))
+        for q in range(4):
+            nc.sync.dma_start(s8[q:P:32, :, :].bitcast(I32), v8[q:16:4].bitcast(I32))
+        nc.sync.dma_start(w4[0][:].bitcast(I32), w4v[:, :E].bitcast(I32))
+        nc.sync.dma_start(w8[1][:].bitcast(I32), w8v[:, E // 2 :].bitcast(I32))
+        nc.sync.dma_start(w4[1][:].bitcast(I32), w4v[:, E:].bitcast(I32))
         for r, pos in enumerate((pos1, pos2, pos3, pos4)):
             nc.sync.dma_start(pos_t[r][:], pos)
         nc.vector.memset(scales[:].bitcast(I32), 0)
@@ -102,8 +104,8 @@ def tile_moe_tk_lin_bias_kernel(
             )
 
         def in_slots(a, lo, hi):
-            if a < 2 and lo >= S // 2:
-                return late_words[:, a, lo - S // 2 : hi - S // 2]
+            if a == 1 and lo >= EARLY * C:
+                return late_words[:, lo - EARLY * C : hi - EARLY * C]
             return slot_words[a][:, lo:hi]
 
         def gather_words(a, lo, hi):
@@ -118,15 +120,14 @@ def tile_moe_tk_lin_bias_kernel(
             queue.dma_start(moved_scales[: P - ROW[2], lo:hi].bitcast(I32), slot_scales[ROW[2] :, lo:hi].bitcast(I32))
 
         def weights(a, e, n):
-            g = max(g for g, (lo, hi) in enumerate(GROUPS) if lo <= e)
-            i = e - GROUPS[g][0]
+            h, i = divmod(e, E // 2)
             if a == 0:
-                return w8[g][:, i, 4 * P * n : 4 * P * (n + 1)].bitcast(FP8X4)
-            return w4[g][:, 2 * i + a - 1, 2 * P * n : 2 * P * (n + 1)].bitcast(FP4X4)
+                return w8[h][:, i, 4 * P * n : 4 * P * (n + 1)].bitcast(FP8X4)
+            return w4[h][:, 2 * i + a - 1, 2 * P * n : 2 * P * (n + 1)].bitcast(FP4X4)
 
         def multiply(a, e, n, acc, lo=0, hi=C, opens=True, closes=True):
             cols = slice(C * e + lo, C * e + hi)
-            w_scales = s8[W8_ROW:, e, :] if a == 0 else s4[:, 2 * e + a - 1, :]
+            w_scales = s8[:, e, :] if a == 0 else s4[:, 2 * e + a - 1, :]
             nc.tensor.matmul_mx(
                 out=acc,
                 lhsT=weights(a, e, n),
@@ -146,24 +147,35 @@ def tile_moe_tk_lin_bias_kernel(
         sums = {}
 
         def expert_pass(a, e):
-            last = e == E - 1
+            rows = range(1, min(NT, E - e))
             if a == 0:
-                first = [bank(6, P), bank(0, P)] if last else [bank(2 * (e % OPEN), C)]
-                sums[e] = (first, bank(2 * (e % OPEN) + 1, NT - 1, C))
+                sums[e] = (bank(2 * (e % OPEN), C), bank(2 * (e % OPEN) + 1, len(rows), C))
             first, others = sums[e]
-            width = C // len(first)
-            for i, acc in enumerate(first):
-                multiply(a, e, 0, acc[:], i * width, (i + 1) * width)
-                if a == 2:
-                    empty(e, 0, acc[:], i * width, (i + 1) * width)
-            for n in range(1, NT):
-                multiply(a, e, n, others[:, n - 1, :], opens=(n == 1), closes=(n == NT - 1))
+            multiply(a, e, 0, first[:])
+            for n in rows:
+                multiply(a, e, n, others[:, n - 1, :], opens=(n == rows[0]), closes=(n == rows[-1]))
             if a == 2:
-                for n in range(1, NT):
+                empty(e, 0, first[:])
+                for n in rows:
                     if e < E - 2:
                         empty(e, n, others[:, n - 1, :])
-                    elif (e, n) != (E - 1, NT - 1):
-                        nc.vector.tensor_scalar_add(y[n][:, C * e : C * (e + 1)], others[:, n - 1, :], bias[:, n, e : e + 1])
+
+        def last_expert_pass(a):
+            e = E - 1
+            if a == 0:
+                sums[e] = (bank(6, P), bank(7, P))
+            for half, lo in zip(sums[e], (0, P)):
+                if a == 2:
+                    gather_words(2, C * e + lo, C * e + lo + P)
+                multiply(a, e, 0, half[:], lo, lo + P)
+                if a == 2:
+                    empty(e, 0, half[:], lo, lo + P)
+
+        def late_product(e, n, i):
+            acc = bank(i, C)
+            for a in range(3):
+                multiply(a, e, n, acc[:])
+            empty(e, n, acc[:])
 
         interleave(0, 0, P, on_vector=True)
         interleave(0, P, HALF)
@@ -171,120 +183,153 @@ def tile_moe_tk_lin_bias_kernel(
         interleave(0, HALF, HALF + VECTOR_SHARE, on_vector=True)
         interleave(0, HALF + VECTOR_SHARE, T)
         quantise(0, HALF, T)
-        for a in (1, 2):
-            for lo in (0, HALF):
-                interleave(a, lo, lo + HALF)
-        gather_words(0, 0, S // 2)
+        interleave(1, 0, T)
+        interleave(2, 0, T)
+        for lo in range(0, S, S // 2):
+            gather_words(0, lo, lo + S // 2)
         quantise(1, 0, T)
-        s4 = keep.tile([P, 2 * E, N], U8, name="raw1", align_bytes=64)
+        s4 = keep.tile([P, 2 * E, N], U8, name="raw0", align_bytes=64)
         for q in range(4):
             nc.gpsimd.dma_start(s4[q:P:32, :, :].bitcast(I32), v4[q:16:4].bitcast(I32))
-        gather_words(1, 0, S // 2)
+        gather_words(1, 0, EARLY * C)
         quantise(2, 0, T)
 
-        late_words = keep.tile([P, 2, S // 2], U32, name="grouped2", align_bytes=64)
+        gates = keep.tile([P, (TOP - 1) * T + TOP * BLOCKS], F32, name="raw2", align_bytes=64)
+        gate_cols = gates[:, (TOP - 1) * T :]
+        acc = bank(0, P)
+        nc.tensor.transpose(acc[:], gate_rows[:], ident[:])
+        nc.scalar.copy(gate_cols, acc[:, : TOP * BLOCKS])
+        for r in range(TOP - 1):
+            acc = bank(r + 1, T)
+            for c in range(BLOCKS):
+                at = BLOCKS * r + c
+                nc.tensor.transpose(acc[:, P * c : P * (c + 1)], gate_cols[:, at : at + 1].to_broadcast([P, P]), ident[:])
+            nc.scalar.copy(gates[:, T * r : T * (r + 1)], acc[:])
+
+        late_words = keep.tile([P, S - EARLY * C], U32, name="grouped2", align_bytes=64)
         gather_scales(0, C)
-        gather_scales(C, S // 2)
-        move_scales(0, S // 2, nc.scalar)
-        gather_words(2, 0, 2 * C)
-        gather_scales(S // 2, S)
-        move_scales(S // 2, S, nc.sync)
-        gather_words(2, 2 * C, 4 * C)
-        gather_words(0, 4 * C, 6 * C)
-        gather_words(1, 4 * C, 6 * C)
-        gather_words(2, 4 * C, 5 * C)
-        gather_words(0, 6 * C, S)
-        gather_words(2, 5 * C, 6 * C)
-        gather_words(1, 6 * C, S)
-        gather_words(2, 6 * C, 7 * C)
-        gather_words(2, 7 * C, 7 * C + P)
-        gather_words(2, 7 * C + P, S)
-        for e in range(OPEN):
-            expert_pass(0, e)
-            expert_pass(1, e)
+        gather_scales(C, 2 * C)
+        move_scales(0, 2 * C, nc.scalar)
+        gather_scales(2 * C, 6 * C)
+        move_scales(2 * C, 6 * C, nc.scalar)
+        gather_words(1, EARLY * C, OPEN * C)
+        for lo in range(0, OPEN * C, 2 * C):
+            gather_words(2, lo, lo + 2 * C)
+        gather_scales(6 * C, S)
+        move_scales(6 * C, S, nc.sync)
+        for first in range(0, OPEN, 2):
+            for a in range(2):
+                for e in (first, first + 1):
+                    expert_pass(a, e)
         for e in range(OPEN):
             expert_pass(2, e)
-            if e == 1:
-                gates = keep.tile([P, TOP, T], F32, name="w4_0", align_bytes=64)
-                nc.sync.dma_start(gates[:], gate[:, :P, :].rearrange("r p t -> p r t"))
-        for a, e in ((0, 4), (0, 5), (1, 4), (1, 5), (2, 4), (0, 6), (0, 7), (2, 5), (1, 6), (1, 7), (2, 6), (2, 7)):
-            expert_pass(a, e)
+        for e in range(OPEN, OPEN + 2):
+            expert_pass(0, e)
+        for e in range(OPEN, E - 1):
+            if e % 2 == 0:
+                gather_words(1, C * e, C * (e + 2))
+            gather_words(2, C * e, C * (e + 1))
+            expert_pass(1, e)
+            expert_pass(2, e)
+            if e + 2 < E - 1:
+                expert_pass(0, e + 2)
+            if e + 2 == E - 1:
+                last_expert_pass(0)
+        last_expert_pass(1)
+        last_expert_pass(2)
+        nc.vector.tensor_scalar_add(y[1][:, S - 2 * C : S - C], sums[E - 2][1][:, 0, :], bias[:, 1, E - 2 : E - 1])
 
-        prod = [keep.tile([P, TOP, T], F32, name="prod%d" % n) for n in range(NT)]
-        turned = [keep.tile([P, T], F32, name="turned%d" % n) for n in range(NT)]
-        final = keep.tile([P, T], F32, name="final")
-        last_list = keep.tile([P, T], F32, name="last_list")
+        def piece(name):
+            return keep.tile([P, T], F32, name=name)
 
-        def fetch(dst, n, r, lo=0, hi=T):
-            nc.vector.tensor_tensor(
-                dst[:, lo:hi], y[n][:].indirect(pos_t[r][:, lo // 16 : hi // 16]), gates[:, r, lo:hi], MULT
-            )
+        def fetch(n, r, name):
+            dst = piece(name)
+            nc.vector.tensor_tensor(dst[:], y[n][:].indirect(pos_t[r][:]), gates[:, T * r : T * (r + 1)], MULT)
+            return dst
 
-        def fetch_plain(n, r, hi=T):
-            nc.scalar.activation(prod[n][:, r, :hi], y[n][:].indirect(pos_t[r][:, : hi // 16]), COPY)
+        def fetch_plain(n, r):
+            dst = piece("plain%d%d" % (n, r))
+            nc.scalar.activation(dst[:], y[n][:].indirect(pos_t[r][:]), COPY)
+            return dst
 
-        def times_gate(n, r, lo=0, hi=T):
-            nc.vector.tensor_tensor(prod[n][:, r, lo:hi], prod[n][:, r, lo:hi], gates[:, r, lo:hi], MULT)
+        def turn(dst, src, opens=True, closes=True):
+            for c in range(BLOCKS):
+                nc.tensor.matmul(dst(c), lhsT=src(c), rhs=ident[:], is_transpose=True,
+                                 start=(opens and c == 0), stop=(closes and c == BLOCKS - 1))
 
-        def add_turned(total, n, r, lo, hi, first, final):
-            for c in range(lo, hi, P):
-                nc.tensor.matmul(
-                    total[:, c - lo : c - lo + P],
-                    lhsT=prod[n][:, r, c : c + P],
-                    rhs=ident[:],
-                    is_transpose=True,
-                    start=(r == first and c == lo),
-                    stop=(r == final and c == hi - P),
-                )
+        def blocks(t):
+            return lambda c: t[:, P * c : P * (c + 1)]
 
-        def turn_back(total, back, n, lo, hi):
-            nc.scalar.copy(turned[n][:, lo:hi], total[:])
-            for c in range(lo, hi, P):
-                nc.tensor.transpose(back[:, c - lo : c - lo + P], turned[n][:, c : c + P], ident[:])
+        def turn_one(dst, src, opens, closes):
+            nc.tensor.matmul(dst, lhsT=src, rhs=ident[:], is_transpose=True, start=opens, stop=closes)
 
-        def store(n, back):
-            res = keep.tile([P, T], F32, name="prod%d" % (n + 1))
-            nc.scalar.copy(res[:], back[:])
-            nc.sync.dma_start(out[P * n : P * (n + 1), :], res[:])
+        def gate_blocks(dst, turned, r, first=0, count=BLOCKS):
+            for c in range(first, first + count):
+                at = BLOCKS * r + c
+                nc.scalar.activation(blocks(dst)(c), blocks(turned)(c - first), COPY, scale=gate_cols[:, at : at + 1])
 
-        totals = [bank(0, T), bank(2, T)]
-        backs = [bank(1, T), bank(3, T)]
+        last = E - 1
+        f0 = [fetch(0, r, "f0%d" % r) for r in range(3)]
+        p3 = [fetch_plain(0, 3)]
+        late_product(last, 1, 4)
+        p3.append(fetch_plain(1, 3))
+        late_product(last - 1, 2, 5)
+        late_product(last, 2, 6)
+        p12 = fetch_plain(1, 2)
+        pair = [bank(1, 2, 2, P), bank(2, 2, 2, P)]
+        own = bank(3, T)
         for n in range(2):
-            for r in range(2):
-                fetch(prod[n][:, r, :], n, r)
-                fetch_plain(n, r + 2)
-                if (n, r) == (0, 0):
-                    empty(E - 1, 2, sums[E - 1][1][:, 1, :])
-            for r in range(2, TOP):
-                times_gate(n, r)
-            for r in range(TOP):
-                add_turned(totals[n], n, r, 0, T, 0, 3)
-        n = NT - 1
-        fetch_plain(n, 2)
-        turn_back(totals[0], backs[0], 0, 0, T)
-        fetch_plain(n, 3, HALF)
-        turn_back(totals[1], backs[1], 1, 0, T)
-        store(0, backs[0])
+            for c in range(BLOCKS):
+                turn_one(pair[c // 2][:, c % 2, n, :], blocks(p3[n])(c), n == 0 and c % 2 == 0, n == 1 and c % 2 == 1)
+            turn(blocks(own), blocks(f0[n]), opens=(n == 0), closes=False)
+        turn(blocks(own), blocks(f0[2]), opens=False)
+        t12 = bank(4, T)
+        turn(blocks(t12), blocks(p12))
+        f1 = [fetch(1, r, "f1%d" % r) for r in range(2)]
+        own_sum = piece("own_sum")
+        nc.vector.tensor_copy(own_sum[:], own[:])
+        nc.vector.tensor_tensor(f1[0][:], f1[0][:], f1[1][:], ADD)
+        f2 = keep.tile([P, 2, T], F32, name="f02")
+        for r in range(2):
+            nc.vector.tensor_tensor(f2[:, r, :], y[2][:].indirect(pos_t[r][:]), gates[:, T * r : T * (r + 1)], MULT)
 
-        pieces = ((0, HALF), (HALF, T))
-        totals = [bank(7, HALF), bank(4, HALF)]
-        fetch(prod[n][:, 0, :], n, 0)
-        times_gate(n, 2)
-        for r in (0, 2):
-            for total, (lo, hi) in zip(totals, pieces):
-                add_turned(total, n, r, lo, hi, 0, 3)
-        ends = []
-        for i, (lo, hi) in enumerate(pieces):
-            if i == 0:
-                times_gate(n, 3, lo, hi)
-            else:
-                fetch(prod[n][:, 3, :], n, 3, lo, hi)
-            add_turned(totals[i], n, 3, lo, hi, 0, 3)
-            ends.append(bank(5 + i, hi - lo))
-            turn_back(totals[i], ends[i], n, lo, hi)
-        store(1, backs[1])
-        for lo, hi in pieces:
-            fetch(last_list, n, 1, lo, hi)
-        for end, (lo, hi) in zip(ends, pieces):
-            nc.vector.tensor_tensor(final[:, lo:hi], end[:], last_list[:, lo:hi], ADD)
-            nc.sync.dma_start(out[P * n : P * (n + 1), lo:hi], final[:, lo:hi])
+        g3 = keep.tile([P, BLOCKS, 2, P], F32, name="g3")
+        back = [bank(5, T), bank(6, T)]
+        for c in range(BLOCKS):
+            at = BLOCKS * 3 + c
+            nc.scalar.activation(g3[:, c], pair[c // 2][:, c % 2], COPY, scale=gate_cols[:, at : at + 1])
+            for n in range(2):
+                turn_one(blocks(back[n])(c), g3[:, c, n, :], c == 0, False)
+        p22 = fetch_plain(2, 2)
+        t22 = bank(0, T)
+        turn(blocks(t22), blocks(p22))
+        turn(blocks(back[0]), blocks(own_sum), opens=False)
+        g12 = piece("g12")
+        gate_blocks(g12, t12, 2)
+        turn(blocks(back[1]), blocks(g12), opens=False)
+        p23 = piece("p23")
+        t23 = [bank(7, HALF), bank(3, HALF)]
+        for h in range(2):
+            nc.scalar.activation(p23[:, HALF * h : HALF * (h + 1)], y[2][:].indirect(pos_t[3][:, HALF * h // 16 : HALF * (h + 1) // 16]), COPY)
+            for c in range(2):
+                turn_one(blocks(t23[h])(c), blocks(p23)(2 * h + c), c == 0, c == 1)
+        g22 = piece("g22")
+        gate_blocks(g22, t22, 2)
+        ends = [bank(1, HALF), bank(2, HALF)]
+        for c in range(BLOCKS):
+            turn_one(blocks(ends[c // 2])(c % 2), blocks(g22)(c), c % 2 == 0, False)
+        g23 = piece("g23")
+        for h in range(2):
+            gate_blocks(g23, t23[h], 3, 2 * h, 2)
+            for c in range(2):
+                turn_one(blocks(ends[h])(c), blocks(g23)(2 * h + c), False, c == 1)
+        res = [piece("res%d" % n) for n in range(NT)]
+        nc.vector.tensor_tensor(res[1][:], back[1][:], f1[0][:], ADD)
+        nc.sync.dma_start(out[P : 2 * P, :], res[1][:])
+        nc.vector.tensor_tensor(f2[:, 0, :], f2[:, 0, :], f2[:, 1, :], ADD)
+        nc.scalar.copy(res[0][:], back[0][:])
+        nc.sync.dma_start(out[:P, :], res[0][:])
+        for h in range(2):
+            cols = slice(HALF * h, HALF * (h + 1))
+            nc.vector.tensor_tensor(res[2][:, cols], ends[h][:], f2[:, 0, cols], ADD)
+            nc.sync.dma_start(out[2 * P :, cols], res[2][:, cols])

@@ -175,7 +175,10 @@ def tile_moe_tk_lin_bias_kernel(
             acc = bank(i, C)
             for a in range(3):
                 multiply(a, e, n, acc[:])
-            empty(e, n, acc[:])
+            if e == E - 1:
+                empty(e, n, acc[:])
+            else:
+                nc.vector.tensor_scalar_add(y[n][:, C * e : C * (e + 1)], acc[:], bias[:, n, e : e + 1])
 
         interleave(0, 0, P, on_vector=True)
         interleave(0, P, HALF)
@@ -326,10 +329,12 @@ def tile_moe_tk_lin_bias_kernel(
         res = [piece("res%d" % n) for n in range(NT)]
         nc.vector.tensor_tensor(res[1][:], back[1][:], f1[0][:], ADD)
         nc.sync.dma_start(out[P : 2 * P, :], res[1][:])
-        nc.vector.tensor_tensor(f2[:, 0, :], f2[:, 0, :], f2[:, 1, :], ADD)
+        sum2 = piece("g12")
+        for lo in (0, HALF):
+            nc.vector.tensor_tensor(sum2[:, lo : lo + HALF], f2[:, 0, lo : lo + HALF], f2[:, 1, lo : lo + HALF], ADD)
         nc.scalar.copy(res[0][:], back[0][:])
         nc.sync.dma_start(out[:P, :], res[0][:])
         for h in range(2):
             cols = slice(HALF * h, HALF * (h + 1))
-            nc.vector.tensor_tensor(res[2][:, cols], ends[h][:], f2[:, 0, cols], ADD)
+            nc.vector.tensor_tensor(res[2][:, cols], ends[h][:], sum2[:, cols], ADD)
             nc.sync.dma_start(out[2 * P :, cols], res[2][:, cols])

@@ -175,10 +175,7 @@ def tile_moe_tk_lin_bias_kernel(
             acc = bank(i, C)
             for a in range(3):
                 multiply(a, e, n, acc[:])
-            if e == E - 1:
-                empty(e, n, acc[:])
-            else:
-                nc.vector.tensor_scalar_add(y[n][:, C * e : C * (e + 1)], acc[:], bias[:, n, e : e + 1])
+            empty(e, n, acc[:])
 
         interleave(0, 0, P, on_vector=True)
         interleave(0, P, HALF)
@@ -245,96 +242,101 @@ def tile_moe_tk_lin_bias_kernel(
         def piece(name):
             return keep.tile([P, T], F32, name=name)
 
-        def fetch(n, r, name):
-            dst = piece(name)
-            nc.vector.tensor_tensor(dst[:], y[n][:].indirect(pos_t[r][:]), gates[:, T * r : T * (r + 1)], MULT)
-            return dst
+        def block(tile, c):
+            return tile[:, P * c : P * (c + 1)]
 
-        def fetch_plain(n, r):
-            dst = piece("plain%d%d" % (n, r))
-            nc.scalar.activation(dst[:], y[n][:].indirect(pos_t[r][:]), COPY)
-            return dst
+        def fetch_gated(dst, n, r):
+            nc.vector.tensor_tensor(dst, y[n][:].indirect(pos_t[r][:]), gates[:, T * r : T * (r + 1)], MULT)
+
+        def fetch_plain(dst, n, r, lo=0, hi=T):
+            nc.scalar.activation(dst[:, lo:hi], y[n][:].indirect(pos_t[r][:, lo // 16 : hi // 16]), COPY)
+
+        def turn_block(dst, src, opens, closes):
+            nc.tensor.matmul(dst, lhsT=src, rhs=ident[:], is_transpose=True, start=opens, stop=closes)
 
         def turn(dst, src, opens=True, closes=True):
             for c in range(BLOCKS):
-                nc.tensor.matmul(dst(c), lhsT=src(c), rhs=ident[:], is_transpose=True,
-                                 start=(opens and c == 0), stop=(closes and c == BLOCKS - 1))
+                turn_block(block(dst, c), block(src, c), opens and c == 0, closes and c == BLOCKS - 1)
 
-        def blocks(t):
-            return lambda c: t[:, P * c : P * (c + 1)]
+        def times_gate(dst, turned, r, c):
+            at = BLOCKS * r + c
+            nc.scalar.activation(dst, turned, COPY, scale=gate_cols[:, at : at + 1])
 
-        def turn_one(dst, src, opens, closes):
-            nc.tensor.matmul(dst, lhsT=src, rhs=ident[:], is_transpose=True, start=opens, stop=closes)
-
-        def gate_blocks(dst, turned, r, first=0, count=BLOCKS):
-            for c in range(first, first + count):
-                at = BLOCKS * r + c
-                nc.scalar.activation(blocks(dst)(c), blocks(turned)(c - first), COPY, scale=gate_cols[:, at : at + 1])
-
-        last = E - 1
-        f0 = [fetch(0, r, "f0%d" % r) for r in range(3)]
-        p3 = [fetch_plain(0, 3)]
-        late_product(last, 1, 4)
-        p3.append(fetch_plain(1, 3))
-        late_product(last - 1, 2, 5)
-        late_product(last, 2, 6)
-        p12 = fetch_plain(1, 2)
-        pair = [bank(1, 2, 2, P), bank(2, 2, 2, P)]
-        own = bank(3, T)
+        gated_0 = [piece("gated_0%d" % r) for r in range(3)]
+        for r in range(3):
+            fetch_gated(gated_0[r][:], 0, r)
+        plain_3 = [piece("plain_03"), piece("plain_13")]
+        fetch_plain(plain_3[0], 0, 3)
+        late_product(E - 1, 1, 4)
+        fetch_plain(plain_3[1], 1, 3)
+        late_product(E - 2, 2, 5)
+        late_product(E - 1, 2, 6)
+        plain_12 = piece("plain_12")
+        fetch_plain(plain_12, 1, 2)
+        turned_3 = [bank(1, 2, 2, P), bank(2, 2, 2, P)]
+        turned_sum = bank(3, T)
         for n in range(2):
             for c in range(BLOCKS):
-                turn_one(pair[c // 2][:, c % 2, n, :], blocks(p3[n])(c), n == 0 and c % 2 == 0, n == 1 and c % 2 == 1)
-            turn(blocks(own), blocks(f0[n]), opens=(n == 0), closes=False)
-        turn(blocks(own), blocks(f0[2]), opens=False)
-        t12 = bank(4, T)
-        turn(blocks(t12), blocks(p12))
-        f1 = [fetch(1, r, "f1%d" % r) for r in range(2)]
-        own_sum = piece("own_sum")
-        nc.vector.tensor_copy(own_sum[:], own[:])
-        nc.vector.tensor_tensor(f1[0][:], f1[0][:], f1[1][:], ADD)
-        f2 = keep.tile([P, 2, T], F32, name="f02")
-        for r in range(2):
-            nc.vector.tensor_tensor(f2[:, r, :], y[2][:].indirect(pos_t[r][:]), gates[:, T * r : T * (r + 1)], MULT)
+                turn_block(turned_3[c // 2][:, c % 2, n, :], block(plain_3[n], c), n == 0 and c % 2 == 0, n == 1 and c % 2 == 1)
+            turn(turned_sum, gated_0[n], opens=(n == 0), closes=False)
+        turn(turned_sum, gated_0[2], opens=False)
+        turned_12 = bank(4, T)
+        turn(turned_12, plain_12)
 
-        g3 = keep.tile([P, BLOCKS, 2, P], F32, name="g3")
+        gated_1 = [piece("gated_1%d" % r) for r in range(2)]
+        for r in range(2):
+            fetch_gated(gated_1[r][:], 1, r)
+        sum_0 = piece("sum_0")
+        nc.vector.tensor_copy(sum_0[:], turned_sum[:])
+        nc.vector.tensor_tensor(gated_1[0][:], gated_1[0][:], gated_1[1][:], ADD)
+        gated_2 = keep.tile([P, 2, T], F32, name="gated_02")
+        for r in range(2):
+            fetch_gated(gated_2[:, r, :], 2, r)
+
+        scaled_3 = keep.tile([P, BLOCKS, 2, P], F32, name="scaled_3")
         back = [bank(5, T), bank(6, T)]
         for c in range(BLOCKS):
-            at = BLOCKS * 3 + c
-            nc.scalar.activation(g3[:, c], pair[c // 2][:, c % 2], COPY, scale=gate_cols[:, at : at + 1])
+            times_gate(scaled_3[:, c], turned_3[c // 2][:, c % 2], 3, c)
             for n in range(2):
-                turn_one(blocks(back[n])(c), g3[:, c, n, :], c == 0, False)
-        p22 = fetch_plain(2, 2)
-        t22 = bank(0, T)
-        turn(blocks(t22), blocks(p22))
-        turn(blocks(back[0]), blocks(own_sum), opens=False)
-        g12 = piece("g12")
-        gate_blocks(g12, t12, 2)
-        turn(blocks(back[1]), blocks(g12), opens=False)
-        p23 = piece("p23")
-        t23 = [bank(7, HALF), bank(3, HALF)]
-        for h in range(2):
-            nc.scalar.activation(p23[:, HALF * h : HALF * (h + 1)], y[2][:].indirect(pos_t[3][:, HALF * h // 16 : HALF * (h + 1) // 16]), COPY)
-            for c in range(2):
-                turn_one(blocks(t23[h])(c), blocks(p23)(2 * h + c), c == 0, c == 1)
-        g22 = piece("g22")
-        gate_blocks(g22, t22, 2)
-        ends = [bank(1, HALF), bank(2, HALF)]
+                turn_block(block(back[n], c), scaled_3[:, c, n, :], c == 0, False)
+        plain_22 = piece("plain_22")
+        fetch_plain(plain_22, 2, 2)
+        turned_22 = bank(0, T)
+        turn(turned_22, plain_22)
+        turn(back[0], sum_0, opens=False)
+        scaled_12 = piece("scaled_12")
         for c in range(BLOCKS):
-            turn_one(blocks(ends[c // 2])(c % 2), blocks(g22)(c), c % 2 == 0, False)
-        g23 = piece("g23")
+            times_gate(block(scaled_12, c), block(turned_12, c), 2, c)
+        turn(back[1], scaled_12, opens=False)
+
+        plain_23 = piece("plain_23")
+        turned_23 = [bank(7, HALF), bank(3, HALF)]
         for h in range(2):
-            gate_blocks(g23, t23[h], 3, 2 * h, 2)
+            fetch_plain(plain_23, 2, 3, HALF * h, HALF * (h + 1))
             for c in range(2):
-                turn_one(blocks(ends[h])(c), blocks(g23)(2 * h + c), False, c == 1)
-        res = [piece("res%d" % n) for n in range(NT)]
-        nc.vector.tensor_tensor(res[1][:], back[1][:], f1[0][:], ADD)
-        nc.sync.dma_start(out[P : 2 * P, :], res[1][:])
-        sum2 = piece("g12")
-        for lo in (0, HALF):
-            nc.vector.tensor_tensor(sum2[:, lo : lo + HALF], f2[:, 0, lo : lo + HALF], f2[:, 1, lo : lo + HALF], ADD)
-        nc.scalar.copy(res[0][:], back[0][:])
-        nc.sync.dma_start(out[:P, :], res[0][:])
+                turn_block(block(turned_23[h], c), block(plain_23, 2 * h + c), c == 0, c == 1)
+        scaled_22 = piece("scaled_22")
+        for c in range(BLOCKS):
+            times_gate(block(scaled_22, c), block(turned_22, c), 2, c)
+        back_2 = [bank(1, HALF), bank(2, HALF)]
+        for c in range(BLOCKS):
+            turn_block(block(back_2[c // 2], c % 2), block(scaled_22, c), c % 2 == 0, False)
+        scaled_23 = piece("scaled_23")
         for h in range(2):
-            cols = slice(HALF * h, HALF * (h + 1))
-            nc.vector.tensor_tensor(res[2][:, cols], ends[h][:], sum2[:, cols], ADD)
-            nc.sync.dma_start(out[2 * P :, cols], res[2][:, cols])
+            for c in range(2):
+                times_gate(block(scaled_23, 2 * h + c), block(turned_23[h], c), 3, 2 * h + c)
+            for c in range(2):
+                turn_block(block(back_2[h], c), block(scaled_23, 2 * h + c), False, c == 1)
+
+        result = [piece("result%d" % n) for n in range(NT)]
+        nc.vector.tensor_tensor(result[1][:], back[1][:], gated_1[0][:], ADD)
+        nc.sync.dma_start(out[P : 2 * P, :], result[1][:])
+        sum_2 = piece("scaled_12")
+        halves = [slice(0, HALF), slice(HALF, T)]
+        for cols in halves:
+            nc.vector.tensor_tensor(sum_2[:, cols], gated_2[:, 0, cols], gated_2[:, 1, cols], ADD)
+        nc.scalar.copy(result[0][:], back[0][:])
+        nc.sync.dma_start(out[:P, :], result[0][:])
+        for half, cols in zip(back_2, halves):
+            nc.vector.tensor_tensor(result[2][:, cols], half[:], sum_2[:, cols], ADD)
+            nc.sync.dma_start(out[2 * P :, cols], result[2][:, cols])

from contextlib import ExitStack

import concourse.mybir as mybir
from concourse.masks import make_identity

K, T, E, C, N = 1536, 512, 8, 256, 384
S = E * C
FLOPS = 2 * K * N * S
BYTES = 4 * K * T + E * K * N // 3 + E * K * N // 3 + E * K * N // 32 + 4 * N * E + 16 * T + 2 * 128 * (S + 4 * T) // 16 + 4 * N * T

F32 = mybir.dt.float32
BF16 = mybir.dt.bfloat16
U32 = mybir.dt.uint32
I32 = mybir.dt.int32
U16 = mybir.dt.uint16
U8 = mybir.dt.uint8
FP8X4 = mybir.dt.float8_e4m3fn_x4
FP4X4 = mybir.dt.float4_e2m1fn_x4
COPY = mybir.ActivationFunctionType.Copy
IDENT = mybir.ActivationFunctionType.Identity
MULT = mybir.AluOpType.mult
ADD = mybir.AluOpType.add

P = 128
NT = N // P
TOP = 4
BLOCKS = T // P
HALF = T // 2
LONG = 1376
SHORT = 1024
ROW = (4, 0, 8)
VECTOR_SHARE = 160
OPEN = 4
EARLY = 2


def tile_moe_tk_lin_bias_kernel(
    tc, xT, w8_words, w8_scales, w4_words, w4_scales, b, gate, offs, pos1, pos2, pos3, pos4, out
):
    nc = tc.nc
    with ExitStack() as ctx:
        keep = ctx.enter_context(tc.tile_pool(name="keep", bufs=1))
        psum = ctx.enter_context(tc.psum_pool(name="psum", bufs=1))

        offs_t = keep.tile([P, S // 16], U16, name="offs_t")
        pos_t = [keep.tile([P, T // 16], U16, name="pos_t%d" % r) for r in range(TOP)]
        raw = [keep.tile([P, 4, T], F32, name="raw%d" % a, align_bytes=64) for a in range(3)]
        grouped = [keep.tile([P, T, 4], BF16, name="grouped%d" % a, align_bytes=64) for a in range(3)]
        words = keep.tile([P, 2 * T + LONG], U32, name="words", align_bytes=64)
        scales = keep.tile([P, LONG], U8, name="scales", align_bytes=64)
        slot_words = [keep.tile([P, EARLY * C if a == 1 else S], U32, name="slot_words%d" % a, align_bytes=64) for a in range(3)]
        slot_scales = keep.tile([P, S], U8, name="slot_scales", align_bytes=64)
        ident = keep.tile([P, P], F32, name="ident")
        moved_scales = keep.tile([P, S], U8, name="moved_scales", align_bytes=64)
        w8 = [keep.tile([P, E // 2, 4 * N], U8, name="w8_%d" % h, align_bytes=64) for h in range(2)]
        w4 = [keep.tile([P, E, 2 * N], U8, name="w4_%d" % h, align_bytes=64) for h in range(2)]
        s8 = keep.tile([P, E, N], U8, name="s8", align_bytes=64)
        bias = keep.tile([P, NT, E], F32, name="bias")
        y = [keep.tile([P, S], F32, name="y%d" % n) for n in range(NT)]
        gate_rows = keep.tile([P, P], F32, name="gate_rows")

        nc.gpsimd.memset(gate_rows[:], 0.0)
        make_identity(nc, ident[:])
        nc.vector.memset(s8[:].rearrange("p e n -> p (e n)").bitcast(I32), 0)
        xv = xT.rearrange("(a p j) t -> a p j t", p=P, j=4)
        nc.sync.dma_start(raw[0][:, :, :HALF], xv[0, :, :, :HALF])
        nc.sync.dma_start(raw[0][:, :, HALF:], xv[0, :, :, HALF:])
        nc.sync.dma_start(offs_t[:], offs)
        nc.sync.dma_start(raw[1][:], xv[1])
        nc.sync.dma_start(raw[2][:], xv[2])
        runs = gate.rearrange("r n (c t) -> (r n c) t", t=P)
        nc.gpsimd.dma_start(gate_rows[: TOP * BLOCKS, :], runs[0 : (TOP * BLOCKS - 1) * (N + 1) + 1 : N + 1])
        nc.gpsimd.dma_start(bias[:], b.rearrange("(c p) e -> p c e", p=P))
        v8 = w8_scales.rearrange("e a q n -> q (e a) n")
        v4 = w4_scales.rearrange("e a q n -> q (e a) n")
        w8v = w8_words.rearrange("e a p n r -> p (e a) (n r)")
        w4v = w4_words.rearrange("e a p n -> p (e a) n")

        nc.sync.dma_start(w8[0][:].bitcast(I32), w8v[:, : E // 2].bitcast(I32))
        for q in range(4):
            nc.sync.dma_start(s8[q:P:32, :, :].bitcast(I32), v8[q:16:4].bitcast(I32))
        nc.sync.dma_start(w4[0][:].bitcast(I32), w4v[:, :E].bitcast(I32))
        nc.sync.dma_start(w8[1][:].bitcast(I32), w8v[:, E // 2 :].bitcast(I32))
        nc.sync.dma_start(w4[1][:].bitcast(I32), w4v[:, E:].bitcast(I32))
        for r, pos in enumerate((pos1, pos2, pos3, pos4)):
            nc.sync.dma_start(pos_t[r][:], pos)
        nc.vector.memset(scales[:].bitcast(I32), 0)
        nc.vector.memset(words[:, 3 * T :].bitcast(I32), 0)
        nc.vector.memset(moved_scales[:].bitcast(I32), 0)

        def interleave(a, lo, hi, on_vector=False):
            dst = grouped[a][:, lo:hi, :].rearrange("p (c i) j -> p c j i", i=4)
            src = raw[a][:, :, lo:hi].rearrange("p j (c i) -> p c j i", i=4)
            if on_vector:
                nc.vector.tensor_copy(dst, src)
            else:
                nc.scalar.activation(dst, src, COPY)

        def quantise(a, lo, hi):
            nc.vector.quantize_mx(
                out=words[:, (2 - a) * T + lo : (2 - a) * T + hi].bitcast(FP8X4),
                scales=scales[ROW[a] :, lo:hi],
                in_=grouped[a][:, lo:hi, :].rearrange("p t j -> p (t j)"),
            )

        def in_slots(a, lo, hi):
            if a == 1 and lo >= EARLY * C:
                return late_words[:, lo - EARLY * C : hi - EARLY * C]
            return slot_words[a][:, lo:hi]

        def gather_words(a, lo, hi):
            width = LONG if hi - lo > 3 * C else SHORT
            window = words[:, (2 - a) * T : (2 - a) * T + width]
            nc.vector.tensor_copy(in_slots(a, lo, hi), window.indirect(offs_t[:, lo // 16 : hi // 16]))

        def gather_scales(lo, hi):
            nc.vector.tensor_copy(slot_scales[:, lo:hi], scales[:].indirect(offs_t[:, lo // 16 : hi // 16]))

        def move_scales(lo, hi, queue):
            queue.dma_start(moved_scales[: P - ROW[2], lo:hi].bitcast(I32), slot_scales[ROW[2] :, lo:hi].bitcast(I32))

        def weights(a, e, n):
            h, i = divmod(e, E // 2)
            if a == 0:
                return w8[h][:, i, 4 * P * n : 4 * P * (n + 1)].bitcast(FP8X4)
            return w4[h][:, 2 * i + a - 1, 2 * P * n : 2 * P * (n + 1)].bitcast(FP4X4)

        def multiply(a, e, n, acc, lo=0, hi=C, opens=True, closes=True):
            cols = slice(C * e + lo, C * e + hi)
            w_scales = s8[:, e, :] if a == 0 else s4[:, 2 * e + a - 1, :]
            nc.tensor.matmul_mx(
                out=acc,
                lhsT=weights(a, e, n),
                lhsT_scale=w_scales[:, P * n : P * (n + 1)],
                rhs=in_slots(a, cols.start, cols.stop).bitcast(FP8X4),
                rhs_scale=moved_scales[:, cols] if a == 2 else slot_scales[ROW[a] :, cols],
                start=(a == 0 and opens),
                stop=(a == 2 and closes),
            )

        def empty(e, n, acc, lo=0, hi=C):
            nc.scalar.activation(y[n][:, C * e + lo : C * e + hi], acc, IDENT, bias=bias[:, n, e : e + 1])

        def bank(i, *shape):
            return psum.tile([P, *shape], F32, name="bank%d" % i)

        sums = {}

        def expert_pass(a, e):
            rows = range(1, min(NT, E - e))
            if a == 0:
                sums[e] = (bank(2 * (e % OPEN), C), bank(2 * (e % OPEN) + 1, len(rows), C))
            first, others = sums[e]
            multiply(a, e, 0, first[:])
            for n in rows:
                multiply(a, e, n, others[:, n - 1, :], opens=(n == rows[0]), closes=(n == rows[-1]))
            if a == 2:
                empty(e, 0, first[:])
                for n in rows:
                    if e < E - 2:
                        empty(e, n, others[:, n - 1, :])

        def last_expert_pass(a):
            e = E - 1
            if a == 0:
                sums[e] = (bank(6, P), bank(7, P))
            for half, lo in zip(sums[e], (0, P)):
                if a == 2:
                    gather_words(2, C * e + lo, C * e + lo + P)
                multiply(a, e, 0, half[:], lo, lo + P)
                if a == 2:
                    empty(e, 0, half[:], lo, lo + P)

        def late_product(e, n, i):
            acc = bank(i, C)
            for a in range(3):
                multiply(a, e, n, acc[:])
            empty(e, n, acc[:])

        interleave(0, 0, P, on_vector=True)
        interleave(0, P, HALF)
        quantise(0, 0, HALF)
        interleave(0, HALF, HALF + VECTOR_SHARE, on_vector=True)
        interleave(0, HALF + VECTOR_SHARE, T)
        quantise(0, HALF, T)
        interleave(1, 0, T)
        interleave(2, 0, T)
        for lo in range(0, S, S // 2):
            gather_words(0, lo, lo + S // 2)
        quantise(1, 0, T)
        s4 = keep.tile([P, 2 * E, N], U8, name="raw0", align_bytes=64)
        for q in range(4):
            nc.gpsimd.dma_start(s4[q:P:32, :, :].bitcast(I32), v4[q:16:4].bitcast(I32))
        gather_words(1, 0, EARLY * C)
        quantise(2, 0, T)

        gates = keep.tile([P, (TOP - 1) * T + TOP * BLOCKS], F32, name="raw2", align_bytes=64)
        gate_cols = gates[:, (TOP - 1) * T :]
        acc = bank(0, P)
        nc.tensor.transpose(acc[:], gate_rows[:], ident[:])
        nc.scalar.copy(gate_cols, acc[:, : TOP * BLOCKS])
        for r in range(TOP - 1):
            acc = bank(r + 1, T)
            for c in range(BLOCKS):
                at = BLOCKS * r + c
                nc.tensor.transpose(acc[:, P * c : P * (c + 1)], gate_cols[:, at : at + 1].to_broadcast([P, P]), ident[:])
            nc.scalar.copy(gates[:, T * r : T * (r + 1)], acc[:])

        late_words = keep.tile([P, S - EARLY * C], U32, name="grouped2", align_bytes=64)
        gather_scales(0, C)
        gather_scales(C, 2 * C)
        move_scales(0, 2 * C, nc.scalar)
        gather_scales(2 * C, 6 * C)
        move_scales(2 * C, 6 * C, nc.scalar)
        gather_words(1, EARLY * C, OPEN * C)
        for lo in range(0, OPEN * C, 2 * C):
            gather_words(2, lo, lo + 2 * C)
        gather_scales(6 * C, S)
        move_scales(6 * C, S, nc.sync)
        for first in range(0, OPEN, 2):
            for a in range(2):
                for e in (first, first + 1):
                    expert_pass(a, e)
        for e in range(OPEN):
            expert_pass(2, e)
        for e in range(OPEN, OPEN + 2):
            expert_pass(0, e)
        for e in range(OPEN, E - 1):
            if e % 2 == 0:
                gather_words(1, C * e, C * (e + 2))
            gather_words(2, C * e, C * (e + 1))
            expert_pass(1, e)
            expert_pass(2, e)
            if e + 2 < E - 1:
                expert_pass(0, e + 2)
            if e + 2 == E - 1:
                last_expert_pass(0)
        last_expert_pass(1)
        last_expert_pass(2)
        nc.vector.tensor_scalar_add(y[1][:, S - 2 * C : S - C], sums[E - 2][1][:, 0, :], bias[:, 1, E - 2 : E - 1])

        def piece(name):
            return keep.tile([P, T], F32, name=name)

        def block(tile, c):
            return tile[:, P * c : P * (c + 1)]

        def fetch_gated(dst, n, r):
            nc.vector.tensor_tensor(dst, y[n][:].indirect(pos_t[r][:]), gates[:, T * r : T * (r + 1)], MULT)

        def fetch_plain(dst, n, r, lo=0, hi=T):
            nc.scalar.activation(dst[:, lo:hi], y[n][:].indirect(pos_t[r][:, lo // 16 : hi // 16]), COPY)

        def turn_block(dst, src, opens, closes):
            nc.tensor.matmul(dst, lhsT=src, rhs=ident[:], is_transpose=True, start=opens, stop=closes)

        def turn(dst, src, opens=True, closes=True):
            for c in range(BLOCKS):
                turn_block(block(dst, c), block(src, c), opens and c == 0, closes and c == BLOCKS - 1)

        def times_gate(dst, turned, r, c):
            at = BLOCKS * r + c
            nc.scalar.activation(dst, turned, COPY, scale=gate_cols[:, at : at + 1])

        gated_0 = [piece("gated_0%d" % r) for r in range(3)]
        for r in range(3):
            fetch_gated(gated_0[r][:], 0, r)
        plain_3 = [piece("plain_03"), piece("plain_13")]
        fetch_plain(plain_3[0], 0, 3)
        late_product(E - 1, 1, 4)
        fetch_plain(plain_3[1], 1, 3)
        late_product(E - 2, 2, 5)
        late_product(E - 1, 2, 6)
        plain_12 = piece("plain_12")
        fetch_plain(plain_12, 1, 2)
        turned_3 = [bank(1, 2, 2, P), bank(2, 2, 2, P)]
        turned_sum = bank(3, T)
        for n in range(2):
            for c in range(BLOCKS):
                turn_block(turned_3[c // 2][:, c % 2, n, :], block(plain_3[n], c), n == 0 and c % 2 == 0, n == 1 and c % 2 == 1)
            turn(turned_sum, gated_0[n], opens=(n == 0), closes=False)
        turn(turned_sum, gated_0[2], opens=False)
        turned_12 = bank(4, T)
        turn(turned_12, plain_12)

        gated_1 = [piece("gated_1%d" % r) for r in range(2)]
        for r in range(2):
            fetch_gated(gated_1[r][:], 1, r)
        sum_0 = piece("sum_0")
        nc.vector.tensor_copy(sum_0[:], turned_sum[:])
        nc.vector.tensor_tensor(gated_1[0][:], gated_1[0][:], gated_1[1][:], ADD)
        gated_2 = keep.tile([P, 2, T], F32, name="gated_02")
        for r in range(2):
            fetch_gated(gated_2[:, r, :], 2, r)

        scaled_3 = keep.tile([P, BLOCKS, 2, P], F32, name="scaled_3")
        back = [bank(5, T), bank(6, T)]
        for c in range(BLOCKS):
            times_gate(scaled_3[:, c], turned_3[c // 2][:, c % 2], 3, c)
            for n in range(2):
                turn_block(block(back[n], c), scaled_3[:, c, n, :], c == 0, False)
        plain_22 = piece("plain_22")
        fetch_plain(plain_22, 2, 2)
        turned_22 = bank(0, T)
        turn(turned_22, plain_22)
        turn(back[0], sum_0, opens=False)
        scaled_12 = piece("scaled_12")
        for c in range(BLOCKS):
            times_gate(block(scaled_12, c), block(turned_12, c), 2, c)
        turn(back[1], scaled_12, opens=False)

        plain_23 = piece("plain_23")
        turned_23 = [bank(7, HALF), bank(3, HALF)]
        for h in range(2):
            fetch_plain(plain_23, 2, 3, HALF * h, HALF * (h + 1))
            for c in range(2):
                turn_block(block(turned_23[h], c), block(plain_23, 2 * h + c), c == 0, c == 1)
        scaled_22 = piece("scaled_22")
        for c in range(BLOCKS):
            times_gate(block(scaled_22, c), block(turned_22, c), 2, c)
        back_2 = [bank(1, HALF), bank(2, HALF)]
        for c in range(BLOCKS):
            turn_block(block(back_2[c // 2], c % 2), block(scaled_22, c), c % 2 == 0, False)
        scaled_23 = piece("scaled_23")
        for h in range(2):
            for c in range(2):
                times_gate(block(scaled_23, 2 * h + c), block(turned_23[h], c), 3, 2 * h + c)
            for c in range(2):
                turn_block(block(back_2[h], c), block(scaled_23, 2 * h + c), False, c == 1)

        result = [piece("result%d" % n) for n in range(NT)]
        nc.vector.tensor_tensor(result[1][:], back[1][:], gated_1[0][:], ADD)
        nc.sync.dma_start(out[P : 2 * P, :], result[1][:])
        sum_2 = piece("scaled_12")
        halves = [slice(0, HALF), slice(HALF, T)]
        for cols in halves:
            nc.vector.tensor_tensor(sum_2[:, cols], gated_2[:, 0, cols], gated_2[:, 1, cols], ADD)
        nc.scalar.copy(result[0][:], back[0][:])
        nc.sync.dma_start(out[:P, :], result[0][:])
        for half, cols in zip(back_2, halves):
            nc.vector.tensor_tensor(result[2][:, cols], half[:], sum_2[:, cols], ADD)
            nc.sync.dma_start(out[2 * P :, cols], result[2][:, cols])
